import numpy as np
import ml_dtypes


def mxq(x, axis, fmt="e4m3"):
    dtype, down = {"e4m3": (ml_dtypes.float8_e4m3fn, 7), "e5m2": (ml_dtypes.float8_e5m2, 14)}[fmt]
    v = np.moveaxis(np.asarray(x, np.float32).astype(ml_dtypes.bfloat16).astype(np.float64), axis, -1)
    blocks = v.reshape(v.shape[:-1] + (-1, 32))
    amax = np.abs(blocks).max(-1, keepdims=True)
    byte = np.maximum(np.where(amax > 0, np.frexp(amax)[1] - 1 + 127, 0) - down, 1)
    scale = np.exp2(byte - 127.0)
    codes = (blocks / scale).astype(np.float32).astype(dtype).astype(np.float64)
    return np.moveaxis((codes * scale).reshape(v.shape), -1, axis)


WIDE = False


def mx_kscale(k):
    if not WIDE:
        return np.ones(k)
    levels = np.array([10, -10, 5, -5, 0])
    if k % 512:
        return np.exp2(np.random.permutation(np.resize(levels, k // 32))).repeat(32)
    a = np.empty((k // 512, 16))
    for p in range(k // 512):
        a[p, :8] = np.random.permutation(np.resize(levels, 8))
        for g in range(8):
            far = levels[np.abs(levels - a[p, g]) >= 10]
            a[p, g + 8] = far[np.random.randint(len(far))]
    return np.exp2(a.ravel()).repeat(32)


def f64(x):
    return np.asarray(x).astype(np.float64)


def striped(idx):
    return np.tile(idx.reshape(-1, 16).T, (8, 1)).astype(np.uint16)


def unstriped(offs):
    return offs[:16].T.reshape(-1).astype(np.int64)


E2M1 = np.array([0.0, 0.5, 1.0, 1.5, 2.0, 3.0, 4.0, 6.0, -0.0, -0.5, -1.0, -1.5, -2.0, -3.0, -4.0, -6.0])


def pack_weight(w, fmt):
    k, n = w.shape
    w = f64(np.asarray(w, np.float32).astype(ml_dtypes.bfloat16)).reshape(k // 32, 32, n)
    amax = np.abs(w).max(1)
    if fmt == "e4m3":
        byte = np.frexp(amax)[1] - 1 + 127 - 7
    else:
        mant, ex = np.frexp(amax / 6.0)
        byte = np.where(mant > 0.5, ex, ex - 1) + 127
    byte = np.clip(np.where(amax > 0, byte, 1), 1, 254)
    scaled = (w * np.exp2(127.0 - byte)[:, None, :]).reshape(k, n).astype(np.float32)
    by_word = np.ascontiguousarray(scaled.reshape(k // 512, 128, 4, n).transpose(0, 1, 3, 2))
    if fmt == "e4m3":
        words = by_word.astype(ml_dtypes.float8_e4m3fn).view(np.uint8)
    else:
        c = by_word.astype(ml_dtypes.float4_e2m1fn).view(np.uint8) & 0xF
        words = (c[..., 0::2] | (c[..., 1::2] << 4)).reshape(k // 512, 128, 2 * n)
    return np.ascontiguousarray(words), np.ascontiguousarray(byte.astype(np.uint8).reshape(k // 512, 16, n))


def unpack_weight(words, scales, fmt):
    g, _, n = scales.shape
    words = np.ascontiguousarray(words).reshape(g, 128, n, -1)
    if fmt == "e4m3":
        vals = words.view(ml_dtypes.float8_e4m3fn).astype(np.float64)
    else:
        nib = np.empty((g, 128, n, 4), np.uint8)
        nib[..., 0::2] = words & 0xF
        nib[..., 1::2] = words >> 4
        vals = E2M1[nib]
    vals = vals * np.repeat(np.exp2(scales.astype(np.float64) - 127.0), 8, axis=1)[..., None]
    return vals.transpose(0, 1, 3, 2).reshape(g * 512, n)


def gelu(v):
    return 0.5 * v * (1.0 + np.tanh(np.sqrt(2.0 / np.pi) * (v + 0.044715 * v**3)))


K, T, S, P, H = 1536, 2048, 1024, 512, 1024

def setup_inputs():
    n = np.random.standard_normal
    s = mx_kscale(K)[:, None]
    u = mx_kscale(H)[:, None]
    tab_words, tab_scales = pack_weight(n((K, T)) * s, "e4m3")
    w4_words, w4_scales = pack_weight(n((K, H)) / np.sqrt(K) / s, "e2m1")
    w2 = (1.5 * n((H, H)) / np.sqrt(H) / u).astype(np.float32)
    gain = (np.exp(0.3 * n(H)) * u[:, 0]).astype(np.float32)
    d = (0.7 * n(H)).astype(np.float32)
    offs = striped(np.random.permutation(T)[:S])
    pos1 = striped(np.random.permutation(S)[:P])
    pos2 = striped(np.random.permutation(S)[:P])
    return {"tab_words": tab_words, "tab_scales": tab_scales, "offs": offs,
            "pos1": pos1, "pos2": pos2,
            "w4_words": w4_words, "w4_scales": w4_scales,
            "gain": gain, "w2": w2, "d": d}

def reference(tab_words, tab_scales, offs, pos1, pos2, w4_words, w4_scales, gain, w2, d):
    v = unpack_weight(tab_words, tab_scales, "e4m3")[:, unstriped(offs)]
    w4 = unpack_weight(w4_words, w4_scales, "e2m1")
    h = np.tanh(w4.T @ v)
    x = f64(gain)[:, None] * h[:, unstriped(pos1)]
    xq = mxq(x, 0, "e4m3")
    w2q = mxq(f64(w2), 0, "e4m3")
    y = w2q.T @ xq
    f = h[:, unstriped(pos2)]
    return np.square(f) * y + f64(d)[:, None] * f

@@ -1,0 +1,197 @@
+from contextlib import ExitStack
+
+import concourse.mybir as mybir
+from concourse.masks import make_identity
+
+K, T, S, P, H = 1536, 2048, 1024, 512, 1024
+FLOPS = 2 * K * H * S + 2 * H * H * P
+
+F32 = mybir.dt.float32
+BF16 = mybir.dt.bfloat16
+I32 = mybir.dt.int32
+U32 = mybir.dt.uint32
+U16 = mybir.dt.uint16
+U8 = mybir.dt.uint8
+FP8X4 = mybir.dt.float8_e4m3fn_x4
+FP4X4 = mybir.dt.float4_e2m1fn_x4
+MULT = mybir.AluOpType.mult
+ADD = mybir.AluOpType.add
+TANH = mybir.ActivationFunctionType.Tanh
+
+NP = 128
+A1 = K // 512
+A2 = H // 512
+N = 512
+
+
+def tile_list_well_log_corrector_kernel(tc, tab_words, tab_scales, offs, pos1, pos2, w4_words, w4_scales, gain, w2, d, out):
+    nc = tc.nc
+    with ExitStack() as ctx:
+        lists = ctx.enter_context(tc.tile_pool(name="lists", bufs=1))
+        keep = ctx.enter_context(tc.tile_pool(name="keep", bufs=1))
+        shared = ctx.enter_context(tc.tile_pool(name="shared", bufs=1))
+        ring = ctx.enter_context(tc.tile_pool(name="ring", bufs=4))
+        psum = ctx.enter_context(tc.psum_pool(name="psum", bufs=8))
+
+        offs_sb = lists.tile([NP, S // 16], U16, name="offs_sb")
+        nc.sync.dma_start(offs_sb[:], offs)
+
+        warm = keep.tile([NP, 8], F32, name="warm")
+        nc.vector.memset(warm[:], 0.0)
+        warm2 = keep.tile([NP, 8], F32, name="warm2")
+        nc.scalar.activation(warm2[:], warm[:], TANH)
+        gvec = keep.tile([NP, 2 * NP], F32, name="gvec")
+        for lo, hi in ((0, 28), (32, 64), (64, 128)):
+            nc.gpsimd.memset(gvec[lo:hi, :], 0.0)
+        nc.sync.dma_start(gvec[28:32, :].rearrange("t (g i) -> t g i", i=8), gain.rearrange("(g t i) -> t g i", t=4, i=8))
+        ident = keep.tile([NP, NP], F32, name="ident")
+        make_identity(nc, ident[:])
+
+        swin = keep.tile([NP, T], U8, name="swin", align_bytes=64)
+        s4raw = shared.tile([64, H], U8, name="s4raw", align_bytes=64, offset=S)
+        nc.vector.memset(swin[0:16, :].bitcast(I32), 0)
+        nc.vector.memset(swin[64:128, :].bitcast(I32), 0)
+        nc.vector.memset(s4raw[0:16, :].bitcast(I32), 0)
+        rows = tab_scales.rearrange("a s t -> (a s) t").rearrange("(g r) t -> r g t", r=4)
+        nc.scalar.dma_start(swin[16:64, :].bitcast(I32), rows.bitcast(I32))
+
+        twin = [keep.tile([NP, T], I32, name=f"twin{a}", tag=f"twin{a}", align_bytes=64) for a in range(A1)]
+        w4raw = keep.tile([NP, A1, 2 * H], U8, name="w4raw", align_bytes=64)
+        nc.sync.dma_start(twin[0][:], tab_words[0].rearrange("p t i -> p (t i)").bitcast(I32))
+        rows4 = w4_scales.rearrange("a s c -> (a s) c").rearrange("(g r) c -> r g c", r=4)
+        nc.sync.dma_start(s4raw[16:64, :].bitcast(I32), rows4.bitcast(I32))
+        nc.sync.dma_start(w4raw[:].bitcast(I32), w4_words.rearrange("a p c -> p a c").bitcast(I32))
+        for a in range(1, A1):
+            nc.sync.dma_start(twin[a][:], tab_words[a].rearrange("p t i -> p (t i)").bitcast(I32))
+        pos1_sb = lists.tile([NP, P // 16], U16, name="pos1_sb")
+        pos2_sb = lists.tile([NP, P // 16], U16, name="pos2_sb")
+        nc.sync.dma_start(pos1_sb[:], pos1)
+        nc.sync.dma_start(pos2_sb[:], pos2)
+
+
+        def columns(vec, first, name):
+            bank = psum.tile([NP, N], F32, name="bank", tag="bank")
+            for b in range(A2):
+                nc.tensor.transpose(bank[:, NP * b : NP * (b + 1)], vec[:, NP * b : NP * (b + 1)], ident[:])
+            col = keep.tile([NP, A2, 4], F32, name=name)
+            nc.scalar.copy(col[:], bank[:, 0 : 2 * NP].rearrange("p (b c) -> p b c", b=A2)[:, :, first : first + 4])
+            return col
+
+        gcol = columns(gvec, 28, "gcol")
+        gfull = []
+        for b in range(A2):
+            gf = keep.tile([NP, 4, P], F32, name=f"gfull{b}", tag=f"gfull{b}")
+            nc.scalar.copy(gf[:], gcol[:, b, :].unsqueeze(2).to_broadcast([NP, 4, P]))
+            gfull.append(gf)
+
+        planes = keep.tile([NP, A1, S + H], U8, name="planes", align_bytes=64)
+        nc.vector.memset(planes[:].bitcast(I32), 0)
+
+        gs = shared.tile([NP, S], U8, name="gs", align_bytes=64, offset=0)
+        nc.vector.tensor_copy(gs[:], swin[:].indirect(offs_sb[:]))
+        both = keep.tile([64, S + H], U8, name="both", tag="both", align_bytes=64)
+        nc.vector.tensor_copy(
+            both[:, S:].bitcast(I32).rearrange("p (b t q i) -> p b t q i", b=A2, t=4, i=2),
+            s4raw[:].bitcast(I32).rearrange("p (b q t i) -> p b t q i", b=A2, t=4, i=2))
+        nc.vector.tensor_copy(both[:, :S].bitcast(I32), gs[0:64, :].bitcast(I32))
+        for q in range(4):
+            nc.scalar.dma_start(planes[32 * q : 32 * q + 4, :, :].bitcast(I32), both[16 + q : 64 : 4, :].bitcast(I32))
+
+        dvec = keep.tile([NP, 2 * NP], F32, name="dvec", tag="both", align_bytes=64)
+        nc.gpsimd.memset(dvec[:], 0.0)
+        nc.sync.dma_start(dvec[0:4, :].rearrange("t (g i) -> t g i", i=8), d.rearrange("(g t i) -> t g i", t=4, i=8))
+        vw = [shared.tile([NP, S], U32, name="vw0", align_bytes=64, offset=0)]
+        vw.extend(keep.tile([NP, S], U32, name=f"vw{a}", align_bytes=64) for a in range(1, A1))
+        nc.vector.tensor_copy(vw[0][:], twin[0][:].bitcast(U32).indirect(offs_sb[:]))
+
+        w4w = keep.tile([NP, A2, 4, A1, 256], U8, name="w4w", tag="w4w", align_bytes=64)
+        for b in range(A2):
+            nc.vector.tensor_copy(
+                w4w[:, b].bitcast(I32).rearrange("p t a (q i) -> p t a q i", i=4),
+                w4raw[:].bitcast(I32).rearrange("p a (b q t i) -> p b t a q i", b=A2, t=4, i=4)[:, b])
+
+        nc.vector.tensor_copy(vw[1][:], twin[1][:].bitcast(U32).indirect(offs_sb[:]))
+        for c in range(2):
+            nc.vector.tensor_copy(vw[2][:, N * c : N * (c + 1)],
+                                  twin[2][:].bitcast(U32).indirect(offs_sb[:, 32 * c : 32 * (c + 1)]))
+
+        w2rows = w2.rearrange("(a q j i) n -> a j q i n", a=A2, j=4, i=8)
+        w2raw = []
+        for a in range(A2):
+            raw = keep.tile([NP, 4, H], F32, name=f"w2raw{a}", tag=f"twin{a + 1}", align_bytes=64)
+            for j in range(4):
+                nc.sync.dma_start(raw[:, j, :], w2rows[a, j])
+            w2raw.append(raw)
+
+        def first_pass(acc, b, t, a, c):
+            cols = slice(N * c, N * (c + 1))
+            nc.tensor.matmul_mx(out=acc[:], lhsT=w4w[:, b, t, a, :].bitcast(FP4X4), lhsT_scale=planes[:, a, S + N * b + NP * t : S + N * b + NP * (t + 1)],
+                                rhs=vw[a][:, cols].bitcast(FP8X4), rhs_scale=planes[:, a, cols],
+                                start=(a == 0), stop=(a == A1 - 1))
+
+        def weave_w2(b, tag):
+            made = []
+            for a in range(A2):
+                wb = keep.tile([NP, 4, NP, 4], BF16, name=f"wb{a}{b}", tag=tag[a], align_bytes=64)
+                for t in range(4):
+                    nc.scalar.copy(
+                        wb[:, t].rearrange("p (q u i) j -> p q u j i", u=2, i=4),
+                        w2raw[a][:].rearrange("p j (b q t u i) -> p b t q u j i", b=A2, t=4, u=2, i=4)[:, b, t])
+                wq = keep.tile([NP, N], U32, name=f"wq{a}{b}", align_bytes=64)
+                ws = keep.tile([NP, N], U8, name=f"ws{a}{b}", align_bytes=64)
+                nc.vector.quantize_mx(out=wq[:].bitcast(FP8X4), scales=ws[:], in_=wb[:].rearrange("p t m j -> p (t m j)"))
+                made.append((wq, ws))
+            return made
+
+        x32, fine = [], []
+        for b in range(A2):
+            xb32 = keep.tile([NP, 4, P], F32, name=f"x32{b}", tag=f"x32{b}", align_bytes=64)
+            hs = []
+            if b == 0:
+                fb = keep.tile([NP, 4, P], F32, name="fine0")
+            for t in range(4):
+                h = keep.tile([NP, S], F32, name=f"h{b}{t}")
+                for c in range(2):
+                    acc = psum.tile([NP, N], F32, name="bank", tag="bank")
+                    for a in range(A1):
+                        first_pass(acc, b, t, a, c)
+                    nc.scalar.activation(h[:, N * c : N * (c + 1)], acc[:], TANH)
+                nc.vector.tensor_tensor(xb32[:, t, :], h[:].indirect(pos1_sb[:]), gfull[b][:, t, :], MULT)
+                if b == 0:
+                    nc.vector.tensor_copy(fb[:, t, :], h[:].indirect(pos2_sb[:]))
+                hs.append(h)
+            if b == 1:
+                fb = keep.tile([NP, 4, P], F32, name="fine1", tag="gfull1")
+                for t in range(4):
+                    nc.vector.tensor_copy(fb[:, t, :], hs[t][:].indirect(pos2_sb[:]))
+            x32.append(xb32)
+            fine.append(fb)
+
+        dcol = columns(dvec, 0, "dcol")
+        wmx = [weave_w2(0, ("wb00", "wb10"))]
+
+        xmx = []
+        for a in range(A2):
+            xb = keep.tile([NP, P, 4], BF16, name=f"xb{a}", tag=("w4w", "xb1")[a], align_bytes=64)
+            nc.scalar.copy(xb[:].rearrange("p (c i) t -> p c t i", i=4), x32[a][:].rearrange("p t (c i) -> p c t i", i=4))
+            xq = keep.tile([NP, P], U32, name=f"xq{a}", align_bytes=64)
+            xs = keep.tile([NP, P], U8, name=f"xs{a}", align_bytes=64)
+            nc.vector.quantize_mx(out=xq[:].bitcast(FP8X4), scales=xs[:], in_=xb[:].rearrange("p m t -> p (m t)"))
+            xmx.append((xq, xs))
+
+        wmx.append(weave_w2(1, ("x321", "x320")))
+
+        out_rows = out.rearrange("(b q t i) m -> b t q i m", b=A2, t=4, i=8)
+        for b in range(A2):
+            for t in range(4):
+                acc = psum.tile([NP, N], F32, name="bank", tag="bank")
+                cols = slice(NP * t, NP * (t + 1))
+                for a in range(A2):
+                    nc.tensor.matmul_mx(out=acc[:], lhsT=wmx[b][a][0][:, cols].bitcast(FP8X4), lhsT_scale=wmx[b][a][1][:, cols],
+                                        rhs=xmx[a][0][:].bitcast(FP8X4), rhs_scale=xmx[a][1][:],
+                                        start=(a == 0), stop=(a == A2 - 1))
+                fy = ring.tile([NP, P], F32, name="fy")
+                nc.vector.tensor_tensor(fy[:], acc[:], fine[b][:, t, :], MULT)
+                res = ring.tile([NP, P], F32, name="res")
+                nc.vector.scalar_tensor_tensor(res[:], fy[:], dcol[:, b, t : t + 1], fine[b][:, t, :], ADD, MULT)
+                nc.sync.dma_start(out_rows[b, t], res[:])

@@ -56,13 +56,15 @@ def tile_list_well_log_corrector_kernel(tc, tab_words, tab_scales, offs, pos1, p
         nc.scalar.dma_start(swin[16:64, :].bitcast(I32), rows.bitcast(I32))
 
         twin = [keep.tile([NP, T], I32, name=f"twin{a}", tag=f"twin{a}", align_bytes=64) for a in range(A1)]
-        w4raw = keep.tile([NP, A1, 2 * H], U8, name="w4raw", align_bytes=64)
+        w4raw = [keep.tile([NP, A1, H], U8, name=f"w4raw{b}", align_bytes=64) for b in range(A2)]
+        w4src = w4_words.rearrange("a p (b c) -> b p a c", b=A2)
         nc.sync.dma_start(twin[0][:], tab_words[0].rearrange("p t i -> p (t i)").bitcast(I32))
         rows4 = w4_scales.rearrange("a s c -> (a s) c").rearrange("(g r) c -> r g c", r=4)
         nc.sync.dma_start(s4raw[16:64, :].bitcast(I32), rows4.bitcast(I32))
-        nc.sync.dma_start(w4raw[:].bitcast(I32), w4_words.rearrange("a p c -> p a c").bitcast(I32))
+        nc.sync.dma_start(w4raw[0][:].bitcast(I32), w4src[0].bitcast(I32))
         for a in range(1, A1):
             nc.sync.dma_start(twin[a][:], tab_words[a].rearrange("p t i -> p (t i)").bitcast(I32))
+        nc.sync.dma_start(w4raw[1][:].bitcast(I32), w4src[1].bitcast(I32))
         pos1_sb = lists.tile([NP, P // 16], U16, name="pos1_sb")
         pos2_sb = lists.tile([NP, P // 16], U16, name="pos2_sb")
         nc.sync.dma_start(pos1_sb[:], pos1)
@@ -105,16 +107,20 @@ def tile_list_well_log_corrector_kernel(tc, tab_words, tab_scales, offs, pos1, p
         nc.vector.tensor_copy(vw[0][:], twin[0][:].bitcast(U32).indirect(offs_sb[:]))
 
         w4w = keep.tile([NP, A2, 4, A1, 256], U8, name="w4w", tag="w4w", align_bytes=64)
-        for b in range(A2):
+
+        def order_w4(b):
             nc.vector.tensor_copy(
                 w4w[:, b].bitcast(I32).rearrange("p t a (q i) -> p t a q i", i=4),
-                w4raw[:].bitcast(I32).rearrange("p a (b q t i) -> p b t a q i", b=A2, t=4, i=4)[:, b])
+                w4raw[b][:].bitcast(I32).rearrange("p a (q t i) -> p t a q i", t=4, i=4))
+
+        order_w4(0)
 
         nc.vector.tensor_copy(vw[1][:], twin[1][:].bitcast(U32).indirect(offs_sb[:]))
         for c in range(2):
             nc.vector.tensor_copy(vw[2][:, N * c : N * (c + 1)],
                                   twin[2][:].bitcast(U32).indirect(offs_sb[:, 32 * c : 32 * (c + 1)]))
 
+        order_w4(1)
         w2rows = w2.rearrange("(a q j i) n -> a j q i n", a=A2, j=4, i=8)
         w2raw = []
         for a in range(A2):
@@ -135,8 +141,8 @@ def tile_list_well_log_corrector_kernel(tc, tab_words, tab_scales, offs, pos1, p
                 wb = keep.tile([NP, 4, NP, 4], BF16, name=f"wb{a}{b}", tag=tag[a], align_bytes=64)
                 for t in range(4):
                     nc.scalar.copy(
-                        wb[:, t].rearrange("p (q u i) j -> p q u j i", u=2, i=4),
-                        w2raw[a][:].rearrange("p j (b q t u i) -> p b t q u j i", b=A2, t=4, u=2, i=4)[:, b, t])
+                        wb[:, t].rearrange("p (q i) j -> p q i j", i=8),
+                        w2raw[a][:].rearrange("p j (b q t i) -> p b t q i j", b=A2, t=4, i=8)[:, b, t])
                 wq = keep.tile([NP, N], U32, name=f"wq{a}{b}", align_bytes=64)
                 ws = keep.tile([NP, N], U8, name=f"ws{a}{b}", align_bytes=64)
                 nc.vector.quantize_mx(out=wq[:].bitcast(FP8X4), scales=ws[:], in_=wb[:].rearrange("p t m j -> p (t m j)"))
@@ -173,7 +179,7 @@ def tile_list_well_log_corrector_kernel(tc, tab_words, tab_scales, offs, pos1, p
         xmx = []
         for a in range(A2):
             xb = keep.tile([NP, P, 4], BF16, name=f"xb{a}", tag=("w4w", "xb1")[a], align_bytes=64)
-            nc.scalar.copy(xb[:].rearrange("p (c i) t -> p c t i", i=4), x32[a][:].rearrange("p t (c i) -> p c t i", i=4))
+            nc.scalar.copy(xb[:], x32[a][:].rearrange("p t m -> p m t"))
             xq = keep.tile([NP, P], U32, name=f"xq{a}", align_bytes=64)
             xs = keep.tile([NP, P], U8, name=f"xs{a}", align_bytes=64)
             nc.vector.quantize_mx(out=xq[:].bitcast(FP8X4), scales=xs[:], in_=xb[:].rearrange("p m t -> p (m t)"))
@@ -182,16 +188,28 @@ def tile_list_well_log_corrector_kernel(tc, tab_words, tab_scales, offs, pos1, p
         wmx.append(weave_w2(1, ("x321", "x320")))
 
         out_rows = out.rearrange("(b q t i) m -> b t q i m", b=A2, t=4, i=8)
-        for b in range(A2):
-            for t in range(4):
-                acc = psum.tile([NP, N], F32, name="bank", tag="bank")
-                cols = slice(NP * t, NP * (t + 1))
-                for a in range(A2):
-                    nc.tensor.matmul_mx(out=acc[:], lhsT=wmx[b][a][0][:, cols].bitcast(FP8X4), lhsT_scale=wmx[b][a][1][:, cols],
-                                        rhs=xmx[a][0][:].bitcast(FP8X4), rhs_scale=xmx[a][1][:],
-                                        start=(a == 0), stop=(a == A2 - 1))
-                fy = ring.tile([NP, P], F32, name="fy")
-                nc.vector.tensor_tensor(fy[:], acc[:], fine[b][:, t, :], MULT)
-                res = ring.tile([NP, P], F32, name="res")
-                nc.vector.scalar_tensor_tensor(res[:], fy[:], dcol[:, b, t : t + 1], fine[b][:, t, :], ADD, MULT)
-                nc.sync.dma_start(out_rows[b, t], res[:])
+
+        def times_y(b, t):
+            acc = psum.tile([NP, N], F32, name="bank", tag="bank")
+            cols = slice(NP * t, NP * (t + 1))
+            for a in range(A2):
+                nc.tensor.matmul_mx(out=acc[:], lhsT=wmx[b][a][0][:, cols].bitcast(FP8X4), lhsT_scale=wmx[b][a][1][:, cols],
+                                    rhs=xmx[a][0][:].bitcast(FP8X4), rhs_scale=xmx[a][1][:],
+                                    start=(a == 0), stop=(a == A2 - 1))
+            fy = ring.tile([NP, P], F32, name="fy")
+            nc.vector.tensor_tensor(fy[:], acc[:], fine[b][:, t, :], MULT)
+            return fy
+
+        def finish(b, t, fy):
+            res = ring.tile([NP, P], F32, name="res")
+            nc.vector.scalar_tensor_tensor(res[:], fy[:], dcol[:, b, t : t + 1], fine[b][:, t, :], ADD, MULT)
+            nc.sync.dma_start(out_rows[b, t], res[:])
+
+        tiles = [(b, t) for b in range(A2) for t in range(4)]
+        held = None
+        for b, t in tiles:
+            fy = times_y(b, t)
+            if held is not None:
+                finish(*held)
+            held = (b, t, fy)
+        finish(*held)

@@ -1,7 +1,6 @@
 from contextlib import ExitStack
 
 import concourse.mybir as mybir
-from concourse.masks import make_identity
 
 K, T, S, P, H = 1536, 2048, 1024, 512, 1024
 FLOPS = 2 * K * H * S + 2 * H * H * P
@@ -34,74 +33,60 @@ def tile_list_well_log_corrector_kernel(tc, tab_words, tab_scales, offs, pos1, p
         psum = ctx.enter_context(tc.psum_pool(name="psum", bufs=8))
 
         offs_sb = lists.tile([NP, S // 16], U16, name="offs_sb")
+        pos1_sb = lists.tile([NP, P // 16], U16, name="pos1_sb")
+        pos2_sb = lists.tile([NP, P // 16], U16, name="pos2_sb")
+        swin = keep.tile([NP, T], U8, name="swin", align_bytes=64)
+        s4raw = shared.tile([NP, H], U8, name="s4raw", align_bytes=64, offset=S)
+        gcol = keep.tile([NP, A2, 4], F32, name="gcol")
+        dcol = keep.tile([NP, A2, 4], F32, name="dcol")
+        rows = tab_scales.rearrange("a s t -> (a s) t").rearrange("(g r) t -> r g t", r=4)
+        rows4 = w4_scales.rearrange("a s c -> (a s) c").rearrange("(g r) c -> r g c", r=4)
+        nc.sync.dma_start(swin[16:64, :].bitcast(I32), rows.bitcast(I32))
+        nc.scalar.dma_start(gcol[:], gain.rearrange("(b p t) -> p b t", b=A2, t=4))
+        nc.scalar.dma_start(s4raw[16:64, :].bitcast(I32), rows4.bitcast(I32))
         nc.sync.dma_start(offs_sb[:], offs)
+        nc.sync.dma_start(pos1_sb[:], pos1)
+        nc.scalar.dma_start(dcol[:], d.rearrange("(b p t) -> p b t", b=A2, t=4))
+        nc.sync.dma_start(pos2_sb[:], pos2)
+        for tile in (s4raw, swin):
+            nc.vector.memset(tile[0:16, :].bitcast(I32), 0)
+            nc.vector.memset(tile[64:128, :].bitcast(I32), 0)
 
         warm = keep.tile([NP, 8], F32, name="warm")
         nc.vector.memset(warm[:], 0.0)
         warm2 = keep.tile([NP, 8], F32, name="warm2")
         nc.scalar.activation(warm2[:], warm[:], TANH)
-        gvec = keep.tile([NP, 2 * NP], F32, name="gvec")
-        for lo, hi in ((0, 28), (32, 64), (64, 128)):
-            nc.gpsimd.memset(gvec[lo:hi, :], 0.0)
-        nc.sync.dma_start(gvec[28:32, :].rearrange("t (g i) -> t g i", i=8), gain.rearrange("(g t i) -> t g i", t=4, i=8))
-        ident = keep.tile([NP, NP], F32, name="ident")
-        make_identity(nc, ident[:])
-
-        swin = keep.tile([NP, T], U8, name="swin", align_bytes=64)
-        s4raw = shared.tile([64, H], U8, name="s4raw", align_bytes=64, offset=S)
-        nc.vector.memset(swin[0:16, :].bitcast(I32), 0)
-        nc.vector.memset(swin[64:128, :].bitcast(I32), 0)
-        nc.vector.memset(s4raw[0:16, :].bitcast(I32), 0)
-        rows = tab_scales.rearrange("a s t -> (a s) t").rearrange("(g r) t -> r g t", r=4)
-        nc.scalar.dma_start(swin[16:64, :].bitcast(I32), rows.bitcast(I32))
 
         twin = [keep.tile([NP, T], I32, name=f"twin{a}", tag=f"twin{a}", align_bytes=64) for a in range(A1)]
-        w4raw = [keep.tile([NP, A1, H], U8, name=f"w4raw{b}", align_bytes=64) for b in range(A2)]
+        w4raw = [keep.tile([NP, A1, H], U8, name=f"w4raw{b}", tag=f"w4raw{b}", align_bytes=64) for b in range(A2)]
         w4src = w4_words.rearrange("a p (b c) -> b p a c", b=A2)
         nc.sync.dma_start(twin[0][:], tab_words[0].rearrange("p t i -> p (t i)").bitcast(I32))
-        rows4 = w4_scales.rearrange("a s c -> (a s) c").rearrange("(g r) c -> r g c", r=4)
-        nc.sync.dma_start(s4raw[16:64, :].bitcast(I32), rows4.bitcast(I32))
         nc.sync.dma_start(w4raw[0][:].bitcast(I32), w4src[0].bitcast(I32))
         for a in range(1, A1):
             nc.sync.dma_start(twin[a][:], tab_words[a].rearrange("p t i -> p (t i)").bitcast(I32))
         nc.sync.dma_start(w4raw[1][:].bitcast(I32), w4src[1].bitcast(I32))
-        pos1_sb = lists.tile([NP, P // 16], U16, name="pos1_sb")
-        pos2_sb = lists.tile([NP, P // 16], U16, name="pos2_sb")
-        nc.sync.dma_start(pos1_sb[:], pos1)
-        nc.sync.dma_start(pos2_sb[:], pos2)
 
-
-        def columns(vec, first, name):
-            bank = psum.tile([NP, N], F32, name="bank", tag="bank")
-            for b in range(A2):
-                nc.tensor.transpose(bank[:, NP * b : NP * (b + 1)], vec[:, NP * b : NP * (b + 1)], ident[:])
-            col = keep.tile([NP, A2, 4], F32, name=name)
-            nc.scalar.copy(col[:], bank[:, 0 : 2 * NP].rearrange("p (b c) -> p b c", b=A2)[:, :, first : first + 4])
-            return col
-
-        gcol = columns(gvec, 28, "gcol")
-        gfull = []
-        for b in range(A2):
+        def spread_gain(b):
             gf = keep.tile([NP, 4, P], F32, name=f"gfull{b}", tag=f"gfull{b}")
             nc.scalar.copy(gf[:], gcol[:, b, :].unsqueeze(2).to_broadcast([NP, 4, P]))
-            gfull.append(gf)
+            return gf
+
+        gfull = [spread_gain(0)]
 
         planes = keep.tile([NP, A1, S + H], U8, name="planes", align_bytes=64)
         nc.vector.memset(planes[:].bitcast(I32), 0)
 
         gs = shared.tile([NP, S], U8, name="gs", align_bytes=64, offset=0)
-        nc.vector.tensor_copy(gs[:], swin[:].indirect(offs_sb[:]))
-        both = keep.tile([64, S + H], U8, name="both", tag="both", align_bytes=64)
+        both = keep.tile([NP, S + H], U8, name="both", tag="both", align_bytes=64)
         nc.vector.tensor_copy(
-            both[:, S:].bitcast(I32).rearrange("p (b t q i) -> p b t q i", b=A2, t=4, i=2),
-            s4raw[:].bitcast(I32).rearrange("p (b q t i) -> p b t q i", b=A2, t=4, i=2))
-        nc.vector.tensor_copy(both[:, :S].bitcast(I32), gs[0:64, :].bitcast(I32))
+            both[:, S:].rearrange("p (b t m) -> p b t m", b=A2, t=4),
+            s4raw[:].rearrange("p (b m t) -> p b t m", b=A2, t=4))
+        nc.vector.tensor_copy(gs[:], swin[:].indirect(offs_sb[:]))
+        nc.vector.tensor_copy(both[:, :S].bitcast(I32), gs[:].bitcast(I32))
         for q in range(4):
             nc.scalar.dma_start(planes[32 * q : 32 * q + 4, :, :].bitcast(I32), both[16 + q : 64 : 4, :].bitcast(I32))
+        gfull.append(spread_gain(1))
 
-        dvec = keep.tile([NP, 2 * NP], F32, name="dvec", tag="both", align_bytes=64)
-        nc.gpsimd.memset(dvec[:], 0.0)
-        nc.sync.dma_start(dvec[0:4, :].rearrange("t (g i) -> t g i", i=8), d.rearrange("(g t i) -> t g i", t=4, i=8))
         vw = [shared.tile([NP, S], U32, name="vw0", align_bytes=64, offset=0)]
         vw.extend(keep.tile([NP, S], U32, name=f"vw{a}", align_bytes=64) for a in range(1, A1))
         nc.vector.tensor_copy(vw[0][:], twin[0][:].bitcast(U32).indirect(offs_sb[:]))
@@ -110,8 +95,8 @@ def tile_list_well_log_corrector_kernel(tc, tab_words, tab_scales, offs, pos1, p
 
         def order_w4(b):
             nc.vector.tensor_copy(
-                w4w[:, b].bitcast(I32).rearrange("p t a (q i) -> p t a q i", i=4),
-                w4raw[b][:].bitcast(I32).rearrange("p a (q t i) -> p t a q i", t=4, i=4))
+                w4w[:, b].bitcast(U16),
+                w4raw[b][:].bitcast(U16).rearrange("p a (m t) -> p t a m", t=4))
 
         order_w4(0)
 
@@ -121,13 +106,13 @@ def tile_list_well_log_corrector_kernel(tc, tab_words, tab_scales, offs, pos1, p
                                   twin[2][:].bitcast(U32).indirect(offs_sb[:, 32 * c : 32 * (c + 1)]))
 
         order_w4(1)
-        w2rows = w2.rearrange("(a q j i) n -> a j q i n", a=A2, j=4, i=8)
-        w2raw = []
-        for a in range(A2):
-            raw = keep.tile([NP, 4, H], F32, name=f"w2raw{a}", tag=f"twin{a + 1}", align_bytes=64)
-            for j in range(4):
-                nc.sync.dma_start(raw[:, j, :], w2rows[a, j])
-            w2raw.append(raw)
+        w2rows = w2.rearrange("(a p j) (b n) -> a b p j n", a=A2, j=4, b=A2)
+        w2raw = {}
+        for b in range(A2):
+            for a in range(A2):
+                raw = keep.tile([NP, 4, N], F32, name=f"w2raw{a}{b}", tag=(("twin1", "both"), ("twin2", "w4raw1"))[b][a], align_bytes=64)
+                nc.sync.dma_start(raw[:], w2rows[a, b])
+                w2raw[a, b] = raw
 
         def first_pass(acc, b, t, a, c):
             cols = slice(N * c, N * (c + 1))
@@ -139,10 +124,10 @@ def tile_list_well_log_corrector_kernel(tc, tab_words, tab_scales, offs, pos1, p
             made = []
             for a in range(A2):
                 wb = keep.tile([NP, 4, NP, 4], BF16, name=f"wb{a}{b}", tag=tag[a], align_bytes=64)
-                for t in range(4):
+                for c in range(4):
                     nc.scalar.copy(
-                        wb[:, t].rearrange("p (q i) j -> p q i j", i=8),
-                        w2raw[a][:].rearrange("p j (b q t i) -> p b t q i j", b=A2, t=4, i=8)[:, b, t])
+                        wb[:].rearrange("p t m j -> p m t j")[:, 32 * c : 32 * (c + 1)],
+                        w2raw[a, b][:].rearrange("p j (m t) -> p m t j", t=4)[:, 32 * c : 32 * (c + 1)])
                 wq = keep.tile([NP, N], U32, name=f"wq{a}{b}", align_bytes=64)
                 ws = keep.tile([NP, N], U8, name=f"ws{a}{b}", align_bytes=64)
                 nc.vector.quantize_mx(out=wq[:].bitcast(FP8X4), scales=ws[:], in_=wb[:].rearrange("p t m j -> p (t m j)"))
@@ -173,7 +158,6 @@ def tile_list_well_log_corrector_kernel(tc, tab_words, tab_scales, offs, pos1, p
             x32.append(xb32)
             fine.append(fb)
 
-        dcol = columns(dvec, 0, "dcol")
         wmx = [weave_w2(0, ("wb00", "wb10"))]
 
         xmx = []
@@ -187,7 +171,7 @@ def tile_list_well_log_corrector_kernel(tc, tab_words, tab_scales, offs, pos1, p
 
         wmx.append(weave_w2(1, ("x321", "x320")))
 
-        out_rows = out.rearrange("(b q t i) m -> b t q i m", b=A2, t=4, i=8)
+        out_rows = out.rearrange("(b p t) m -> b t p m", b=A2, t=4)
 
         def times_y(b, t):
             acc = psum.tile([NP, N], F32, name="bank", tag="bank")

@@ -15,6 +15,7 @@ FP8X4 = mybir.dt.float8_e4m3fn_x4
 FP4X4 = mybir.dt.float4_e2m1fn_x4
 MULT = mybir.AluOpType.mult
 ADD = mybir.AluOpType.add
+COPY = mybir.ActivationFunctionType.Copy
 TANH = mybir.ActivationFunctionType.Tanh
 
 NP = 128
@@ -41,12 +42,14 @@ def tile_list_well_log_corrector_kernel(tc, tab_words, tab_scales, offs, pos1, p
         dcol = keep.tile([NP, A2, 4], F32, name="dcol")
         rows = tab_scales.rearrange("a s t -> (a s) t").rearrange("(g r) t -> r g t", r=4)
         rows4 = w4_scales.rearrange("a s c -> (a s) c").rearrange("(g r) c -> r g c", r=4)
-        nc.sync.dma_start(swin[16:64, :].bitcast(I32), rows.bitcast(I32))
-        nc.scalar.dma_start(gcol[:], gain.rearrange("(b p t) -> p b t", b=A2, t=4))
+        w4raw = [keep.tile([NP, A1, H], U8, name=f"w4raw{b}", tag=f"w4raw{b}", align_bytes=64) for b in range(A2)]
+        w4src = w4_words.rearrange("a p (b c) -> b p a c", b=A2)
+        nc.sync.dma_start(w4raw[0][:].bitcast(I32), w4src[0].bitcast(I32))
         nc.scalar.dma_start(s4raw[16:64, :].bitcast(I32), rows4.bitcast(I32))
+        nc.sync.dma_start(swin[16:64, :].bitcast(I32), rows.bitcast(I32))
         nc.sync.dma_start(offs_sb[:], offs)
+        nc.scalar.dma_start(gcol[:], gain.rearrange("(b p t) -> p b t", b=A2, t=4))
         nc.sync.dma_start(pos1_sb[:], pos1)
-        nc.scalar.dma_start(dcol[:], d.rearrange("(b p t) -> p b t", b=A2, t=4))
         nc.sync.dma_start(pos2_sb[:], pos2)
         for tile in (s4raw, swin):
             nc.vector.memset(tile[0:16, :].bitcast(I32), 0)
@@ -58,23 +61,24 @@ def tile_list_well_log_corrector_kernel(tc, tab_words, tab_scales, offs, pos1, p
         nc.scalar.activation(warm2[:], warm[:], TANH)
 
         twin = [keep.tile([NP, T], I32, name=f"twin{a}", tag=f"twin{a}", align_bytes=64) for a in range(A1)]
-        w4raw = [keep.tile([NP, A1, H], U8, name=f"w4raw{b}", tag=f"w4raw{b}", align_bytes=64) for b in range(A2)]
-        w4src = w4_words.rearrange("a p (b c) -> b p a c", b=A2)
         nc.sync.dma_start(twin[0][:], tab_words[0].rearrange("p t i -> p (t i)").bitcast(I32))
-        nc.sync.dma_start(w4raw[0][:].bitcast(I32), w4src[0].bitcast(I32))
         for a in range(1, A1):
             nc.sync.dma_start(twin[a][:], tab_words[a].rearrange("p t i -> p (t i)").bitcast(I32))
         nc.sync.dma_start(w4raw[1][:].bitcast(I32), w4src[1].bitcast(I32))
+        nc.sync.dma_start(dcol[:], d.rearrange("(b p t) -> p b t", b=A2, t=4))
 
-        def spread_gain(b):
-            gf = keep.tile([NP, 4, P], F32, name=f"gfull{b}", tag=f"gfull{b}")
-            nc.scalar.copy(gf[:], gcol[:, b, :].unsqueeze(2).to_broadcast([NP, 4, P]))
-            return gf
-
-        gfull = [spread_gain(0)]
 
         planes = keep.tile([NP, A1, S + H], U8, name="planes", align_bytes=64)
         nc.vector.memset(planes[:].bitcast(I32), 0)
+
+        w4w = keep.tile([NP, A2, 4, A1, 256], U8, name="w4w", tag="w4w", align_bytes=64)
+
+        def order_w4(b):
+            nc.vector.tensor_copy(
+                w4w[:, b].bitcast(U16),
+                w4raw[b][:].bitcast(U16).rearrange("p a (m t) -> p t a m", t=4))
+
+        order_w4(0)
 
         gs = shared.tile([NP, S], U8, name="gs", align_bytes=64, offset=0)
         both = keep.tile([NP, S + H], U8, name="both", tag="both", align_bytes=64)
@@ -85,20 +89,12 @@ def tile_list_well_log_corrector_kernel(tc, tab_words, tab_scales, offs, pos1, p
         nc.vector.tensor_copy(both[:, :S].bitcast(I32), gs[:].bitcast(I32))
         for q in range(4):
             nc.scalar.dma_start(planes[32 * q : 32 * q + 4, :, :].bitcast(I32), both[16 + q : 64 : 4, :].bitcast(I32))
-        gfull.append(spread_gain(1))
+        gfull = keep.tile([NP, 4, P], F32, name="gfull", tag="gfull1")
+        nc.scalar.copy(gfull[:], gcol[:, 1, :].unsqueeze(2).to_broadcast([NP, 4, P]))
 
         vw = [shared.tile([NP, S], U32, name="vw0", align_bytes=64, offset=0)]
         vw.extend(keep.tile([NP, S], U32, name=f"vw{a}", align_bytes=64) for a in range(1, A1))
         nc.vector.tensor_copy(vw[0][:], twin[0][:].bitcast(U32).indirect(offs_sb[:]))
-
-        w4w = keep.tile([NP, A2, 4, A1, 256], U8, name="w4w", tag="w4w", align_bytes=64)
-
-        def order_w4(b):
-            nc.vector.tensor_copy(
-                w4w[:, b].bitcast(U16),
-                w4raw[b][:].bitcast(U16).rearrange("p a (m t) -> p t a m", t=4))
-
-        order_w4(0)
 
         nc.vector.tensor_copy(vw[1][:], twin[1][:].bitcast(U32).indirect(offs_sb[:]))
         for c in range(2):
@@ -110,7 +106,7 @@ def tile_list_well_log_corrector_kernel(tc, tab_words, tab_scales, offs, pos1, p
         w2raw = {}
         for b in range(A2):
             for a in range(A2):
-                raw = keep.tile([NP, 4, N], F32, name=f"w2raw{a}{b}", tag=(("twin1", "both"), ("twin2", "w4raw1"))[b][a], align_bytes=64)
+                raw = keep.tile([NP, 4, N], F32, name=f"w2raw{a}{b}", tag=(("twin0", "twin1"), ("twin2", "w4raw1"))[b][a], align_bytes=64)
                 nc.sync.dma_start(raw[:], w2rows[a, b])
                 w2raw[a, b] = raw
 
@@ -147,8 +143,10 @@ def tile_list_well_log_corrector_kernel(tc, tab_words, tab_scales, offs, pos1, p
                     for a in range(A1):
                         first_pass(acc, b, t, a, c)
                     nc.scalar.activation(h[:, N * c : N * (c + 1)], acc[:], TANH)
-                nc.vector.tensor_tensor(xb32[:, t, :], h[:].indirect(pos1_sb[:]), gfull[b][:, t, :], MULT)
+                if b == 1:
+                    nc.vector.tensor_tensor(xb32[:, t, :], h[:].indirect(pos1_sb[:]), gfull[:, t, :], MULT)
                 if b == 0:
+                    nc.vector.tensor_copy(xb32[:, t, :], h[:].indirect(pos1_sb[:]))
                     nc.vector.tensor_copy(fb[:, t, :], h[:].indirect(pos2_sb[:]))
                 hs.append(h)
             if b == 1:
@@ -162,8 +160,13 @@ def tile_list_well_log_corrector_kernel(tc, tab_words, tab_scales, offs, pos1, p
 
         xmx = []
         for a in range(A2):
-            xb = keep.tile([NP, P, 4], BF16, name=f"xb{a}", tag=("w4w", "xb1")[a], align_bytes=64)
-            nc.scalar.copy(xb[:], x32[a][:].rearrange("p t m -> p m t"))
+            src = x32[a]
+            if a == 0:
+                src = keep.tile([NP, 4, P], BF16, name="xg", tag="w4w", align_bytes=64)
+                for t in range(4):
+                    nc.scalar.activation(src[:, t, :], x32[a][:, t, :], COPY, scale=gcol[:, a, t : t + 1])
+            xb = keep.tile([NP, P, 4], BF16, name=f"xb{a}", align_bytes=64)
+            nc.scalar.copy(xb[:], src[:].rearrange("p t m -> p m t"))
             xq = keep.tile([NP, P], U32, name=f"xq{a}", align_bytes=64)
             xs = keep.tile([NP, P], U8, name=f"xs{a}", align_bytes=64)
             nc.vector.quantize_mx(out=xq[:].bitcast(FP8X4), scales=xs[:], in_=xb[:].rearrange("p m t -> p (m t)"))
@@ -180,20 +183,26 @@ def tile_list_well_log_corrector_kernel(tc, tab_words, tab_scales, offs, pos1, p
                 nc.tensor.matmul_mx(out=acc[:], lhsT=wmx[b][a][0][:, cols].bitcast(FP8X4), lhsT_scale=wmx[b][a][1][:, cols],
                                     rhs=xmx[a][0][:].bitcast(FP8X4), rhs_scale=xmx[a][1][:],
                                     start=(a == 0), stop=(a == A2 - 1))
+            return acc
+
+        def times_fine(acc, b, t, m):
             fy = ring.tile([NP, P], F32, name="fy")
-            nc.vector.tensor_tensor(fy[:], acc[:], fine[b][:, t, :], MULT)
+            nc.vector.tensor_tensor(fy[:, m], acc[:, m], fine[b][:, t, m], MULT)
             return fy
 
-        def finish(b, t, fy):
+        def finish(b, t, m, fy):
             res = ring.tile([NP, P], F32, name="res")
-            nc.vector.scalar_tensor_tensor(res[:], fy[:], dcol[:, b, t : t + 1], fine[b][:, t, :], ADD, MULT)
-            nc.sync.dma_start(out_rows[b, t], res[:])
+            nc.vector.scalar_tensor_tensor(res[:, m], fy[:, m], dcol[:, b, t : t + 1], fine[b][:, t, m], ADD, MULT)
+            nc.sync.dma_start(out_rows[b, t][:, m], res[:, m])
 
-        tiles = [(b, t) for b in range(A2) for t in range(4)]
         held = None
-        for b, t in tiles:
-            fy = times_y(b, t)
-            if held is not None:
-                finish(*held)
-            held = (b, t, fy)
+        for b in range(A2):
+            for t in range(4):
+                acc = times_y(b, t)
+                last = b == A2 - 1 and t == 3
+                for m in ([slice(0, P // 2), slice(P // 2, P)] if last else [slice(0, P)]):
+                    fy = times_fine(acc, b, t, m)
+                    if held is not None:
+                        finish(*held)
+                    held = (b, t, m, fy)
         finish(*held)

@@ -15,7 +15,6 @@ FP8X4 = mybir.dt.float8_e4m3fn_x4
 FP4X4 = mybir.dt.float4_e2m1fn_x4
 MULT = mybir.AluOpType.mult
 ADD = mybir.AluOpType.add
-COPY = mybir.ActivationFunctionType.Copy
 TANH = mybir.ActivationFunctionType.Tanh
 
 NP = 128
@@ -31,27 +30,29 @@ def tile_list_well_log_corrector_kernel(tc, tab_words, tab_scales, offs, pos1, p
         keep = ctx.enter_context(tc.tile_pool(name="keep", bufs=1))
         shared = ctx.enter_context(tc.tile_pool(name="shared", bufs=1))
         ring = ctx.enter_context(tc.tile_pool(name="ring", bufs=4))
-        psum = ctx.enter_context(tc.psum_pool(name="psum", bufs=8))
+        psum = ctx.enter_context(tc.psum_pool(name="psum", bufs=4))
 
         offs_sb = lists.tile([NP, S // 16], U16, name="offs_sb")
         pos1_sb = lists.tile([NP, P // 16], U16, name="pos1_sb")
         pos2_sb = lists.tile([NP, P // 16], U16, name="pos2_sb")
-        swin = keep.tile([NP, T], U8, name="swin", align_bytes=64)
+        swin = keep.tile([NP, T], U8, name="swin", tag="swin", align_bytes=64)
         s4raw = shared.tile([NP, H], U8, name="s4raw", align_bytes=64, offset=S)
         gcol = keep.tile([NP, A2, 4], F32, name="gcol")
         dcol = keep.tile([NP, A2, 4], F32, name="dcol")
-        rows = tab_scales.rearrange("a s t -> (a s) t").rearrange("(g r) t -> r g t", r=4)
-        rows4 = w4_scales.rearrange("a s c -> (a s) c").rearrange("(g r) c -> r g c", r=4)
-        w4raw = [keep.tile([NP, A1, H], U8, name=f"w4raw{b}", tag=f"w4raw{b}", align_bytes=64) for b in range(A2)]
+        w4raw = [keep.tile([NP, A1, H], U8, name=f"w4raw{b}", tag="w4raw0", align_bytes=64) for b in range(1)]
         w4src = w4_words.rearrange("a p (b c) -> b p a c", b=A2)
-        nc.sync.dma_start(w4raw[0][:].bitcast(I32), w4src[0].bitcast(I32))
-        nc.scalar.dma_start(s4raw[16:64, :].bitcast(I32), rows4.bitcast(I32))
-        nc.sync.dma_start(swin[16:64, :].bitcast(I32), rows.bitcast(I32))
+        twin = [keep.tile([NP, T], I32, name=f"twin{a}", tag=f"twin{a}", align_bytes=64) for a in range(A1 - 1)]
+        for queue, tile, rows in ((nc.sync, swin, tab_scales), (nc.scalar, s4raw, w4_scales)):
+            queue.dma_start(tile[16:48, :].bitcast(I32), rows[0:2].rearrange("a s c -> s a c").bitcast(I32))
+            queue.dma_start(tile[48:64, :].bitcast(I32), rows[2].bitcast(I32))
         nc.sync.dma_start(offs_sb[:], offs)
-        nc.scalar.dma_start(gcol[:], gain.rearrange("(b p t) -> p b t", b=A2, t=4))
+        nc.sync.dma_start(twin[0][:], tab_words[0].rearrange("p t i -> p (t i)").bitcast(I32))
         nc.sync.dma_start(pos1_sb[:], pos1)
+        nc.scalar.dma_start(gcol[:], gain.rearrange("(b p t) -> p b t", b=A2, t=4))
         nc.sync.dma_start(pos2_sb[:], pos2)
-        for tile in (s4raw, swin):
+        nc.scalar.dma_start(dcol[:], d.rearrange("(b p t) -> p b t", b=A2, t=4))
+        nc.sync.dma_start(w4raw[0][:].bitcast(I32), w4src[0].bitcast(I32))
+        for tile in (swin, s4raw):
             nc.vector.memset(tile[0:16, :].bitcast(I32), 0)
             nc.vector.memset(tile[64:128, :].bitcast(I32), 0)
 
@@ -60,124 +61,140 @@ def tile_list_well_log_corrector_kernel(tc, tab_words, tab_scales, offs, pos1, p
         warm2 = keep.tile([NP, 8], F32, name="warm2")
         nc.scalar.activation(warm2[:], warm[:], TANH)
 
-        twin = [keep.tile([NP, T], I32, name=f"twin{a}", tag=f"twin{a}", align_bytes=64) for a in range(A1)]
-        nc.sync.dma_start(twin[0][:], tab_words[0].rearrange("p t i -> p (t i)").bitcast(I32))
-        for a in range(1, A1):
-            nc.sync.dma_start(twin[a][:], tab_words[a].rearrange("p t i -> p (t i)").bitcast(I32))
-        nc.sync.dma_start(w4raw[1][:].bitcast(I32), w4src[1].bitcast(I32))
-        nc.sync.dma_start(dcol[:], d.rearrange("(b p t) -> p b t", b=A2, t=4))
-
-
+        nc.sync.dma_start(twin[1][:], tab_words[1].rearrange("p t i -> p (t i)").bitcast(I32))
         planes = keep.tile([NP, A1, S + H], U8, name="planes", align_bytes=64)
-        nc.vector.memset(planes[:].bitcast(I32), 0)
+        nc.gpsimd.memset(planes[:].bitcast(I32), 0)
 
-        w4w = keep.tile([NP, A2, 4, A1, 256], U8, name="w4w", tag="w4w", align_bytes=64)
+        w4w = [keep.tile([NP, 4, A1, 256], U8, name="w4w0", align_bytes=64)]
 
         def order_w4(b):
             nc.vector.tensor_copy(
-                w4w[:, b].bitcast(U16),
+                w4w[b][:].bitcast(U16),
                 w4raw[b][:].bitcast(U16).rearrange("p a (m t) -> p t a m", t=4))
 
-        order_w4(0)
-
-        gs = shared.tile([NP, S], U8, name="gs", align_bytes=64, offset=0)
-        both = keep.tile([NP, S + H], U8, name="both", tag="both", align_bytes=64)
+        gs = shared.tile([NP, S], U8, name="gs", align_bytes=64, offset=4 * S - S // 2)
+        both = keep.tile([NP, S + H], U8, name="both", tag="swin", align_bytes=64)
+        nc.vector.tensor_copy(gs[:], swin[:].indirect(offs_sb[:]))
         nc.vector.tensor_copy(
             both[:, S:].rearrange("p (b t m) -> p b t m", b=A2, t=4),
             s4raw[:].rearrange("p (b m t) -> p b t m", b=A2, t=4))
-        nc.vector.tensor_copy(gs[:], swin[:].indirect(offs_sb[:]))
         nc.vector.tensor_copy(both[:, :S].bitcast(I32), gs[:].bitcast(I32))
         for q in range(4):
-            nc.scalar.dma_start(planes[32 * q : 32 * q + 4, :, :].bitcast(I32), both[16 + q : 64 : 4, :].bitcast(I32))
-        gfull = keep.tile([NP, 4, P], F32, name="gfull", tag="gfull1")
-        nc.scalar.copy(gfull[:], gcol[:, 1, :].unsqueeze(2).to_broadcast([NP, 4, P]))
+            nc.sync.dma_start(planes[32 * q : 32 * q + 4, 0:2, :].bitcast(I32), both[16 + 8 * q : 24 + 8 * q, :].bitcast(I32))
+        twin.append(shared.tile([NP, T], I32, name="twin2", align_bytes=64, offset=4 * S + 64))
+        nc.sync.dma_start(twin[2][:], tab_words[2].rearrange("p t i -> p (t i)").bitcast(I32))
+        for q in range(4):
+            nc.sync.dma_start(planes[32 * q : 32 * q + 4, 2, :].bitcast(I32), both[48 + 4 * q : 52 + 4 * q, :].bitcast(I32))
+        g1 = keep.tile([NP, 4, P], F32, name="gfull1", tag="gfull1")
+        gfull = [[keep.tile([NP, P], F32, name=f"gfull0{t}", tag=("wb00", "wb10", "gfull02", "gfull03")[t], align_bytes=64)[:] for t in range(4)],
+                 [g1[:, t, :] for t in range(4)]]
+        for b in range(A2):
+            for t in range(4):
+                nc.scalar.copy(gfull[b][t], gcol[:, b, t : t + 1].to_broadcast([NP, P]))
 
         vw = [shared.tile([NP, S], U32, name="vw0", align_bytes=64, offset=0)]
-        vw.extend(keep.tile([NP, S], U32, name=f"vw{a}", align_bytes=64) for a in range(1, A1))
+        vw.append(keep.tile([NP, S], U32, name="vw1", align_bytes=64))
+        vlast = [keep.tile([NP, N], U32, name=f"vlast{c}", align_bytes=64) for c in range(2)]
         nc.vector.tensor_copy(vw[0][:], twin[0][:].bitcast(U32).indirect(offs_sb[:]))
-
+        w4raw.append(keep.tile([NP, A1, H], U8, name="w4raw1", tag="twin0", align_bytes=64))
+        nc.sync.dma_start(w4raw[1][:].bitcast(I32), w4src[1].bitcast(I32))
+        order_w4(0)
         nc.vector.tensor_copy(vw[1][:], twin[1][:].bitcast(U32).indirect(offs_sb[:]))
         for c in range(2):
-            nc.vector.tensor_copy(vw[2][:, N * c : N * (c + 1)],
+            nc.vector.tensor_copy(vlast[c][:],
                                   twin[2][:].bitcast(U32).indirect(offs_sb[:, 32 * c : 32 * (c + 1)]))
 
+        w4w.append(shared.tile([NP, 4, A1, 256], U8, name="w4w1", align_bytes=64, offset=4 * S + 4 * T))
         order_w4(1)
         w2rows = w2.rearrange("(a p j) (b n) -> a b p j n", a=A2, j=4, b=A2)
         w2raw = {}
         for b in range(A2):
             for a in range(A2):
-                raw = keep.tile([NP, 4, N], F32, name=f"w2raw{a}{b}", tag=(("twin0", "twin1"), ("twin2", "w4raw1"))[b][a], align_bytes=64)
+                if (a, b) == (0, 1):
+                    raw = shared.tile([NP, 4, N], F32, name="w2raw01", align_bytes=64, offset=4 * S)
+                else:
+                    raw = keep.tile([NP, 4, N], F32, name=f"w2raw{a}{b}", tag=(("w4raw0", "twin1"), ("", "twin0"))[b][a], align_bytes=64)
                 nc.sync.dma_start(raw[:], w2rows[a, b])
                 w2raw[a, b] = raw
 
         def first_pass(acc, b, t, a, c):
             cols = slice(N * c, N * (c + 1))
-            nc.tensor.matmul_mx(out=acc[:], lhsT=w4w[:, b, t, a, :].bitcast(FP4X4), lhsT_scale=planes[:, a, S + N * b + NP * t : S + N * b + NP * (t + 1)],
-                                rhs=vw[a][:, cols].bitcast(FP8X4), rhs_scale=planes[:, a, cols],
+            words = vlast[c][:] if a == A1 - 1 else vw[a][:, cols]
+            nc.tensor.matmul_mx(out=acc[:], lhsT=w4w[b][:, t, a, :].bitcast(FP4X4), lhsT_scale=planes[:, a, S + N * b + NP * t : S + N * b + NP * (t + 1)],
+                                rhs=words.bitcast(FP8X4), rhs_scale=planes[:, a, cols],
                                 start=(a == 0), stop=(a == A1 - 1))
 
-        def weave_w2(b, tag):
+        def weave_w2(b, tag, qtag):
             made = []
             for a in range(A2):
                 wb = keep.tile([NP, 4, NP, 4], BF16, name=f"wb{a}{b}", tag=tag[a], align_bytes=64)
                 for c in range(4):
                     nc.scalar.copy(
-                        wb[:].rearrange("p t m j -> p m t j")[:, 32 * c : 32 * (c + 1)],
-                        w2raw[a, b][:].rearrange("p j (m t) -> p m t j", t=4)[:, 32 * c : 32 * (c + 1)])
-                wq = keep.tile([NP, N], U32, name=f"wq{a}{b}", align_bytes=64)
+                        wb[:].rearrange("p t m j -> p m j t")[:, 32 * c : 32 * (c + 1)],
+                        w2raw[a, b][:].rearrange("p j (m t) -> p m j t", t=4)[:, 32 * c : 32 * (c + 1)])
+                wq = keep.tile([NP, N], U32, name=f"wq{a}{b}", tag=qtag[a], align_bytes=64)
                 ws = keep.tile([NP, N], U8, name=f"ws{a}{b}", align_bytes=64)
                 nc.vector.quantize_mx(out=wq[:].bitcast(FP8X4), scales=ws[:], in_=wb[:].rearrange("p t m j -> p (t m j)"))
                 made.append((wq, ws))
             return made
 
+        early = {(0, t, c): psum.tile([NP, N], F32, name="bank1", tag="bank1") for t in range(2) for c in range(2)}
+        for a in range(A1 - 1):
+            for (b, t, c), acc in early.items():
+                first_pass(acc, b, t, a, c)
+
         x32, fine = [], []
         for b in range(A2):
             xb32 = keep.tile([NP, 4, P], F32, name=f"x32{b}", tag=f"x32{b}", align_bytes=64)
             hs = []
-            if b == 0:
-                fb = keep.tile([NP, 4, P], F32, name="fine0")
+            fb = []
             for t in range(4):
                 h = keep.tile([NP, S], F32, name=f"h{b}{t}")
                 for c in range(2):
-                    acc = psum.tile([NP, N], F32, name="bank", tag="bank")
-                    for a in range(A1):
-                        first_pass(acc, b, t, a, c)
+                    if (b, t, c) in early:
+                        acc = early[b, t, c]
+                        first_pass(acc, b, t, A1 - 1, c)
+                    else:
+                        acc = psum.tile([NP, N], F32, name="bank1", tag="bank1")
+                        for a in range(A1):
+                            first_pass(acc, b, t, a, c)
                     nc.scalar.activation(h[:, N * c : N * (c + 1)], acc[:], TANH)
-                if b == 1:
-                    nc.vector.tensor_tensor(xb32[:, t, :], h[:].indirect(pos1_sb[:]), gfull[:, t, :], MULT)
+                nc.vector.tensor_tensor(xb32[:, t, :], h[:].indirect(pos1_sb[:]), gfull[b][t], MULT)
                 if b == 0:
-                    nc.vector.tensor_copy(xb32[:, t, :], h[:].indirect(pos1_sb[:]))
-                    nc.vector.tensor_copy(fb[:, t, :], h[:].indirect(pos2_sb[:]))
+                    f = keep.tile([NP, P], F32, name=f"fine0{t}", tag=f"fine0{t}", align_bytes=64)
+                    nc.vector.tensor_copy(f[:], h[:].indirect(pos2_sb[:]))
+                    fb.append(f[:])
                 hs.append(h)
             if b == 1:
-                fb = keep.tile([NP, 4, P], F32, name="fine1", tag="gfull1")
-                for t in range(4):
-                    nc.vector.tensor_copy(fb[:, t, :], hs[t][:].indirect(pos2_sb[:]))
+                f3 = keep.tile([NP, 3, P], F32, name="fine1", tag="gfull1")
+                for t in range(3):
+                    nc.vector.tensor_copy(f3[:, t, :], hs[t][:].indirect(pos2_sb[:]))
+                    fb.append(f3[:, t, :])
             x32.append(xb32)
             fine.append(fb)
 
-        wmx = [weave_w2(0, ("wb00", "wb10"))]
+        wmx = [weave_w2(0, ("wb00", "wb10"), ("wq00", "wq10"))]
 
         xmx = []
         for a in range(A2):
-            src = x32[a]
             if a == 0:
-                src = keep.tile([NP, 4, P], BF16, name="xg", tag="w4w", align_bytes=64)
-                for t in range(4):
-                    nc.scalar.activation(src[:, t, :], x32[a][:, t, :], COPY, scale=gcol[:, a, t : t + 1])
-            xb = keep.tile([NP, P, 4], BF16, name=f"xb{a}", align_bytes=64)
-            nc.scalar.copy(xb[:], src[:].rearrange("p t m -> p m t"))
+                xb = shared.tile([NP, P, 4], BF16, name="xb0", align_bytes=64, offset=4 * S + 4 * T)
+            else:
+                xb = keep.tile([NP, P, 4], BF16, name="xb1", tag="xb1", align_bytes=64)
+            nc.scalar.copy(xb[:].rearrange("p (c i) t -> p c t i", i=4), x32[a][:].rearrange("p t (c i) -> p c t i", i=4))
             xq = keep.tile([NP, P], U32, name=f"xq{a}", align_bytes=64)
             xs = keep.tile([NP, P], U8, name=f"xs{a}", align_bytes=64)
             nc.vector.quantize_mx(out=xq[:].bitcast(FP8X4), scales=xs[:], in_=xb[:].rearrange("p m t -> p (m t)"))
             xmx.append((xq, xs))
 
-        wmx.append(weave_w2(1, ("x321", "x320")))
+        f = keep.tile([NP, P], F32, name="fine13", tag="xb1", align_bytes=64)
+        nc.vector.tensor_copy(f[:], hs[3][:].indirect(pos2_sb[:]))
+        fine[1].append(f[:])
 
         out_rows = out.rearrange("(b p t) m -> b t p m", b=A2, t=4)
 
         def times_y(b, t):
-            acc = psum.tile([NP, N], F32, name="bank", tag="bank")
+            acc = psum.tile([NP, N], F32, name="bank2", tag="bank2")
             cols = slice(NP * t, NP * (t + 1))
             for a in range(A2):
                 nc.tensor.matmul_mx(out=acc[:], lhsT=wmx[b][a][0][:, cols].bitcast(FP8X4), lhsT_scale=wmx[b][a][1][:, cols],
@@ -187,12 +204,12 @@ def tile_list_well_log_corrector_kernel(tc, tab_words, tab_scales, offs, pos1, p
 
         def times_fine(acc, b, t, m):
             fy = ring.tile([NP, P], F32, name="fy")
-            nc.vector.tensor_tensor(fy[:, m], acc[:, m], fine[b][:, t, m], MULT)
+            nc.vector.tensor_tensor(fy[:, m], acc[:, m], fine[b][t][:, m], MULT)
             return fy
 
         def finish(b, t, m, fy):
             res = ring.tile([NP, P], F32, name="res")
-            nc.vector.scalar_tensor_tensor(res[:, m], fy[:, m], dcol[:, b, t : t + 1], fine[b][:, t, m], ADD, MULT)
+            nc.vector.scalar_tensor_tensor(res[:, m], fy[:, m], dcol[:, b, t : t + 1], fine[b][t][:, m], ADD, MULT)
             nc.sync.dma_start(out_rows[b, t][:, m], res[:, m])
 
         held = None
@@ -205,4 +222,6 @@ def tile_list_well_log_corrector_kernel(tc, tab_words, tab_scales, offs, pos1, p
                     if held is not None:
                         finish(*held)
                     held = (b, t, m, fy)
+                if (b, t) == (0, 2):
+                    wmx.append(weave_w2(1, ("x321", "wb11"), ("fine00", "fine01")))
         finish(*held)

@@ -17,7 +17,10 @@ MULT = mybir.AluOpType.mult
 ADD = mybir.AluOpType.add
 TANH = mybir.ActivationFunctionType.Tanh
 
+IDENT = mybir.ActivationFunctionType.Identity
+
 NP = 128
+SHARE = 6
 A1 = K // 512
 A2 = H // 512
 N = 512
@@ -29,7 +32,8 @@ def tile_list_well_log_corrector_kernel(tc, tab_words, tab_scales, offs, pos1, p
         lists = ctx.enter_context(tc.tile_pool(name="lists", bufs=1))
         keep = ctx.enter_context(tc.tile_pool(name="keep", bufs=1))
         shared = ctx.enter_context(tc.tile_pool(name="shared", bufs=1))
-        ring = ctx.enter_context(tc.tile_pool(name="ring", bufs=4))
+        late = ctx.enter_context(tc.tile_pool(name="late", bufs=1))
+        ring = ctx.enter_context(tc.tile_pool(name="ring", bufs=9))
         psum = ctx.enter_context(tc.psum_pool(name="psum", bufs=4))
 
         offs_sb = lists.tile([NP, S // 16], U16, name="offs_sb")
@@ -124,18 +128,25 @@ def tile_list_well_log_corrector_kernel(tc, tab_words, tab_scales, offs, pos1, p
                                 rhs=words.bitcast(FP8X4), rhs_scale=planes[:, a, cols],
                                 start=(a == 0), stop=(a == A1 - 1))
 
-        def weave_w2(b, tag, qtag):
+        def weave_w2(b):
             made = []
             for a in range(A2):
-                wb = keep.tile([NP, 4, NP, 4], BF16, name=f"wb{a}{b}", tag=tag[a], align_bytes=64)
+                if b == 0:
+                    wb = keep.tile([NP, 4, NP, 4], BF16, name=f"wb{a}{b}", tag=f"wb{a}{b}", align_bytes=64)
+                else:
+                    wb = late.tile([NP, 4, NP, 4], BF16, name=f"wb{a}{b}", align_bytes=64, offset=16 * P + 8 * P * a)
                 for c in range(4):
                     nc.scalar.copy(
                         wb[:].rearrange("p t m j -> p m j t")[:, 32 * c : 32 * (c + 1)],
                         w2raw[a, b][:].rearrange("p j (m t) -> p m j t", t=4)[:, 32 * c : 32 * (c + 1)])
-                wq = keep.tile([NP, N], U32, name=f"wq{a}{b}", tag=qtag[a], align_bytes=64)
+                wq = keep.tile([NP, N], U32, name=f"wq{a}{b}", align_bytes=64)
                 ws = keep.tile([NP, N], U8, name=f"ws{a}{b}", align_bytes=64)
                 nc.vector.quantize_mx(out=wq[:].bitcast(FP8X4), scales=ws[:], in_=wb[:].rearrange("p t m j -> p (t m j)"))
                 made.append((wq, ws))
+                if b == 1:
+                    f = late.tile([NP, P], F32, name=f"fine1{2 + a}", align_bytes=64, offset=16 * P + 8 * P * a)
+                    nc.vector.tensor_copy(f[:], hs[2 + a][:].indirect(pos2_sb[:]))
+                    fine[1].append(f[:])
             return made
 
         early = {(0, t, c): psum.tile([NP, N], F32, name="bank1", tag="bank1") for t in range(2) for c in range(2)}
@@ -145,7 +156,7 @@ def tile_list_well_log_corrector_kernel(tc, tab_words, tab_scales, offs, pos1, p
 
         x32, fine = [], []
         for b in range(A2):
-            xb32 = keep.tile([NP, 4, P], F32, name=f"x32{b}", tag=f"x32{b}", align_bytes=64)
+            xb32 = late.tile([NP, 4, P], F32, name=f"x32{b}", align_bytes=64, offset=16 * P * b)
             hs = []
             fb = []
             for t in range(4):
@@ -160,20 +171,20 @@ def tile_list_well_log_corrector_kernel(tc, tab_words, tab_scales, offs, pos1, p
                             first_pass(acc, b, t, a, c)
                     nc.scalar.activation(h[:, N * c : N * (c + 1)], acc[:], TANH)
                 nc.vector.tensor_tensor(xb32[:, t, :], h[:].indirect(pos1_sb[:]), gfull[b][t], MULT)
-                if b == 0:
+                if b == 0 and t < 3:
                     f = keep.tile([NP, P], F32, name=f"fine0{t}", tag=f"fine0{t}", align_bytes=64)
                     nc.vector.tensor_copy(f[:], h[:].indirect(pos2_sb[:]))
                     fb.append(f[:])
                 hs.append(h)
             if b == 1:
-                f3 = keep.tile([NP, 3, P], F32, name="fine1", tag="gfull1")
-                for t in range(3):
-                    nc.vector.tensor_copy(f3[:, t, :], hs[t][:].indirect(pos2_sb[:]))
-                    fb.append(f3[:, t, :])
+                f = keep.tile([NP, P], F32, name="fine03", tag="gfull1")
+                nc.vector.tensor_copy(f[:], h03[:].indirect(pos2_sb[:]))
+                fine[0].append(f[:])
+            h03 = hs[3]
             x32.append(xb32)
             fine.append(fb)
 
-        wmx = [weave_w2(0, ("wb00", "wb10"), ("wq00", "wq10"))]
+        wmx = [weave_w2(0)]
 
         xmx = []
         for a in range(A2):
@@ -187,9 +198,10 @@ def tile_list_well_log_corrector_kernel(tc, tab_words, tab_scales, offs, pos1, p
             nc.vector.quantize_mx(out=xq[:].bitcast(FP8X4), scales=xs[:], in_=xb[:].rearrange("p m t -> p (m t)"))
             xmx.append((xq, xs))
 
-        f = keep.tile([NP, P], F32, name="fine13", tag="xb1", align_bytes=64)
-        nc.vector.tensor_copy(f[:], hs[3][:].indirect(pos2_sb[:]))
-        fine[1].append(f[:])
+        f2 = keep.tile([NP, 2, P], F32, name="fine1", tag="xb1", align_bytes=64)
+        for t in range(2):
+            nc.vector.tensor_copy(f2[:, t, :], hs[t][:].indirect(pos2_sb[:]))
+            fine[1].append(f2[:, t, :])
 
         out_rows = out.rearrange("(b p t) m -> b t p m", b=A2, t=4)
 
@@ -209,8 +221,14 @@ def tile_list_well_log_corrector_kernel(tc, tab_words, tab_scales, offs, pos1, p
 
         def finish(b, t, m, fy):
             res = ring.tile([NP, P], F32, name="res")
-            nc.vector.scalar_tensor_tensor(res[:, m], fy[:, m], dcol[:, b, t : t + 1], fine[b][t][:, m], ADD, MULT)
-            nc.sync.dma_start(out_rows[b, t][:, m], res[:, m])
+            if 4 * b + t < SHARE:
+                fyd = ring.tile([NP, P], F32, name="fyd", bufs=3)
+                nc.scalar.activation(fyd[:], fy[:], IDENT, bias=dcol[:, b, t : t + 1])
+                nc.gpsimd.tensor_tensor(res[:], fyd[:], fine[b][t], MULT)
+            else:
+                nc.vector.scalar_tensor_tensor(res[:, m], fy[:, m], dcol[:, b, t : t + 1], fine[b][t][:, m], ADD, MULT)
+            queue = nc.sync if 4 * b + t < SHARE else nc.scalar
+            queue.dma_start(out_rows[b, t][:, m], res[:, m])
 
         held = None
         for b in range(A2):
@@ -223,5 +241,5 @@ def tile_list_well_log_corrector_kernel(tc, tab_words, tab_scales, offs, pos1, p
                         finish(*held)
                     held = (b, t, m, fy)
                 if (b, t) == (0, 2):
-                    wmx.append(weave_w2(1, ("x321", "wb11"), ("fine00", "fine01")))
+                    wmx.append(weave_w2(1))
         finish(*held)

@@ -16,14 +16,25 @@ FP4X4 = mybir.dt.float4_e2m1fn_x4
 MULT = mybir.AluOpType.mult
 ADD = mybir.AluOpType.add
 TANH = mybir.ActivationFunctionType.Tanh
-
 IDENT = mybir.ActivationFunctionType.Identity
 
 NP = 128
-SHARE = 6
 A1 = K // 512
 A2 = H // 512
 N = 512
+LINK = 64
+GPSIMD_TILES = 5
+EARLY_TILES = 2
+EARLY_FINE = 3
+WEAVE_STEPS = 4
+OUT_PIECES = 9
+
+WORDS = 4 * S
+WINDOW = 4 * T
+W4_RAW = A1 * H
+W4_PAIR = W4_RAW // 2
+X32 = 16 * P
+X16 = 8 * P
 
 
 def tile_list_well_log_corrector_kernel(tc, tab_words, tab_scales, offs, pos1, pos2, w4_words, w4_scales, gain, w2, d, out):
@@ -33,134 +44,151 @@ def tile_list_well_log_corrector_kernel(tc, tab_words, tab_scales, offs, pos1, p
         keep = ctx.enter_context(tc.tile_pool(name="keep", bufs=1))
         shared = ctx.enter_context(tc.tile_pool(name="shared", bufs=1))
         late = ctx.enter_context(tc.tile_pool(name="late", bufs=1))
-        ring = ctx.enter_context(tc.tile_pool(name="ring", bufs=9))
-        psum = ctx.enter_context(tc.psum_pool(name="psum", bufs=4))
+        first = ctx.enter_context(tc.tile_pool(name="first", bufs=1))
+        second = ctx.enter_context(tc.tile_pool(name="second", bufs=1))
+        ring = ctx.enter_context(tc.tile_pool(name="ring", bufs=OUT_PIECES))
+        psum = ctx.enter_context(tc.psum_pool(name="psum", bufs=2 * EARLY_TILES))
 
         offs_sb = lists.tile([NP, S // 16], U16, name="offs_sb")
         pos1_sb = lists.tile([NP, P // 16], U16, name="pos1_sb")
         pos2_sb = lists.tile([NP, P // 16], U16, name="pos2_sb")
-        swin = keep.tile([NP, T], U8, name="swin", tag="swin", align_bytes=64)
-        s4raw = shared.tile([NP, H], U8, name="s4raw", align_bytes=64, offset=S)
-        gcol = keep.tile([NP, A2, 4], F32, name="gcol")
-        dcol = keep.tile([NP, A2, 4], F32, name="dcol")
-        w4raw = [keep.tile([NP, A1, H], U8, name=f"w4raw{b}", tag="w4raw0", align_bytes=64) for b in range(1)]
-        w4src = w4_words.rearrange("a p (b c) -> b p a c", b=A2)
-        twin = [keep.tile([NP, T], I32, name=f"twin{a}", tag=f"twin{a}", align_bytes=64) for a in range(A1 - 1)]
-        for queue, tile, rows in ((nc.sync, swin, tab_scales), (nc.scalar, s4raw, w4_scales)):
+        tab_rows = keep.tile([NP, T], U8, name="tab_rows", tag="rows", align_bytes=64)
+        w4_rows = shared.tile([NP, H], U8, name="w4_rows", align_bytes=64, offset=S)
+        gain_col = keep.tile([NP, A2, 4], F32, name="gain_col")
+        d_col = keep.tile([NP, A2, 4], F32, name="d_col")
+        w4_raw = [second.tile([NP, A1, H], U8, name="w4_raw0", align_bytes=64, offset=X16 - LINK)]
+        w4_src = w4_words.rearrange("a p (b c) -> b p a c", b=A2)
+        window = [first.tile([NP, T], I32, name="window0", align_bytes=64, offset=W4_RAW - LINK),
+                  keep.tile([NP, T], I32, name="window1", tag="window1", align_bytes=64)]
+        for queue, tile, rows in ((nc.sync, tab_rows, tab_scales), (nc.scalar, w4_rows, w4_scales)):
             queue.dma_start(tile[16:48, :].bitcast(I32), rows[0:2].rearrange("a s c -> s a c").bitcast(I32))
             queue.dma_start(tile[48:64, :].bitcast(I32), rows[2].bitcast(I32))
         nc.sync.dma_start(offs_sb[:], offs)
-        nc.sync.dma_start(twin[0][:], tab_words[0].rearrange("p t i -> p (t i)").bitcast(I32))
+        nc.sync.dma_start(window[0][:], tab_words[0].rearrange("p t i -> p (t i)").bitcast(I32))
         nc.sync.dma_start(pos1_sb[:], pos1)
-        nc.scalar.dma_start(gcol[:], gain.rearrange("(b p t) -> p b t", b=A2, t=4))
+        nc.scalar.dma_start(gain_col[:], gain.rearrange("(b p t) -> p b t", b=A2, t=4))
         nc.sync.dma_start(pos2_sb[:], pos2)
-        nc.scalar.dma_start(dcol[:], d.rearrange("(b p t) -> p b t", b=A2, t=4))
-        nc.sync.dma_start(w4raw[0][:].bitcast(I32), w4src[0].bitcast(I32))
-        for tile in (swin, s4raw):
+        nc.scalar.dma_start(d_col[:], d.rearrange("(b p t) -> p b t", b=A2, t=4))
+        nc.sync.dma_start(w4_raw[0][:].bitcast(I32), w4_src[0].bitcast(I32))
+        for tile in (tab_rows, w4_rows):
             nc.vector.memset(tile[0:16, :].bitcast(I32), 0)
             nc.vector.memset(tile[64:128, :].bitcast(I32), 0)
 
-        warm = keep.tile([NP, 8], F32, name="warm")
-        nc.vector.memset(warm[:], 0.0)
-        warm2 = keep.tile([NP, 8], F32, name="warm2")
-        nc.scalar.activation(warm2[:], warm[:], TANH)
+        warm_in = keep.tile([NP, 8], F32, name="warm_in")
+        nc.vector.memset(warm_in[:], 0.0)
+        warm_out = keep.tile([NP, 8], F32, name="warm_out")
+        nc.scalar.activation(warm_out[:], warm_in[:], TANH)
 
-        nc.sync.dma_start(twin[1][:], tab_words[1].rearrange("p t i -> p (t i)").bitcast(I32))
+        nc.sync.dma_start(window[1][:], tab_words[1].rearrange("p t i -> p (t i)").bitcast(I32))
         planes = keep.tile([NP, A1, S + H], U8, name="planes", align_bytes=64)
         nc.gpsimd.memset(planes[:].bitcast(I32), 0)
 
-        w4w = [keep.tile([NP, 4, A1, 256], U8, name="w4w0", align_bytes=64)]
+        w4_pair = [keep.tile([NP, 2, A1, 2 * NP], U8, name="w4_pair0", align_bytes=64)]
 
-        def order_w4(b):
+        def order_w4(g):
             nc.vector.tensor_copy(
-                w4w[b][:].bitcast(U16),
-                w4raw[b][:].bitcast(U16).rearrange("p a (m t) -> p t a m", t=4))
+                w4_pair[g][:].bitcast(U16),
+                w4_raw[g // 2][:].bitcast(U16).rearrange("p a (m t) -> p t a m", t=4)[:, 2 * (g % 2) : 2 * (g % 2) + 2])
 
-        gs = shared.tile([NP, S], U8, name="gs", align_bytes=64, offset=4 * S - S // 2)
-        both = keep.tile([NP, S + H], U8, name="both", tag="swin", align_bytes=64)
-        nc.vector.tensor_copy(gs[:], swin[:].indirect(offs_sb[:]))
+        picked_rows = shared.tile([NP, S], U8, name="picked_rows", align_bytes=64, offset=WORDS - S // 2)
+        both_rows = keep.tile([NP, S + H], U8, name="both_rows", tag="rows", align_bytes=64)
+        nc.vector.tensor_copy(picked_rows[:], tab_rows[:].indirect(offs_sb[:]))
         nc.vector.tensor_copy(
-            both[:, S:].rearrange("p (b t m) -> p b t m", b=A2, t=4),
-            s4raw[:].rearrange("p (b m t) -> p b t m", b=A2, t=4))
-        nc.vector.tensor_copy(both[:, :S].bitcast(I32), gs[:].bitcast(I32))
+            both_rows[:, S:].rearrange("p (b t m) -> p b t m", b=A2, t=4),
+            w4_rows[:].rearrange("p (b m t) -> p b t m", b=A2, t=4))
+        nc.vector.tensor_copy(both_rows[:, :S].bitcast(I32), picked_rows[:].bitcast(I32))
         for q in range(4):
-            nc.sync.dma_start(planes[32 * q : 32 * q + 4, 0:2, :].bitcast(I32), both[16 + 8 * q : 24 + 8 * q, :].bitcast(I32))
-        twin.append(shared.tile([NP, T], I32, name="twin2", align_bytes=64, offset=4 * S + 64))
-        nc.sync.dma_start(twin[2][:], tab_words[2].rearrange("p t i -> p (t i)").bitcast(I32))
+            nc.sync.dma_start(planes[32 * q : 32 * q + 4, 0:2, :].bitcast(I32), both_rows[16 + 8 * q : 24 + 8 * q, :].bitcast(I32))
+        window.append(shared.tile([NP, T], I32, name="window2", align_bytes=64, offset=WORDS + LINK))
+        nc.sync.dma_start(window[2][:], tab_words[2].rearrange("p t i -> p (t i)").bitcast(I32))
         for q in range(4):
-            nc.sync.dma_start(planes[32 * q : 32 * q + 4, 2, :].bitcast(I32), both[48 + 4 * q : 52 + 4 * q, :].bitcast(I32))
-        g1 = keep.tile([NP, 4, P], F32, name="gfull1", tag="gfull1")
-        gfull = [[keep.tile([NP, P], F32, name=f"gfull0{t}", tag=("wb00", "wb10", "gfull02", "gfull03")[t], align_bytes=64)[:] for t in range(4)],
-                 [g1[:, t, :] for t in range(4)]]
+            nc.sync.dma_start(planes[32 * q : 32 * q + 4, 2, :].bitcast(I32), both_rows[48 + 4 * q : 52 + 4 * q, :].bitcast(I32))
+
+        gain1 = keep.tile([NP, 4, P], F32, name="gain1", tag="gain1")
+        gain_full = [[keep.tile([NP, P], F32, name=f"gain0{t}", tag=("w2_bf00", "w2_bf10", "gain02", "gain03")[t], align_bytes=64)[:] for t in range(4)],
+                     [gain1[:, t, :] for t in range(4)]]
         for b in range(A2):
             for t in range(4):
-                nc.scalar.copy(gfull[b][t], gcol[:, b, t : t + 1].to_broadcast([NP, P]))
+                nc.scalar.copy(gain_full[b][t], gain_col[:, b, t : t + 1].to_broadcast([NP, P]))
 
-        vw = [shared.tile([NP, S], U32, name="vw0", align_bytes=64, offset=0)]
-        vw.append(keep.tile([NP, S], U32, name="vw1", align_bytes=64))
-        vlast = [keep.tile([NP, N], U32, name=f"vlast{c}", align_bytes=64) for c in range(2)]
-        nc.vector.tensor_copy(vw[0][:], twin[0][:].bitcast(U32).indirect(offs_sb[:]))
-        w4raw.append(keep.tile([NP, A1, H], U8, name="w4raw1", tag="twin0", align_bytes=64))
-        nc.sync.dma_start(w4raw[1][:].bitcast(I32), w4src[1].bitcast(I32))
+        words = [shared.tile([NP, S], U32, name="words0", align_bytes=64, offset=0)]
+        words.append(keep.tile([NP, S], U32, name="words1", align_bytes=64))
+        words_last = [keep.tile([NP, N], U32, name=f"words_last{c}", align_bytes=64) for c in range(2)]
+        nc.vector.tensor_copy(words[0][:], window[0][:].bitcast(U32).indirect(offs_sb[:]))
+        w4_raw.append(first.tile([NP, A1, H], U8, name="w4_raw1", align_bytes=64, offset=0))
+        nc.sync.dma_start(w4_raw[1][:].bitcast(I32), w4_src[1].bitcast(I32))
         order_w4(0)
-        nc.vector.tensor_copy(vw[1][:], twin[1][:].bitcast(U32).indirect(offs_sb[:]))
+        nc.vector.tensor_copy(words[1][:], window[1][:].bitcast(U32).indirect(offs_sb[:]))
         for c in range(2):
-            nc.vector.tensor_copy(vlast[c][:],
-                                  twin[2][:].bitcast(U32).indirect(offs_sb[:, 32 * c : 32 * (c + 1)]))
+            nc.vector.tensor_copy(words_last[c][:],
+                                  window[2][:].bitcast(U32).indirect(offs_sb[:, N // 16 * c : N // 16 * (c + 1)]))
 
-        w4w.append(shared.tile([NP, 4, A1, 256], U8, name="w4w1", align_bytes=64, offset=4 * S + 4 * T))
-        order_w4(1)
-        w2rows = w2.rearrange("(a p j) (b n) -> a b p j n", a=A2, j=4, b=A2)
-        w2raw = {}
+        w4_pair.append(shared.tile([NP, 2, A1, 2 * NP], U8, name="w4_pair1", align_bytes=64, offset=WORDS + WINDOW))
+        w4_pair.append(second.tile([NP, 2, A1, 2 * NP], U8, name="w4_pair2", align_bytes=64, offset=X16 - W4_PAIR))
+        w4_pair.append(second.tile([NP, 2, A1, 2 * NP], U8, name="w4_pair3", align_bytes=64, offset=X16))
+        for g in range(1, 4):
+            order_w4(g)
+
+        w2_src = w2.rearrange("(a p j) (b n) -> a b p j n", a=A2, j=4, b=A2)
+        w2_raw = {}
         for b in range(A2):
             for a in range(A2):
-                if (a, b) == (0, 1):
-                    raw = shared.tile([NP, 4, N], F32, name="w2raw01", align_bytes=64, offset=4 * S)
+                if (a, b) == (0, 0):
+                    raw = first.tile([NP, 4, N], F32, name="w2_raw00", align_bytes=64, offset=W4_RAW + WINDOW - 2 * LINK)
+                elif (a, b) == (1, 0):
+                    raw = keep.tile([NP, 4, N], F32, name="w2_raw10", tag="window1", align_bytes=64)
+                elif (a, b) == (0, 1):
+                    raw = shared.tile([NP, 4, N], F32, name="w2_raw01", align_bytes=64, offset=WORDS)
                 else:
-                    raw = keep.tile([NP, 4, N], F32, name=f"w2raw{a}{b}", tag=(("w4raw0", "twin1"), ("", "twin0"))[b][a], align_bytes=64)
-                nc.sync.dma_start(raw[:], w2rows[a, b])
-                w2raw[a, b] = raw
+                    raw = first.tile([NP, 4, N], F32, name="w2_raw11", align_bytes=64, offset=0)
+                nc.sync.dma_start(raw[:], w2_src[a, b])
+                w2_raw[a, b] = raw
 
         def first_pass(acc, b, t, a, c):
             cols = slice(N * c, N * (c + 1))
-            words = vlast[c][:] if a == A1 - 1 else vw[a][:, cols]
-            nc.tensor.matmul_mx(out=acc[:], lhsT=w4w[b][:, t, a, :].bitcast(FP4X4), lhsT_scale=planes[:, a, S + N * b + NP * t : S + N * b + NP * (t + 1)],
-                                rhs=words.bitcast(FP8X4), rhs_scale=planes[:, a, cols],
+            moving = words_last[c][:] if a == A1 - 1 else words[a][:, cols]
+            w4_cols = slice(S + N * b + NP * t, S + N * b + NP * (t + 1))
+            nc.tensor.matmul_mx(out=acc[:], lhsT=w4_pair[2 * b + t // 2][:, t % 2, a, :].bitcast(FP4X4), lhsT_scale=planes[:, a, w4_cols],
+                                rhs=moving.bitcast(FP8X4), rhs_scale=planes[:, a, cols],
                                 start=(a == 0), stop=(a == A1 - 1))
 
-        def weave_w2(b):
+        hs, fine = {}, {}
+
+        def gather_fine(b, t, dst):
+            nc.vector.tensor_copy(dst, hs[b, t][:].indirect(pos2_sb[:]))
+            fine[b, t] = dst
+
+        def quantise_w2(b):
             made = []
             for a in range(A2):
                 if b == 0:
-                    wb = keep.tile([NP, 4, NP, 4], BF16, name=f"wb{a}{b}", tag=f"wb{a}{b}", align_bytes=64)
+                    w2_bf = keep.tile([NP, 4, NP, 4], BF16, name=f"w2_bf{a}{b}", tag=f"w2_bf{a}{b}", align_bytes=64)
                 else:
-                    wb = late.tile([NP, 4, NP, 4], BF16, name=f"wb{a}{b}", align_bytes=64, offset=16 * P + 8 * P * a)
-                for c in range(4):
-                    nc.scalar.copy(
-                        wb[:].rearrange("p t m j -> p m j t")[:, 32 * c : 32 * (c + 1)],
-                        w2raw[a, b][:].rearrange("p j (m t) -> p m j t", t=4)[:, 32 * c : 32 * (c + 1)])
-                wq = keep.tile([NP, N], U32, name=f"wq{a}{b}", align_bytes=64)
-                ws = keep.tile([NP, N], U8, name=f"ws{a}{b}", align_bytes=64)
-                nc.vector.quantize_mx(out=wq[:].bitcast(FP8X4), scales=ws[:], in_=wb[:].rearrange("p t m j -> p (t m j)"))
-                made.append((wq, ws))
+                    w2_bf = late.tile([NP, 4, NP, 4], BF16, name=f"w2_bf{a}{b}", align_bytes=64, offset=X32 + X16 * a)
+                for step in range(WEAVE_STEPS):
+                    part = slice(NP // WEAVE_STEPS * step, NP // WEAVE_STEPS * (step + 1))
+                    nc.scalar.copy(w2_bf[:].rearrange("p t m j -> p m j t")[:, part],
+                                   w2_raw[a, b][:].rearrange("p j (m t) -> p m j t", t=4)[:, part])
+                codes = keep.tile([NP, N], U32, name=f"w2_codes{a}{b}", align_bytes=64)
+                scales = keep.tile([NP, N], U8, name=f"w2_scales{a}{b}", align_bytes=64)
+                nc.vector.quantize_mx(out=codes[:].bitcast(FP8X4), scales=scales[:], in_=w2_bf[:].rearrange("p t m j -> p (t m j)"))
+                made.append((codes, scales))
                 if b == 1:
-                    f = late.tile([NP, P], F32, name=f"fine1{2 + a}", align_bytes=64, offset=16 * P + 8 * P * a)
-                    nc.vector.tensor_copy(f[:], hs[2 + a][:].indirect(pos2_sb[:]))
-                    fine[1].append(f[:])
+                    f = late.tile([NP, P], F32, name=f"fine1{2 + a}", align_bytes=64, offset=X32 + X16 * a)
+                    gather_fine(1, 2 + a, f[:])
             return made
 
-        early = {(0, t, c): psum.tile([NP, N], F32, name="bank1", tag="bank1") for t in range(2) for c in range(2)}
+        early = {(0, t, c): psum.tile([NP, N], F32, name="bank1", tag="bank1") for t in range(EARLY_TILES) for c in range(2)}
         for a in range(A1 - 1):
             for (b, t, c), acc in early.items():
                 first_pass(acc, b, t, a, c)
 
-        x32, fine = [], []
+        x32 = []
         for b in range(A2):
-            xb32 = late.tile([NP, 4, P], F32, name=f"x32{b}", align_bytes=64, offset=16 * P * b)
-            hs = []
-            fb = []
+            x_half = late.tile([NP, 4, P], F32, name=f"x32{b}", align_bytes=64, offset=X32 * b)
             for t in range(4):
                 h = keep.tile([NP, S], F32, name=f"h{b}{t}")
+                hs[b, t] = h
                 for c in range(2):
                     if (b, t, c) in early:
                         acc = early[b, t, c]
@@ -170,70 +198,64 @@ def tile_list_well_log_corrector_kernel(tc, tab_words, tab_scales, offs, pos1, p
                         for a in range(A1):
                             first_pass(acc, b, t, a, c)
                     nc.scalar.activation(h[:, N * c : N * (c + 1)], acc[:], TANH)
-                nc.vector.tensor_tensor(xb32[:, t, :], h[:].indirect(pos1_sb[:]), gfull[b][t], MULT)
-                if b == 0 and t < 3:
+                nc.vector.tensor_tensor(x_half[:, t, :], h[:].indirect(pos1_sb[:]), gain_full[b][t], MULT)
+                if 4 * b + t < EARLY_FINE:
                     f = keep.tile([NP, P], F32, name=f"fine0{t}", tag=f"fine0{t}", align_bytes=64)
-                    nc.vector.tensor_copy(f[:], h[:].indirect(pos2_sb[:]))
-                    fb.append(f[:])
-                hs.append(h)
-            if b == 1:
-                f = keep.tile([NP, P], F32, name="fine03", tag="gfull1")
-                nc.vector.tensor_copy(f[:], h03[:].indirect(pos2_sb[:]))
-                fine[0].append(f[:])
-            h03 = hs[3]
-            x32.append(xb32)
-            fine.append(fb)
+                    gather_fine(b, t, f[:])
+            x32.append(x_half)
+        f = keep.tile([NP, P], F32, name="fine03", tag="gain1")
+        gather_fine(0, 3, f[:])
 
-        wmx = [weave_w2(0)]
+        w2_mx = [quantise_w2(0)]
 
-        xmx = []
+        x_mx = []
         for a in range(A2):
             if a == 0:
-                xb = shared.tile([NP, P, 4], BF16, name="xb0", align_bytes=64, offset=4 * S + 4 * T)
+                x_bf = second.tile([NP, P, 4], BF16, name="x_bf0", align_bytes=64, offset=W4_PAIR)
             else:
-                xb = keep.tile([NP, P, 4], BF16, name="xb1", tag="xb1", align_bytes=64)
-            nc.scalar.copy(xb[:].rearrange("p (c i) t -> p c t i", i=4), x32[a][:].rearrange("p t (c i) -> p c t i", i=4))
-            xq = keep.tile([NP, P], U32, name=f"xq{a}", align_bytes=64)
-            xs = keep.tile([NP, P], U8, name=f"xs{a}", align_bytes=64)
-            nc.vector.quantize_mx(out=xq[:].bitcast(FP8X4), scales=xs[:], in_=xb[:].rearrange("p m t -> p (m t)"))
-            xmx.append((xq, xs))
+                x_bf = keep.tile([NP, P, 4], BF16, name="x_bf1", tag="x_bf1", align_bytes=64)
+            nc.scalar.copy(x_bf[:].rearrange("p (c i) t -> p c t i", i=4), x32[a][:].rearrange("p t (c i) -> p c t i", i=4))
+            codes = keep.tile([NP, P], U32, name=f"x_codes{a}", align_bytes=64)
+            scales = keep.tile([NP, P], U8, name=f"x_scales{a}", align_bytes=64)
+            nc.vector.quantize_mx(out=codes[:].bitcast(FP8X4), scales=scales[:], in_=x_bf[:].rearrange("p m t -> p (m t)"))
+            x_mx.append((codes, scales))
 
-        f2 = keep.tile([NP, 2, P], F32, name="fine1", tag="xb1", align_bytes=64)
+        f_pair = keep.tile([NP, 2, P], F32, name="fine1", tag="x_bf1", align_bytes=64)
         for t in range(2):
-            nc.vector.tensor_copy(f2[:, t, :], hs[t][:].indirect(pos2_sb[:]))
-            fine[1].append(f2[:, t, :])
+            gather_fine(1, t, f_pair[:, t, :])
 
         out_rows = out.rearrange("(b p t) m -> b t p m", b=A2, t=4)
 
-        def times_y(b, t):
+        def second_product(b, t):
             acc = psum.tile([NP, N], F32, name="bank2", tag="bank2")
             cols = slice(NP * t, NP * (t + 1))
             for a in range(A2):
-                nc.tensor.matmul_mx(out=acc[:], lhsT=wmx[b][a][0][:, cols].bitcast(FP8X4), lhsT_scale=wmx[b][a][1][:, cols],
-                                    rhs=xmx[a][0][:].bitcast(FP8X4), rhs_scale=xmx[a][1][:],
+                nc.tensor.matmul_mx(out=acc[:], lhsT=w2_mx[b][a][0][:, cols].bitcast(FP8X4), lhsT_scale=w2_mx[b][a][1][:, cols],
+                                    rhs=x_mx[a][0][:].bitcast(FP8X4), rhs_scale=x_mx[a][1][:],
                                     start=(a == 0), stop=(a == A2 - 1))
             return acc
 
         def times_fine(acc, b, t, m):
             fy = ring.tile([NP, P], F32, name="fy")
-            nc.vector.tensor_tensor(fy[:, m], acc[:, m], fine[b][t][:, m], MULT)
+            nc.vector.tensor_tensor(fy[:, m], acc[:, m], fine[b, t][:, m], MULT)
             return fy
 
         def finish(b, t, m, fy):
             res = ring.tile([NP, P], F32, name="res")
-            if 4 * b + t < SHARE:
+            if 4 * b + t < GPSIMD_TILES:
                 fyd = ring.tile([NP, P], F32, name="fyd", bufs=3)
-                nc.scalar.activation(fyd[:], fy[:], IDENT, bias=dcol[:, b, t : t + 1])
-                nc.gpsimd.tensor_tensor(res[:], fyd[:], fine[b][t], MULT)
+                nc.scalar.activation(fyd[:], fy[:], IDENT, bias=d_col[:, b, t : t + 1])
+                nc.gpsimd.tensor_tensor(res[:], fyd[:], fine[b, t], MULT)
+                queue = nc.sync
             else:
-                nc.vector.scalar_tensor_tensor(res[:, m], fy[:, m], dcol[:, b, t : t + 1], fine[b][t][:, m], ADD, MULT)
-            queue = nc.sync if 4 * b + t < SHARE else nc.scalar
+                nc.vector.scalar_tensor_tensor(res[:, m], fy[:, m], d_col[:, b, t : t + 1], fine[b, t][:, m], ADD, MULT)
+                queue = nc.scalar
             queue.dma_start(out_rows[b, t][:, m], res[:, m])
 
         held = None
         for b in range(A2):
             for t in range(4):
-                acc = times_y(b, t)
+                acc = second_product(b, t)
                 last = b == A2 - 1 and t == 3
                 for m in ([slice(0, P // 2), slice(P // 2, P)] if last else [slice(0, P)]):
                     fy = times_fine(acc, b, t, m)
@@ -241,5 +263,5 @@ def tile_list_well_log_corrector_kernel(tc, tab_words, tab_scales, offs, pos1, p
                         finish(*held)
                     held = (b, t, m, fy)
                 if (b, t) == (0, 2):
-                    wmx.append(weave_w2(1))
+                    w2_mx.append(quantise_w2(1))
         finish(*held)

@@ -29,10 +29,13 @@ EARLY_FINE = 3
 WEAVE_STEPS = 4
 OUT_PIECES = 9
 
+QUADRANTS = (0, 2, 1, 3)
+
 WORDS = 4 * S
 WINDOW = 4 * T
 W4_RAW = A1 * H
 W4_PAIR = W4_RAW // 2
+PAIRS = WORDS + S // 2
 X32 = 16 * P
 X16 = 8 * P
 
@@ -45,22 +48,22 @@ def tile_list_well_log_corrector_kernel(tc, tab_words, tab_scales, offs, pos1, p
         shared = ctx.enter_context(tc.tile_pool(name="shared", bufs=1))
         late = ctx.enter_context(tc.tile_pool(name="late", bufs=1))
         first = ctx.enter_context(tc.tile_pool(name="first", bufs=1))
-        second = ctx.enter_context(tc.tile_pool(name="second", bufs=1))
+        third = ctx.enter_context(tc.tile_pool(name="third", bufs=1))
         ring = ctx.enter_context(tc.tile_pool(name="ring", bufs=OUT_PIECES))
         psum = ctx.enter_context(tc.psum_pool(name="psum", bufs=2 * EARLY_TILES))
 
         offs_sb = lists.tile([NP, S // 16], U16, name="offs_sb")
         pos1_sb = lists.tile([NP, P // 16], U16, name="pos1_sb")
         pos2_sb = lists.tile([NP, P // 16], U16, name="pos2_sb")
-        tab_rows = keep.tile([NP, T], U8, name="tab_rows", tag="rows", align_bytes=64)
+        tab_rows = keep.tile([NP, T], U8, name="tab_rows", align_bytes=64)
         w4_rows = shared.tile([NP, H], U8, name="w4_rows", align_bytes=64, offset=S)
         gain_col = keep.tile([NP, A2, 4], F32, name="gain_col")
         d_col = keep.tile([NP, A2, 4], F32, name="d_col")
-        w4_raw = [second.tile([NP, A1, H], U8, name="w4_raw0", align_bytes=64, offset=X16 - LINK)]
+        w4_raw = [keep.tile([NP, A1 - 1, H], U8, name="w4_raw0", align_bytes=64)]
         w4_src = w4_words.rearrange("a p (b c) -> b p a c", b=A2)
         window = [first.tile([NP, T], I32, name="window0", align_bytes=64, offset=W4_RAW - LINK),
-                  keep.tile([NP, T], I32, name="window1", tag="window1", align_bytes=64)]
-        for queue, tile, rows in ((nc.sync, tab_rows, tab_scales), (nc.scalar, w4_rows, w4_scales)):
+                  third.tile([NP, T], I32, name="window1", align_bytes=64, offset=WINDOW - LINK)]
+        for queue, tile, rows in ((nc.scalar, w4_rows, w4_scales), (nc.sync, tab_rows, tab_scales)):
             queue.dma_start(tile[16:48, :].bitcast(I32), rows[0:2].rearrange("a s c -> s a c").bitcast(I32))
             queue.dma_start(tile[48:64, :].bitcast(I32), rows[2].bitcast(I32))
         nc.sync.dma_start(offs_sb[:], offs)
@@ -69,8 +72,8 @@ def tile_list_well_log_corrector_kernel(tc, tab_words, tab_scales, offs, pos1, p
         nc.scalar.dma_start(gain_col[:], gain.rearrange("(b p t) -> p b t", b=A2, t=4))
         nc.sync.dma_start(pos2_sb[:], pos2)
         nc.scalar.dma_start(d_col[:], d.rearrange("(b p t) -> p b t", b=A2, t=4))
-        nc.sync.dma_start(w4_raw[0][:].bitcast(I32), w4_src[0].bitcast(I32))
-        for tile in (tab_rows, w4_rows):
+        nc.sync.dma_start(w4_raw[0][:].bitcast(I32), w4_src[0][:, : A1 - 1].bitcast(I32))
+        for tile in (w4_rows, tab_rows):
             nc.vector.memset(tile[0:16, :].bitcast(I32), 0)
             nc.vector.memset(tile[64:128, :].bitcast(I32), 0)
 
@@ -83,25 +86,27 @@ def tile_list_well_log_corrector_kernel(tc, tab_words, tab_scales, offs, pos1, p
         planes = keep.tile([NP, A1, S + H], U8, name="planes", align_bytes=64)
         nc.gpsimd.memset(planes[:].bitcast(I32), 0)
 
-        w4_pair = [keep.tile([NP, 2, A1, 2 * NP], U8, name="w4_pair0", align_bytes=64)]
+        w4_pair = [keep.tile([NP, 2, A1, 2 * NP], U8, name=f"w4_pair{g}", align_bytes=64) for g in range(2)]
 
-        def order_w4(g):
-            nc.vector.tensor_copy(
-                w4_pair[g][:].bitcast(U16),
-                w4_raw[g // 2][:].bitcast(U16).rearrange("p a (m t) -> p t a m", t=4)[:, 2 * (g % 2) : 2 * (g % 2) + 2])
+        def order_w4(copy, g, raw, passes):
+            copy(w4_pair[g][:, :, passes].bitcast(U16),
+                 raw[:].bitcast(U16).rearrange("p a (m t) -> p t a m", t=4)[:, 2 * (g % 2) : 2 * (g % 2) + 2])
+
+        for g in range(2):
+            order_w4(nc.scalar.copy, g, w4_raw[0], slice(0, A1 - 1))
 
         picked_rows = shared.tile([NP, S], U8, name="picked_rows", align_bytes=64, offset=WORDS - S // 2)
-        both_rows = keep.tile([NP, S + H], U8, name="both_rows", tag="rows", align_bytes=64)
-        nc.vector.tensor_copy(picked_rows[:], tab_rows[:].indirect(offs_sb[:]))
+        both_rows = keep.tile([NP, S + H], U8, name="both_rows", align_bytes=64)
         nc.vector.tensor_copy(
             both_rows[:, S:].rearrange("p (b t m) -> p b t m", b=A2, t=4),
             w4_rows[:].rearrange("p (b m t) -> p b t m", b=A2, t=4))
+        nc.vector.tensor_copy(picked_rows[:], tab_rows[:].indirect(offs_sb[:]))
         nc.vector.tensor_copy(both_rows[:, :S].bitcast(I32), picked_rows[:].bitcast(I32))
-        for q in range(4):
+        for q in QUADRANTS:
             nc.sync.dma_start(planes[32 * q : 32 * q + 4, 0:2, :].bitcast(I32), both_rows[16 + 8 * q : 24 + 8 * q, :].bitcast(I32))
         window.append(shared.tile([NP, T], I32, name="window2", align_bytes=64, offset=WORDS + LINK))
         nc.sync.dma_start(window[2][:], tab_words[2].rearrange("p t i -> p (t i)").bitcast(I32))
-        for q in range(4):
+        for q in QUADRANTS:
             nc.sync.dma_start(planes[32 * q : 32 * q + 4, 2, :].bitcast(I32), both_rows[48 + 4 * q : 52 + 4 * q, :].bitcast(I32))
 
         gain1 = keep.tile([NP, 4, P], F32, name="gain1", tag="gain1")
@@ -115,30 +120,32 @@ def tile_list_well_log_corrector_kernel(tc, tab_words, tab_scales, offs, pos1, p
         words.append(keep.tile([NP, S], U32, name="words1", align_bytes=64))
         words_last = [keep.tile([NP, N], U32, name=f"words_last{c}", align_bytes=64) for c in range(2)]
         nc.vector.tensor_copy(words[0][:], window[0][:].bitcast(U32).indirect(offs_sb[:]))
+        w4_last = first.tile([NP, 1, H], U8, name="w4_last", align_bytes=64, offset=W4_RAW + WINDOW - 2 * LINK)
+        nc.sync.dma_start(w4_last[:].bitcast(I32), w4_src[0][:, A1 - 1 :].bitcast(I32))
+        for g in range(2):
+            order_w4(nc.scalar.copy, g, w4_last, slice(A1 - 1, A1))
         w4_raw.append(first.tile([NP, A1, H], U8, name="w4_raw1", align_bytes=64, offset=0))
         nc.sync.dma_start(w4_raw[1][:].bitcast(I32), w4_src[1].bitcast(I32))
-        order_w4(0)
         nc.vector.tensor_copy(words[1][:], window[1][:].bitcast(U32).indirect(offs_sb[:]))
         for c in range(2):
             nc.vector.tensor_copy(words_last[c][:],
                                   window[2][:].bitcast(U32).indirect(offs_sb[:, N // 16 * c : N // 16 * (c + 1)]))
 
-        w4_pair.append(shared.tile([NP, 2, A1, 2 * NP], U8, name="w4_pair1", align_bytes=64, offset=WORDS + WINDOW))
-        w4_pair.append(second.tile([NP, 2, A1, 2 * NP], U8, name="w4_pair2", align_bytes=64, offset=X16 - W4_PAIR))
-        w4_pair.append(second.tile([NP, 2, A1, 2 * NP], U8, name="w4_pair3", align_bytes=64, offset=X16))
-        for g in range(1, 4):
-            order_w4(g)
+        w4_pair.append(shared.tile([NP, 2, A1, 2 * NP], U8, name="w4_pair2", align_bytes=64, offset=PAIRS))
+        w4_pair.append(shared.tile([NP, 2, A1, 2 * NP], U8, name="w4_pair3", align_bytes=64, offset=PAIRS + W4_PAIR))
+        for g in (2, 3):
+            order_w4(nc.vector.tensor_copy, g, w4_raw[1], slice(0, A1))
 
         w2_src = w2.rearrange("(a p j) (b n) -> a b p j n", a=A2, j=4, b=A2)
         w2_raw = {}
         for b in range(A2):
             for a in range(A2):
                 if (a, b) == (0, 0):
-                    raw = first.tile([NP, 4, N], F32, name="w2_raw00", align_bytes=64, offset=W4_RAW + WINDOW - 2 * LINK)
+                    raw = third.tile([NP, 4, N], F32, name="w2_raw00", align_bytes=64, offset=0)
                 elif (a, b) == (1, 0):
-                    raw = keep.tile([NP, 4, N], F32, name="w2_raw10", tag="window1", align_bytes=64)
+                    raw = third.tile([NP, 4, N], F32, name="w2_raw10", align_bytes=64, offset=2 * WINDOW - 2 * LINK)
                 elif (a, b) == (0, 1):
-                    raw = shared.tile([NP, 4, N], F32, name="w2_raw01", align_bytes=64, offset=WORDS)
+                    raw = shared.tile([NP, 4, N], F32, name="w2_raw01", align_bytes=64, offset=WORDS + WINDOW)
                 else:
                     raw = first.tile([NP, 4, N], F32, name="w2_raw11", align_bytes=64, offset=0)
                 nc.sync.dma_start(raw[:], w2_src[a, b])
@@ -211,7 +218,7 @@ def tile_list_well_log_corrector_kernel(tc, tab_words, tab_scales, offs, pos1, p
         x_mx = []
         for a in range(A2):
             if a == 0:
-                x_bf = second.tile([NP, P, 4], BF16, name="x_bf0", align_bytes=64, offset=W4_PAIR)
+                x_bf = shared.tile([NP, P, 4], BF16, name="x_bf0", align_bytes=64, offset=PAIRS)
             else:
                 x_bf = keep.tile([NP, P, 4], BF16, name="x_bf1", tag="x_bf1", align_bytes=64)
             nc.scalar.copy(x_bf[:].rearrange("p (c i) t -> p c t i", i=4), x32[a][:].rearrange("p t (c i) -> p c t i", i=4))

@@ -63,7 +63,7 @@ def tile_list_well_log_corrector_kernel(tc, tab_words, tab_scales, offs, pos1, p
         w4_src = w4_words.rearrange("a p (b c) -> b p a c", b=A2)
         window = [first.tile([NP, T], I32, name="window0", align_bytes=64, offset=W4_RAW - LINK),
                   third.tile([NP, T], I32, name="window1", align_bytes=64, offset=WINDOW - LINK)]
-        for queue, tile, rows in ((nc.scalar, w4_rows, w4_scales), (nc.sync, tab_rows, tab_scales)):
+        for queue, tile, rows in ((nc.sync, tab_rows, tab_scales), (nc.scalar, w4_rows, w4_scales)):
             queue.dma_start(tile[16:48, :].bitcast(I32), rows[0:2].rearrange("a s c -> s a c").bitcast(I32))
             queue.dma_start(tile[48:64, :].bitcast(I32), rows[2].bitcast(I32))
         nc.sync.dma_start(offs_sb[:], offs)
@@ -97,7 +97,7 @@ def tile_list_well_log_corrector_kernel(tc, tab_words, tab_scales, offs, pos1, p
 
         picked_rows = shared.tile([NP, S], U8, name="picked_rows", align_bytes=64, offset=WORDS - S // 2)
         both_rows = keep.tile([NP, S + H], U8, name="both_rows", align_bytes=64)
-        nc.vector.tensor_copy(
+        nc.gpsimd.tensor_copy(
             both_rows[:, S:].rearrange("p (b t m) -> p b t m", b=A2, t=4),
             w4_rows[:].rearrange("p (b m t) -> p b t m", b=A2, t=4))
         nc.vector.tensor_copy(picked_rows[:], tab_rows[:].indirect(offs_sb[:]))

@@ -23,11 +23,10 @@ A1 = K // 512
 A2 = H // 512
 N = 512
 LINK = 64
-GPSIMD_TILES = 5
 EARLY_TILES = 2
 EARLY_FINE = 3
 WEAVE_STEPS = 4
-OUT_PIECES = 9
+OUT_PIECES = 7
 
 QUADRANTS = (0, 2, 1, 3)
 
@@ -165,25 +164,24 @@ def tile_list_well_log_corrector_kernel(tc, tab_words, tab_scales, offs, pos1, p
             nc.vector.tensor_copy(dst, hs[b, t][:].indirect(pos2_sb[:]))
             fine[b, t] = dst
 
-        def quantise_w2(b):
-            made = []
-            for a in range(A2):
-                if b == 0:
-                    w2_bf = keep.tile([NP, 4, NP, 4], BF16, name=f"w2_bf{a}{b}", tag=f"w2_bf{a}{b}", align_bytes=64)
-                else:
-                    w2_bf = late.tile([NP, 4, NP, 4], BF16, name=f"w2_bf{a}{b}", align_bytes=64, offset=X32 + X16 * a)
-                for step in range(WEAVE_STEPS):
-                    part = slice(NP // WEAVE_STEPS * step, NP // WEAVE_STEPS * (step + 1))
-                    nc.scalar.copy(w2_bf[:].rearrange("p t m j -> p m j t")[:, part],
-                                   w2_raw[a, b][:].rearrange("p j (m t) -> p m j t", t=4)[:, part])
-                codes = keep.tile([NP, N], U32, name=f"w2_codes{a}{b}", align_bytes=64)
-                scales = keep.tile([NP, N], U8, name=f"w2_scales{a}{b}", align_bytes=64)
-                nc.vector.quantize_mx(out=codes[:].bitcast(FP8X4), scales=scales[:], in_=w2_bf[:].rearrange("p t m j -> p (t m j)"))
-                made.append((codes, scales))
-                if b == 1:
-                    f = late.tile([NP, P], F32, name=f"fine1{2 + a}", align_bytes=64, offset=X32 + X16 * a)
-                    gather_fine(1, 2 + a, f[:])
-            return made
+        w2_bf, w2_mx = {}, {}
+
+        def weave_w2(a, b):
+            if b == 0:
+                tile = keep.tile([NP, 4, NP, 4], BF16, name=f"w2_bf{a}{b}", tag=f"w2_bf{a}{b}", align_bytes=64)
+            else:
+                tile = late.tile([NP, 4, NP, 4], BF16, name=f"w2_bf{a}{b}", align_bytes=64, offset=X32 + X16 * a)
+            for step in range(WEAVE_STEPS):
+                part = slice(NP // WEAVE_STEPS * step, NP // WEAVE_STEPS * (step + 1))
+                nc.scalar.copy(tile[:].rearrange("p t m j -> p m j t")[:, part],
+                               w2_raw[a, b][:].rearrange("p j (m t) -> p m j t", t=4)[:, part])
+            w2_bf[a, b] = tile
+
+        def quantise_w2(a, b):
+            codes = keep.tile([NP, N], U32, name=f"w2_codes{a}{b}", align_bytes=64)
+            scales = keep.tile([NP, N], U8, name=f"w2_scales{a}{b}", align_bytes=64)
+            nc.vector.quantize_mx(out=codes[:].bitcast(FP8X4), scales=scales[:], in_=w2_bf[a, b][:].rearrange("p t m j -> p (t m j)"))
+            w2_mx[a, b] = (codes, scales)
 
         early = {(0, t, c): psum.tile([NP, N], F32, name="bank1", tag="bank1") for t in range(EARLY_TILES) for c in range(2)}
         for a in range(A1 - 1):
@@ -210,10 +208,10 @@ def tile_list_well_log_corrector_kernel(tc, tab_words, tab_scales, offs, pos1, p
                     f = keep.tile([NP, P], F32, name=f"fine0{t}", tag=f"fine0{t}", align_bytes=64)
                     gather_fine(b, t, f[:])
             x32.append(x_half)
-        f = keep.tile([NP, P], F32, name="fine03", tag="gain1")
-        gather_fine(0, 3, f[:])
 
-        w2_mx = [quantise_w2(0)]
+        for a in range(A2):
+            weave_w2(a, 0)
+            quantise_w2(a, 0)
 
         x_mx = []
         for a in range(A2):
@@ -226,49 +224,82 @@ def tile_list_well_log_corrector_kernel(tc, tab_words, tab_scales, offs, pos1, p
             scales = keep.tile([NP, P], U8, name=f"x_scales{a}", align_bytes=64)
             nc.vector.quantize_mx(out=codes[:].bitcast(FP8X4), scales=scales[:], in_=x_bf[:].rearrange("p m t -> p (m t)"))
             x_mx.append((codes, scales))
+            if a == 0:
+                f03 = shared.tile([NP, P], F32, name="fine03", align_bytes=64, offset=PAIRS)
+                gather_fine(0, 3, f03[:])
 
-        f_pair = keep.tile([NP, 2, P], F32, name="fine1", tag="x_bf1", align_bytes=64)
-        for t in range(2):
-            gather_fine(1, t, f_pair[:, t, :])
+        for a in range(A2):
+            weave_w2(a, 1)
 
         out_rows = out.rearrange("(b p t) m -> b t p m", b=A2, t=4)
+        banks, fys = {}, {}
 
-        def second_product(b, t):
-            acc = psum.tile([NP, N], F32, name="bank2", tag="bank2")
-            cols = slice(NP * t, NP * (t + 1))
-            for a in range(A2):
-                nc.tensor.matmul_mx(out=acc[:], lhsT=w2_mx[b][a][0][:, cols].bitcast(FP8X4), lhsT_scale=w2_mx[b][a][1][:, cols],
+        def second_pass(a, b, tiles=range(4)):
+            for t in tiles:
+                if a == 0:
+                    banks[b, t] = psum.tile([NP, N], F32, name="bank2", tag=("bank2", "bank1")[b])
+                cols = slice(NP * t, NP * (t + 1))
+                nc.tensor.matmul_mx(out=banks[b, t][:], lhsT=w2_mx[a, b][0][:, cols].bitcast(FP8X4), lhsT_scale=w2_mx[a, b][1][:, cols],
                                     rhs=x_mx[a][0][:].bitcast(FP8X4), rhs_scale=x_mx[a][1][:],
                                     start=(a == 0), stop=(a == A2 - 1))
-            return acc
 
-        def times_fine(acc, b, t, m):
-            fy = ring.tile([NP, P], F32, name="fy")
-            nc.vector.tensor_tensor(fy[:, m], acc[:, m], fine[b, t][:, m], MULT)
-            return fy
-
-        def finish(b, t, m, fy):
-            res = ring.tile([NP, P], F32, name="res")
-            if 4 * b + t < GPSIMD_TILES:
-                fyd = ring.tile([NP, P], F32, name="fyd", bufs=3)
-                nc.scalar.activation(fyd[:], fy[:], IDENT, bias=d_col[:, b, t : t + 1])
-                nc.gpsimd.tensor_tensor(res[:], fyd[:], fine[b, t], MULT)
-                queue = nc.sync
+        def times_fine(b, t, m=slice(0, P)):
+            if (b, t) == (0, 3):
+                fy = late.tile([NP, P], F32, name=f"fy{b}{t}", align_bytes=64, offset=X32 + X16 + LINK)
             else:
-                nc.vector.scalar_tensor_tensor(res[:, m], fy[:, m], d_col[:, b, t : t + 1], fine[b, t][:, m], ADD, MULT)
-                queue = nc.scalar
+                fy = keep.tile([NP, P], F32, name=f"fy{b}{t}_{m.start}", tag=f"fy{b}{t}_{m.start}")
+            nc.vector.tensor_tensor(fy[:, m], banks[b, t][:, m], fine[b, t][:, m], MULT)
+            fys[b, t, m.start] = fy
+
+        def finish_on_vector(b, t, res, queue, m=slice(0, P)):
+            nc.vector.scalar_tensor_tensor(res[:, m], fys[b, t, m.start][:, m], d_col[:, b, t : t + 1], fine[b, t][:, m], ADD, MULT)
             queue.dma_start(out_rows[b, t][:, m], res[:, m])
 
-        held = None
-        for b in range(A2):
-            for t in range(4):
-                acc = second_product(b, t)
-                last = b == A2 - 1 and t == 3
-                for m in ([slice(0, P // 2), slice(P // 2, P)] if last else [slice(0, P)]):
-                    fy = times_fine(acc, b, t, m)
-                    if held is not None:
-                        finish(*held)
-                    held = (b, t, m, fy)
-                if (b, t) == (0, 2):
-                    w2_mx.append(quantise_w2(1))
-        finish(*held)
+        def finish_on_gpsimd(b, t, res):
+            if b == 0:
+                fyd = first.tile([NP, P], F32, name=f"fyd{b}{t}", align_bytes=64, offset=4 * P * t)
+            else:
+                fyd = keep.tile([NP, P], F32, name=f"fyd{b}{t}", tag=f"fyd{b}{t}")
+            nc.scalar.activation(fyd[:], fys[b, t, 0][:], IDENT, bias=d_col[:, b, t : t + 1])
+            nc.gpsimd.tensor_tensor(res[:], fyd[:], fine[b, t], MULT)
+            nc.sync.dma_start(out_rows[b, t], res[:])
+
+        def result(name):
+            return ring.tile([NP, P], F32, name=name, tag="res")
+
+        for t in range(4):
+            for a in range(A2):
+                second_pass(a, 0, [t])
+        f10 = keep.tile([NP, P], F32, name="fine10", tag="x_bf1", align_bytes=64)
+        gather_fine(1, 0, f10[:])
+        times_fine(0, 0)
+        times_fine(0, 1)
+        quantise_w2(0, 1)
+        second_pass(0, 1)
+        finish_on_vector(0, 0, result("res00"), nc.sync)
+        times_fine(0, 2)
+        quantise_w2(1, 1)
+        second_pass(1, 1)
+        res01 = late.tile([NP, P], F32, name="res01", align_bytes=64, offset=X32 + X16 + LINK - 4 * P)
+        finish_on_gpsimd(0, 1, res01)
+        finish_on_gpsimd(0, 2, result("res02"))
+        times_fine(0, 3)
+        finish_on_gpsimd(0, 3, result("res03"))
+        f11 = keep.tile([NP, P], F32, name="fine11", tag="fy01_0")
+        gather_fine(1, 1, f11[:])
+        times_fine(1, 0)
+        finish_on_gpsimd(1, 0, result("res10"))
+        times_fine(1, 1)
+        finish_on_gpsimd(1, 1, result("res11"))
+        f12 = late.tile([NP, P], F32, name="fine12", align_bytes=64, offset=X32 + X16 + LINK)
+        gather_fine(1, 2, f12[:])
+        times_fine(1, 2)
+        f13 = keep.tile([NP, P], F32, name="fine13", tag="fy10_0")
+        gather_fine(1, 3, f13[:])
+        halves = [slice(0, P // 2), slice(P // 2, P)]
+        times_fine(1, 3, halves[0])
+        times_fine(1, 3, halves[1])
+        res12 = keep.tile([NP, P], F32, name="res12", tag="fyd11")
+        finish_on_vector(1, 2, res12, nc.scalar)
+        for m in halves:
+            finish_on_vector(1, 3, result(f"res13_{m.start}"), nc.scalar, m)

@@ -26,6 +26,7 @@ LINK = 64
 EARLY_TILES = 2
 EARLY_FINE = 3
 WEAVE_STEPS = 4
+GPSIMD_STEPS = 2
 OUT_PIECES = 7
 
 QUADRANTS = (0, 2, 1, 3)
@@ -37,6 +38,7 @@ W4_PAIR = W4_RAW // 2
 PAIRS = WORDS + S // 2
 X32 = 16 * P
 X16 = 8 * P
+LAST_BF = X32 + X16 + LINK
 
 
 def tile_list_well_log_corrector_kernel(tc, tab_words, tab_scales, offs, pos1, pos2, w4_words, w4_scales, gain, w2, d, out):
@@ -170,8 +172,14 @@ def tile_list_well_log_corrector_kernel(tc, tab_words, tab_scales, offs, pos1, p
             if b == 0:
                 tile = keep.tile([NP, 4, NP, 4], BF16, name=f"w2_bf{a}{b}", tag=f"w2_bf{a}{b}", align_bytes=64)
             else:
-                tile = late.tile([NP, 4, NP, 4], BF16, name=f"w2_bf{a}{b}", align_bytes=64, offset=X32 + X16 * a)
-            for step in range(WEAVE_STEPS):
+                tile = late.tile([NP, 4, NP, 4], BF16, name=f"w2_bf{a}{b}", align_bytes=64, offset=(X32, LAST_BF)[a])
+            steps = WEAVE_STEPS
+            if (a, b) == (1, 1):
+                steps = WEAVE_STEPS - GPSIMD_STEPS
+                part = slice(NP // WEAVE_STEPS * steps, NP)
+                nc.gpsimd.tensor_scalar(tile[:].rearrange("p t m j -> p m t j")[:, part],
+                                        w2_raw[a, b][:].rearrange("p j (m t) -> p m t j", t=4)[:, part], 1.0, 0.0, MULT, ADD)
+            for step in range(steps):
                 part = slice(NP // WEAVE_STEPS * step, NP // WEAVE_STEPS * (step + 1))
                 nc.scalar.copy(tile[:].rearrange("p t m j -> p m j t")[:, part],
                                w2_raw[a, b][:].rearrange("p j (m t) -> p m j t", t=4)[:, part])
@@ -218,7 +226,7 @@ def tile_list_well_log_corrector_kernel(tc, tab_words, tab_scales, offs, pos1, p
             if a == 0:
                 x_bf = shared.tile([NP, P, 4], BF16, name="x_bf0", align_bytes=64, offset=PAIRS)
             else:
-                x_bf = keep.tile([NP, P, 4], BF16, name="x_bf1", tag="x_bf1", align_bytes=64)
+                x_bf = late.tile([NP, P, 4], BF16, name="x_bf1", align_bytes=64, offset=2 * X32)
             nc.scalar.copy(x_bf[:].rearrange("p (c i) t -> p c t i", i=4), x32[a][:].rearrange("p t (c i) -> p c t i", i=4))
             codes = keep.tile([NP, P], U32, name=f"x_codes{a}", align_bytes=64)
             scales = keep.tile([NP, P], U8, name=f"x_scales{a}", align_bytes=64)
@@ -244,8 +252,8 @@ def tile_list_well_log_corrector_kernel(tc, tab_words, tab_scales, offs, pos1, p
                                     start=(a == 0), stop=(a == A2 - 1))
 
         def times_fine(b, t, m=slice(0, P)):
-            if (b, t) == (0, 3):
-                fy = late.tile([NP, P], F32, name=f"fy{b}{t}", align_bytes=64, offset=X32 + X16 + LINK)
+            if b == 0 and t >= 2:
+                fy = late.tile([NP, P], F32, name=f"fy{b}{t}", align_bytes=64, offset=LAST_BF + (LINK - 4 * P) * (3 - t) + LINK * (t - 2))
             else:
                 fy = keep.tile([NP, P], F32, name=f"fy{b}{t}_{m.start}", tag=f"fy{b}{t}_{m.start}")
             nc.vector.tensor_tensor(fy[:, m], banks[b, t][:, m], fine[b, t][:, m], MULT)
@@ -270,18 +278,18 @@ def tile_list_well_log_corrector_kernel(tc, tab_words, tab_scales, offs, pos1, p
         for t in range(4):
             for a in range(A2):
                 second_pass(a, 0, [t])
-        f10 = keep.tile([NP, P], F32, name="fine10", tag="x_bf1", align_bytes=64)
+        f10 = late.tile([NP, P], F32, name="fine10", align_bytes=64, offset=2 * X32 + 2 * LINK)
         gather_fine(1, 0, f10[:])
         times_fine(0, 0)
         times_fine(0, 1)
         quantise_w2(0, 1)
         second_pass(0, 1)
         finish_on_vector(0, 0, result("res00"), nc.sync)
-        times_fine(0, 2)
         quantise_w2(1, 1)
         second_pass(1, 1)
-        res01 = late.tile([NP, P], F32, name="res01", align_bytes=64, offset=X32 + X16 + LINK - 4 * P)
+        res01 = late.tile([NP, P], F32, name="res01", align_bytes=64, offset=LAST_BF + LINK + 4 * P)
         finish_on_gpsimd(0, 1, res01)
+        times_fine(0, 2)
         finish_on_gpsimd(0, 2, result("res02"))
         times_fine(0, 3)
         finish_on_gpsimd(0, 3, result("res03"))
@@ -291,7 +299,7 @@ def tile_list_well_log_corrector_kernel(tc, tab_words, tab_scales, offs, pos1, p
         finish_on_gpsimd(1, 0, result("res10"))
         times_fine(1, 1)
         finish_on_gpsimd(1, 1, result("res11"))
-        f12 = late.tile([NP, P], F32, name="fine12", align_bytes=64, offset=X32 + X16 + LINK)
+        f12 = late.tile([NP, P], F32, name="fine12", align_bytes=64, offset=LAST_BF + LINK)
         gather_fine(1, 2, f12[:])
         times_fine(1, 2)
         f13 = keep.tile([NP, P], F32, name="fine13", tag="fy10_0")

@@ -24,9 +24,9 @@ A2 = H // 512
 N = 512
 LINK = 64
 EARLY_TILES = 2
-EARLY_FINE = 3
-WEAVE_STEPS = 4
-GPSIMD_STEPS = 2
+EARLY_FINE = 2
+WEAVE_STEP = 32
+GPSIMD_COLS = 80
 OUT_PIECES = 7
 
 QUADRANTS = (0, 2, 1, 3)
@@ -38,6 +38,10 @@ W4_PAIR = W4_RAW // 2
 PAIRS = WORDS + S // 2
 X32 = 16 * P
 X16 = 8 * P
+FINE00 = W4_PAIR - LINK + X16
+X_BF0 = PAIRS + 2 * W4_PAIR - LINK
+X_STEPS = 4
+GAIN1 = FINE00 + 8 * P - 2 * LINK + X16
 LAST_BF = X32 + X16 + LINK
 
 
@@ -50,6 +54,7 @@ def tile_list_well_log_corrector_kernel(tc, tab_words, tab_scales, offs, pos1, p
         late = ctx.enter_context(tc.tile_pool(name="late", bufs=1))
         first = ctx.enter_context(tc.tile_pool(name="first", bufs=1))
         third = ctx.enter_context(tc.tile_pool(name="third", bufs=1))
+        mid = ctx.enter_context(tc.tile_pool(name="mid", bufs=1))
         ring = ctx.enter_context(tc.tile_pool(name="ring", bufs=OUT_PIECES))
         psum = ctx.enter_context(tc.psum_pool(name="psum", bufs=2 * EARLY_TILES))
 
@@ -87,7 +92,8 @@ def tile_list_well_log_corrector_kernel(tc, tab_words, tab_scales, offs, pos1, p
         planes = keep.tile([NP, A1, S + H], U8, name="planes", align_bytes=64)
         nc.gpsimd.memset(planes[:].bitcast(I32), 0)
 
-        w4_pair = [keep.tile([NP, 2, A1, 2 * NP], U8, name=f"w4_pair{g}", align_bytes=64) for g in range(2)]
+        w4_pair = [mid.tile([NP, 2, A1, 2 * NP], U8, name="w4_pair0", align_bytes=64, offset=0),
+                   keep.tile([NP, 2, A1, 2 * NP], U8, name="w4_pair1", align_bytes=64)]
 
         def order_w4(copy, g, raw, passes):
             copy(w4_pair[g][:, :, passes].bitcast(U16),
@@ -110,9 +116,12 @@ def tile_list_well_log_corrector_kernel(tc, tab_words, tab_scales, offs, pos1, p
         for q in QUADRANTS:
             nc.sync.dma_start(planes[32 * q : 32 * q + 4, 2, :].bitcast(I32), both_rows[48 + 4 * q : 52 + 4 * q, :].bitcast(I32))
 
-        gain1 = keep.tile([NP, 4, P], F32, name="gain1", tag="gain1")
-        gain_full = [[keep.tile([NP, P], F32, name=f"gain0{t}", tag=("w2_bf00", "w2_bf10", "gain02", "gain03")[t], align_bytes=64)[:] for t in range(4)],
-                     [gain1[:, t, :] for t in range(4)]]
+        gain1 = mid.tile([NP, 4, P], F32, name="gain1", align_bytes=64, offset=GAIN1)
+        gain0 = [keep.tile([NP, P], F32, name="gain00"),
+                 mid.tile([NP, P], F32, name="gain01", align_bytes=64, offset=FINE00 + 4 * P - LINK),
+                 keep.tile([NP, P], F32, name="gain02"),
+                 keep.tile([NP, P], F32, name="gain03")]
+        gain_full = [[tile[:] for tile in gain0], [gain1[:, t, :] for t in range(4)]]
         for b in range(A2):
             for t in range(4):
                 nc.scalar.copy(gain_full[b][t], gain_col[:, b, t : t + 1].to_broadcast([NP, P]))
@@ -132,8 +141,8 @@ def tile_list_well_log_corrector_kernel(tc, tab_words, tab_scales, offs, pos1, p
             nc.vector.tensor_copy(words_last[c][:],
                                   window[2][:].bitcast(U32).indirect(offs_sb[:, N // 16 * c : N // 16 * (c + 1)]))
 
-        w4_pair.append(shared.tile([NP, 2, A1, 2 * NP], U8, name="w4_pair2", align_bytes=64, offset=PAIRS))
-        w4_pair.append(shared.tile([NP, 2, A1, 2 * NP], U8, name="w4_pair3", align_bytes=64, offset=PAIRS + W4_PAIR))
+        w4_pair.append(shared.tile([NP, 2, A1, 2 * NP], U8, name="w4_pair2", align_bytes=64, offset=PAIRS + W4_PAIR))
+        w4_pair.append(shared.tile([NP, 2, A1, 2 * NP], U8, name="w4_pair3", align_bytes=64, offset=PAIRS))
         for g in (2, 3):
             order_w4(nc.vector.tensor_copy, g, w4_raw[1], slice(0, A1))
 
@@ -169,24 +178,28 @@ def tile_list_well_log_corrector_kernel(tc, tab_words, tab_scales, offs, pos1, p
         w2_bf, w2_mx = {}, {}
 
         def weave_w2(a, b):
-            if b == 0:
-                tile = keep.tile([NP, 4, NP, 4], BF16, name=f"w2_bf{a}{b}", tag=f"w2_bf{a}{b}", align_bytes=64)
+            if (a, b) == (0, 0):
+                tile = mid.tile([NP, 4, NP, 4], BF16, name="w2_bf00", align_bytes=64, offset=W4_PAIR - LINK)
+            elif b == 0:
+                tile = mid.tile([NP, 4, NP, 4], BF16, name="w2_bf10", align_bytes=64, offset=FINE00 + 8 * P - 2 * LINK)
             else:
                 tile = late.tile([NP, 4, NP, 4], BF16, name=f"w2_bf{a}{b}", align_bytes=64, offset=(X32, LAST_BF)[a])
-            steps = WEAVE_STEPS
-            if (a, b) == (1, 1):
-                steps = WEAVE_STEPS - GPSIMD_STEPS
-                part = slice(NP // WEAVE_STEPS * steps, NP)
-                nc.gpsimd.tensor_scalar(tile[:].rearrange("p t m j -> p m t j")[:, part],
-                                        w2_raw[a, b][:].rearrange("p j (m t) -> p m t j", t=4)[:, part], 1.0, 0.0, MULT, ADD)
-            for step in range(steps):
-                part = slice(NP // WEAVE_STEPS * step, NP // WEAVE_STEPS * (step + 1))
+            split = NP
+            if a == 1:
+                split = NP - GPSIMD_COLS
+                nc.gpsimd.tensor_scalar(tile[:].rearrange("p t m j -> p m t j")[:, split:],
+                                        w2_raw[a, b][:].rearrange("p j (m t) -> p m t j", t=4)[:, split:], 1.0, 0.0, MULT, ADD)
+            for start in range(0, split, WEAVE_STEP):
+                part = slice(start, min(start + WEAVE_STEP, split))
                 nc.scalar.copy(tile[:].rearrange("p t m j -> p m j t")[:, part],
                                w2_raw[a, b][:].rearrange("p j (m t) -> p m j t", t=4)[:, part])
             w2_bf[a, b] = tile
 
         def quantise_w2(a, b):
-            codes = keep.tile([NP, N], U32, name=f"w2_codes{a}{b}", align_bytes=64)
+            if (a, b) == (1, 0):
+                codes = mid.tile([NP, N], U32, name="w2_codes10", align_bytes=64, offset=GAIN1)
+            else:
+                codes = keep.tile([NP, N], U32, name=f"w2_codes{a}{b}", align_bytes=64)
             scales = keep.tile([NP, N], U8, name=f"w2_scales{a}{b}", align_bytes=64)
             nc.vector.quantize_mx(out=codes[:].bitcast(FP8X4), scales=scales[:], in_=w2_bf[a, b][:].rearrange("p t m j -> p (t m j)"))
             w2_mx[a, b] = (codes, scales)
@@ -212,9 +225,11 @@ def tile_list_well_log_corrector_kernel(tc, tab_words, tab_scales, offs, pos1, p
                             first_pass(acc, b, t, a, c)
                     nc.scalar.activation(h[:, N * c : N * (c + 1)], acc[:], TANH)
                 nc.vector.tensor_tensor(x_half[:, t, :], h[:].indirect(pos1_sb[:]), gain_full[b][t], MULT)
-                if 4 * b + t < EARLY_FINE:
-                    f = keep.tile([NP, P], F32, name=f"fine0{t}", tag=f"fine0{t}", align_bytes=64)
-                    gather_fine(b, t, f[:])
+                if 4 * b + t == EARLY_FINE - 1:
+                    f00 = mid.tile([NP, P], F32, name="fine00", align_bytes=64, offset=FINE00)
+                    f01 = keep.tile([NP, P], F32, name="fine01")
+                    gather_fine(0, 0, f00[:])
+                    gather_fine(0, 1, f01[:])
             x32.append(x_half)
 
         for a in range(A2):
@@ -224,17 +239,23 @@ def tile_list_well_log_corrector_kernel(tc, tab_words, tab_scales, offs, pos1, p
         x_mx = []
         for a in range(A2):
             if a == 0:
-                x_bf = shared.tile([NP, P, 4], BF16, name="x_bf0", align_bytes=64, offset=PAIRS)
+                x_bf = shared.tile([NP, P, 4], BF16, name="x_bf0", align_bytes=64, offset=X_BF0)
             else:
                 x_bf = late.tile([NP, P, 4], BF16, name="x_bf1", align_bytes=64, offset=2 * X32)
-            nc.scalar.copy(x_bf[:].rearrange("p (c i) t -> p c t i", i=4), x32[a][:].rearrange("p t (c i) -> p c t i", i=4))
-            codes = keep.tile([NP, P], U32, name=f"x_codes{a}", align_bytes=64)
+            steps = X_STEPS if a == 0 else 1
+            for step in range(steps):
+                part = slice(P // 4 // steps * step, P // 4 // steps * (step + 1))
+                nc.scalar.copy(x_bf[:].rearrange("p (c i) t -> p c t i", i=4)[:, part], x32[a][:].rearrange("p t (c i) -> p c t i", i=4)[:, part])
+            if a == 0:
+                codes = mid.tile([NP, P], U32, name="x_codes0", align_bytes=64, offset=GAIN1 + 4 * N)
+            else:
+                codes = keep.tile([NP, P], U32, name="x_codes1", align_bytes=64)
             scales = keep.tile([NP, P], U8, name=f"x_scales{a}", align_bytes=64)
             nc.vector.quantize_mx(out=codes[:].bitcast(FP8X4), scales=scales[:], in_=x_bf[:].rearrange("p m t -> p (m t)"))
             x_mx.append((codes, scales))
             if a == 0:
-                f03 = shared.tile([NP, P], F32, name="fine03", align_bytes=64, offset=PAIRS)
-                gather_fine(0, 3, f03[:])
+                f02 = shared.tile([NP, P], F32, name="fine02", align_bytes=64, offset=X_BF0 + LINK)
+                gather_fine(0, 2, f02[:])
 
         for a in range(A2):
             weave_w2(a, 1)
@@ -278,31 +299,29 @@ def tile_list_well_log_corrector_kernel(tc, tab_words, tab_scales, offs, pos1, p
         for t in range(4):
             for a in range(A2):
                 second_pass(a, 0, [t])
-        f10 = late.tile([NP, P], F32, name="fine10", align_bytes=64, offset=2 * X32 + 2 * LINK)
-        gather_fine(1, 0, f10[:])
+        f03 = late.tile([NP, P], F32, name="fine03", align_bytes=64, offset=2 * X32 + 2 * LINK)
+        gather_fine(0, 3, f03[:])
         times_fine(0, 0)
         times_fine(0, 1)
-        quantise_w2(0, 1)
-        second_pass(0, 1)
-        finish_on_vector(0, 0, result("res00"), nc.sync)
-        quantise_w2(1, 1)
-        second_pass(1, 1)
-        res01 = late.tile([NP, P], F32, name="res01", align_bytes=64, offset=LAST_BF + LINK + 4 * P)
-        finish_on_gpsimd(0, 1, res01)
-        times_fine(0, 2)
-        finish_on_gpsimd(0, 2, result("res02"))
-        times_fine(0, 3)
-        finish_on_gpsimd(0, 3, result("res03"))
-        f11 = keep.tile([NP, P], F32, name="fine11", tag="fy01_0")
-        gather_fine(1, 1, f11[:])
-        times_fine(1, 0)
-        finish_on_gpsimd(1, 0, result("res10"))
-        times_fine(1, 1)
-        finish_on_gpsimd(1, 1, result("res11"))
-        f12 = late.tile([NP, P], F32, name="fine12", align_bytes=64, offset=LAST_BF + LINK)
+        for a in range(A2):
+            quantise_w2(a, 1)
+            second_pass(a, 1)
+        res00 = late.tile([NP, P], F32, name="res00", align_bytes=64, offset=LAST_BF + LINK + 4 * P)
+        finish_on_gpsimd(0, 0, res00)
+        finish_on_gpsimd(0, 1, result("res01"))
+        for t in (2, 3):
+            times_fine(0, t)
+            finish_on_gpsimd(0, t, result(f"res0{t}"))
+        for t, product in enumerate(("fy00_0", "fy01_0")):
+            f = keep.tile([NP, P], F32, name=f"fine1{t}", tag=product)
+            gather_fine(1, t, f[:])
+        for t in range(2):
+            times_fine(1, t)
+            finish_on_gpsimd(1, t, result(f"res1{t}"))
+        f12 = keep.tile([NP, P], F32, name="fine12", tag="fy10_0")
         gather_fine(1, 2, f12[:])
         times_fine(1, 2)
-        f13 = keep.tile([NP, P], F32, name="fine13", tag="fy10_0")
+        f13 = keep.tile([NP, P], F32, name="fine13", tag="fy11_0")
         gather_fine(1, 3, f13[:])
         halves = [slice(0, P // 2), slice(P // 2, P)]
         times_fine(1, 3, halves[0])

@@ -29,6 +29,7 @@ WEAVE_STEP = 32
 GPSIMD_COLS = 80
 OUT_PIECES = 7
 
+PIECES = ((0, N), (N, N + N // 2), (N + N // 2, S))
 QUADRANTS = (0, 2, 1, 3)
 
 WORDS = 4 * S
@@ -63,8 +64,7 @@ def tile_list_well_log_corrector_kernel(tc, tab_words, tab_scales, offs, pos1, p
         pos2_sb = lists.tile([NP, P // 16], U16, name="pos2_sb")
         tab_rows = keep.tile([NP, T], U8, name="tab_rows", align_bytes=64)
         w4_rows = shared.tile([NP, H], U8, name="w4_rows", align_bytes=64, offset=S)
-        gain_col = keep.tile([NP, A2, 4], F32, name="gain_col")
-        d_col = keep.tile([NP, A2, 4], F32, name="d_col")
+        gain_col = keep.tile([NP, A2, 8], F32, name="gain_col")
         w4_raw = [keep.tile([NP, A1 - 1, H], U8, name="w4_raw0", align_bytes=64)]
         w4_src = w4_words.rearrange("a p (b c) -> b p a c", b=A2)
         window = [first.tile([NP, T], I32, name="window0", align_bytes=64, offset=W4_RAW - LINK),
@@ -75,11 +75,10 @@ def tile_list_well_log_corrector_kernel(tc, tab_words, tab_scales, offs, pos1, p
         nc.sync.dma_start(offs_sb[:], offs)
         nc.sync.dma_start(window[0][:], tab_words[0].rearrange("p t i -> p (t i)").bitcast(I32))
         nc.sync.dma_start(pos1_sb[:], pos1)
-        nc.scalar.dma_start(gain_col[:], gain.rearrange("(b p t) -> p b t", b=A2, t=4))
+        nc.scalar.dma_start(gain_col[:, :, :4], gain.rearrange("(b p t) -> p b t", b=A2, t=4))
         nc.sync.dma_start(pos2_sb[:], pos2)
-        nc.scalar.dma_start(d_col[:], d.rearrange("(b p t) -> p b t", b=A2, t=4))
         nc.sync.dma_start(w4_raw[0][:].bitcast(I32), w4_src[0][:, : A1 - 1].bitcast(I32))
-        for tile in (w4_rows, tab_rows):
+        for tile in (tab_rows, w4_rows):
             nc.vector.memset(tile[0:16, :].bitcast(I32), 0)
             nc.vector.memset(tile[64:128, :].bitcast(I32), 0)
 
@@ -137,9 +136,9 @@ def tile_list_well_log_corrector_kernel(tc, tab_words, tab_scales, offs, pos1, p
         w4_raw.append(first.tile([NP, A1, H], U8, name="w4_raw1", align_bytes=64, offset=0))
         nc.sync.dma_start(w4_raw[1][:].bitcast(I32), w4_src[1].bitcast(I32))
         nc.vector.tensor_copy(words[1][:], window[1][:].bitcast(U32).indirect(offs_sb[:]))
-        for c in range(2):
-            nc.vector.tensor_copy(words_last[c][:],
-                                  window[2][:].bitcast(U32).indirect(offs_sb[:, N // 16 * c : N // 16 * (c + 1)]))
+        for low, high in PIECES:
+            nc.vector.tensor_copy(words_last[low // N][:, low % N : low % N + high - low],
+                                  window[2][:].bitcast(U32).indirect(offs_sb[:, low // 16 : high // 16]))
 
         w4_pair.append(shared.tile([NP, 2, A1, 2 * NP], U8, name="w4_pair2", align_bytes=64, offset=PAIRS + W4_PAIR))
         w4_pair.append(shared.tile([NP, 2, A1, 2 * NP], U8, name="w4_pair3", align_bytes=64, offset=PAIRS))
@@ -161,9 +160,12 @@ def tile_list_well_log_corrector_kernel(tc, tab_words, tab_scales, offs, pos1, p
                 nc.sync.dma_start(raw[:], w2_src[a, b])
                 w2_raw[a, b] = raw
 
-        def first_pass(acc, b, t, a, c):
-            cols = slice(N * c, N * (c + 1))
-            moving = words_last[c][:] if a == A1 - 1 else words[a][:, cols]
+        d_col = third.tile([NP, A2, 8], F32, name="d_col", align_bytes=64, offset=WINDOW + LINK)
+        nc.sync.dma_start(d_col[:, :, :4], d.rearrange("(b p t) -> p b t", b=A2, t=4))
+
+        def first_pass(acc, b, t, a, low, high):
+            cols = slice(low, high)
+            moving = words_last[low // N][:, low % N : low % N + high - low] if a == A1 - 1 else words[a][:, cols]
             w4_cols = slice(S + N * b + NP * t, S + N * b + NP * (t + 1))
             nc.tensor.matmul_mx(out=acc[:], lhsT=w4_pair[2 * b + t // 2][:, t % 2, a, :].bitcast(FP4X4), lhsT_scale=planes[:, a, w4_cols],
                                 rhs=moving.bitcast(FP8X4), rhs_scale=planes[:, a, cols],
@@ -204,10 +206,15 @@ def tile_list_well_log_corrector_kernel(tc, tab_words, tab_scales, offs, pos1, p
             nc.vector.quantize_mx(out=codes[:].bitcast(FP8X4), scales=scales[:], in_=w2_bf[a, b][:].rearrange("p t m j -> p (t m j)"))
             w2_mx[a, b] = (codes, scales)
 
-        early = {(0, t, c): psum.tile([NP, N], F32, name="bank1", tag="bank1") for t in range(EARLY_TILES) for c in range(2)}
+        def pieces(b, t):
+            return PIECES if (b, t) == (0, 0) else ((0, N), (N, S))
+
+        early = {(0, t, low): psum.tile([NP, high - low], F32, name="bank1", tag="bank2" if low % N else "bank1")
+                 for t in range(EARLY_TILES) for low, high in pieces(0, t)}
         for a in range(A1 - 1):
-            for (b, t, c), acc in early.items():
-                first_pass(acc, b, t, a, c)
+            for t in range(EARLY_TILES):
+                for low, high in pieces(0, t):
+                    first_pass(early[0, t, low], 0, t, a, low, high)
 
         x32 = []
         for b in range(A2):
@@ -215,15 +222,15 @@ def tile_list_well_log_corrector_kernel(tc, tab_words, tab_scales, offs, pos1, p
             for t in range(4):
                 h = keep.tile([NP, S], F32, name=f"h{b}{t}")
                 hs[b, t] = h
-                for c in range(2):
-                    if (b, t, c) in early:
-                        acc = early[b, t, c]
-                        first_pass(acc, b, t, A1 - 1, c)
+                for low, high in pieces(b, t):
+                    if (b, t, low) in early:
+                        acc = early[b, t, low]
+                        first_pass(acc, b, t, A1 - 1, low, high)
                     else:
                         acc = psum.tile([NP, N], F32, name="bank1", tag="bank1")
                         for a in range(A1):
-                            first_pass(acc, b, t, a, c)
-                    nc.scalar.activation(h[:, N * c : N * (c + 1)], acc[:], TANH)
+                            first_pass(acc, b, t, a, low, high)
+                    nc.scalar.activation(h[:, low:high], acc[:], TANH)
                 nc.vector.tensor_tensor(x_half[:, t, :], h[:].indirect(pos1_sb[:]), gain_full[b][t], MULT)
                 if 4 * b + t == EARLY_FINE - 1:
                     f00 = mid.tile([NP, P], F32, name="fine00", align_bytes=64, offset=FINE00)

@@ -116,7 +116,7 @@ def tile_list_well_log_corrector_kernel(tc, tab_words, tab_scales, offs, pos1, p
             nc.sync.dma_start(planes[32 * q : 32 * q + 4, 2, :].bitcast(I32), both_rows[48 + 4 * q : 52 + 4 * q, :].bitcast(I32))
 
         gain1 = mid.tile([NP, 4, P], F32, name="gain1", align_bytes=64, offset=GAIN1)
-        gain0 = [keep.tile([NP, P], F32, name="gain00"),
+        gain0 = [keep.tile([NP, P], F32, name="gain00", tag="w2_bf10", align_bytes=64),
                  mid.tile([NP, P], F32, name="gain01", align_bytes=64, offset=FINE00 + 4 * P - LINK),
                  keep.tile([NP, P], F32, name="gain02"),
                  keep.tile([NP, P], F32, name="gain03")]
@@ -179,31 +179,48 @@ def tile_list_well_log_corrector_kernel(tc, tab_words, tab_scales, offs, pos1, p
 
         w2_bf, w2_mx = {}, {}
 
+        def scalar_weave(dst, src, cols):
+            for start in range(0, cols, WEAVE_STEP):
+                part = slice(start, min(start + WEAVE_STEP, cols))
+                nc.scalar.copy(dst.rearrange("p t m j -> p m j t")[:, part], src.rearrange("p t m j -> p m j t")[:, part])
+
+        def gpsimd_weave(dst, src):
+            nc.gpsimd.tensor_scalar(dst.rearrange("p t m j -> p m t j"), src.rearrange("p t m j -> p m t j"), 1.0, 0.0, MULT, ADD)
+
         def weave_w2(a, b):
+            src = w2_raw[a, b][:].rearrange("p j (m t) -> p t m j", t=4)
             if (a, b) == (0, 0):
-                tile = mid.tile([NP, 4, NP, 4], BF16, name="w2_bf00", align_bytes=64, offset=W4_PAIR - LINK)
-            elif b == 0:
-                tile = mid.tile([NP, 4, NP, 4], BF16, name="w2_bf10", align_bytes=64, offset=FINE00 + 8 * P - 2 * LINK)
+                low = mid.tile([NP, 2, NP, 4], BF16, name="w2_bf00_low", align_bytes=64, offset=W4_PAIR - LINK)
+                high = mid.tile([NP, 2, NP, 4], BF16, name="w2_bf00_high", align_bytes=64, offset=FINE00 + 8 * P - 2 * LINK)
+                gpsimd_weave(high[:], src[:, 2:])
+                for start in range(0, NP, 2 * WEAVE_STEP):
+                    part = slice(start, start + 2 * WEAVE_STEP)
+                    nc.scalar.copy(low[:].rearrange("p t m j -> p m j t")[:, part], src[:, :2].rearrange("p t m j -> p m j t")[:, part])
+                w2_bf[a, b] = [low, high]
+                return
+            if b == 0:
+                tile = keep.tile([NP, 4, NP, 4], BF16, name="w2_bf10", tag="w2_bf10", align_bytes=64)
             else:
                 tile = late.tile([NP, 4, NP, 4], BF16, name=f"w2_bf{a}{b}", align_bytes=64, offset=(X32, LAST_BF)[a])
-            split = NP
-            if a == 1:
-                split = NP - GPSIMD_COLS
-                nc.gpsimd.tensor_scalar(tile[:].rearrange("p t m j -> p m t j")[:, split:],
-                                        w2_raw[a, b][:].rearrange("p j (m t) -> p m t j", t=4)[:, split:], 1.0, 0.0, MULT, ADD)
-            for start in range(0, split, WEAVE_STEP):
-                part = slice(start, min(start + WEAVE_STEP, split))
-                nc.scalar.copy(tile[:].rearrange("p t m j -> p m j t")[:, part],
-                               w2_raw[a, b][:].rearrange("p j (m t) -> p m j t", t=4)[:, part])
-            w2_bf[a, b] = tile
+            cols = NP
+            if (a, b) == (1, 1):
+                cols = NP - GPSIMD_COLS
+                gpsimd_weave(tile[:, :, cols:], src[:, :, cols:])
+            scalar_weave(tile[:], src, cols)
+            w2_bf[a, b] = [tile]
 
         def quantise_w2(a, b):
-            if (a, b) == (1, 0):
+            if (a, b) == (0, 0):
+                codes = third.tile([NP, N], U32, name="w2_codes00", align_bytes=64, offset=0)
+            elif (a, b) == (1, 0):
                 codes = mid.tile([NP, N], U32, name="w2_codes10", align_bytes=64, offset=GAIN1)
             else:
                 codes = keep.tile([NP, N], U32, name=f"w2_codes{a}{b}", align_bytes=64)
             scales = keep.tile([NP, N], U8, name=f"w2_scales{a}{b}", align_bytes=64)
-            nc.vector.quantize_mx(out=codes[:].bitcast(FP8X4), scales=scales[:], in_=w2_bf[a, b][:].rearrange("p t m j -> p (t m j)"))
+            width = N // len(w2_bf[a, b])
+            for i, tile in enumerate(w2_bf[a, b]):
+                cols = slice(width * i, width * (i + 1))
+                nc.vector.quantize_mx(out=codes[:, cols].bitcast(FP8X4), scales=scales[:, cols], in_=tile[:].rearrange("p t m j -> p (t m j)"))
             w2_mx[a, b] = (codes, scales)
 
         def pieces(b, t):

@@ -27,16 +27,16 @@ EARLY_TILES = 2
 EARLY_FINE = 2
 WEAVE_STEP = 32
 GPSIMD_COLS = 80
-OUT_PIECES = 7
+OUT_PIECES = 5
 
-PIECES = ((0, N), (N, N + N // 2), (N + N // 2, S))
+PIECE = N // 2
 QUADRANTS = (0, 2, 1, 3)
 
 WORDS = 4 * S
 WINDOW = 4 * T
 W4_RAW = A1 * H
 W4_PAIR = W4_RAW // 2
-PAIRS = WORDS + S // 2
+PAIRS = WORDS + 2 * WINDOW
 X32 = 16 * P
 X16 = 8 * P
 FINE00 = W4_PAIR - LINK + X16
@@ -101,7 +101,7 @@ def tile_list_well_log_corrector_kernel(tc, tab_words, tab_scales, offs, pos1, p
         for g in range(2):
             order_w4(nc.scalar.copy, g, w4_raw[0], slice(0, A1 - 1))
 
-        picked_rows = shared.tile([NP, S], U8, name="picked_rows", align_bytes=64, offset=WORDS - S // 2)
+        picked_rows = shared.tile([NP, S], U8, name="picked_rows", align_bytes=64, offset=WORDS)
         both_rows = keep.tile([NP, S + H], U8, name="both_rows", align_bytes=64)
         nc.gpsimd.tensor_copy(
             both_rows[:, S:].rearrange("p (b t m) -> p b t m", b=A2, t=4),
@@ -136,7 +136,8 @@ def tile_list_well_log_corrector_kernel(tc, tab_words, tab_scales, offs, pos1, p
         w4_raw.append(first.tile([NP, A1, H], U8, name="w4_raw1", align_bytes=64, offset=0))
         nc.sync.dma_start(w4_raw[1][:].bitcast(I32), w4_src[1].bitcast(I32))
         nc.vector.tensor_copy(words[1][:], window[1][:].bitcast(U32).indirect(offs_sb[:]))
-        for low, high in PIECES:
+        for low in range(0, S, PIECE):
+            high = low + PIECE
             nc.vector.tensor_copy(words_last[low // N][:, low % N : low % N + high - low],
                                   window[2][:].bitcast(U32).indirect(offs_sb[:, low // 16 : high // 16]))
 
@@ -201,7 +202,7 @@ def tile_list_well_log_corrector_kernel(tc, tab_words, tab_scales, offs, pos1, p
             if b == 0:
                 tile = keep.tile([NP, 4, NP, 4], BF16, name="w2_bf10", tag="w2_bf10", align_bytes=64)
             else:
-                tile = late.tile([NP, 4, NP, 4], BF16, name=f"w2_bf{a}{b}", align_bytes=64, offset=(X32, LAST_BF)[a])
+                tile = late.tile([NP, 4, NP, 4], BF16, name=f"w2_bf{a}{b}", align_bytes=64, offset=(X32 + LINK, LAST_BF)[a])
             cols = NP
             if (a, b) == (1, 1):
                 cols = NP - GPSIMD_COLS
@@ -223,37 +224,35 @@ def tile_list_well_log_corrector_kernel(tc, tab_words, tab_scales, offs, pos1, p
                 nc.vector.quantize_mx(out=codes[:, cols].bitcast(FP8X4), scales=scales[:, cols], in_=tile[:].rearrange("p t m j -> p (t m j)"))
             w2_mx[a, b] = (codes, scales)
 
-        def pieces(b, t):
-            return PIECES if (b, t) == (0, 0) else ((0, N), (N, S))
-
-        early = {(0, t, low): psum.tile([NP, high - low], F32, name="bank1", tag="bank2" if low % N else "bank1")
-                 for t in range(EARLY_TILES) for low, high in pieces(0, t)}
+        early = [(t, low + N * c, width) for c in range(2) for t, low, width in ((0, 0, PIECE), (0, PIECE, PIECE), (1, 0, N))]
+        accs = [psum.tile([NP, width], F32, name="bank1", tag="bank2" if low % N else "bank1") for t, low, width in early]
         for a in range(A1 - 1):
-            for t in range(EARLY_TILES):
-                for low, high in pieces(0, t):
-                    first_pass(early[0, t, low], 0, t, a, low, high)
+            for (t, low, width), acc in zip(early, accs):
+                first_pass(acc, 0, t, a, low, low + width)
+        for t in range(EARLY_TILES):
+            hs[0, t] = keep.tile([NP, S], F32, name=f"h0{t}")
+        for (t, low, width), acc in zip(early, accs):
+            first_pass(acc, 0, t, A1 - 1, low, low + width)
+            nc.scalar.activation(hs[0, t][:, low : low + width], acc[:], TANH)
 
         x32 = []
         for b in range(A2):
             x_half = late.tile([NP, 4, P], F32, name=f"x32{b}", align_bytes=64, offset=X32 * b)
             for t in range(4):
-                h = keep.tile([NP, S], F32, name=f"h{b}{t}")
-                hs[b, t] = h
-                for low, high in pieces(b, t):
-                    if (b, t, low) in early:
-                        acc = early[b, t, low]
-                        first_pass(acc, b, t, A1 - 1, low, high)
-                    else:
+                if (b, t) not in hs:
+                    hs[b, t] = keep.tile([NP, S], F32, name=f"h{b}{t}")
+                    for low in range(0, S, N):
                         acc = psum.tile([NP, N], F32, name="bank1", tag="bank1")
                         for a in range(A1):
-                            first_pass(acc, b, t, a, low, high)
-                    nc.scalar.activation(h[:, low:high], acc[:], TANH)
+                            first_pass(acc, b, t, a, low, low + N)
+                        nc.scalar.activation(hs[b, t][:, low : low + N], acc[:], TANH)
+                h = hs[b, t]
                 nc.vector.tensor_tensor(x_half[:, t, :], h[:].indirect(pos1_sb[:]), gain_full[b][t], MULT)
                 if 4 * b + t == EARLY_FINE - 1:
                     f00 = mid.tile([NP, P], F32, name="fine00", align_bytes=64, offset=FINE00)
                     f01 = keep.tile([NP, P], F32, name="fine01")
-                    gather_fine(0, 0, f00[:])
                     gather_fine(0, 1, f01[:])
+                    gather_fine(0, 0, f00[:])
             x32.append(x_half)
 
         for a in range(A2):
@@ -278,7 +277,7 @@ def tile_list_well_log_corrector_kernel(tc, tab_words, tab_scales, offs, pos1, p
             nc.vector.quantize_mx(out=codes[:].bitcast(FP8X4), scales=scales[:], in_=x_bf[:].rearrange("p m t -> p (m t)"))
             x_mx.append((codes, scales))
             if a == 0:
-                f02 = shared.tile([NP, P], F32, name="fine02", align_bytes=64, offset=X_BF0 + LINK)
+                f02 = late.tile([NP, P], F32, name="fine02", align_bytes=64, offset=0)
                 gather_fine(0, 2, f02[:])
 
         for a in range(A2):
@@ -298,21 +297,23 @@ def tile_list_well_log_corrector_kernel(tc, tab_words, tab_scales, offs, pos1, p
 
         def times_fine(b, t, m=slice(0, P)):
             if b == 0 and t >= 2:
-                fy = late.tile([NP, P], F32, name=f"fy{b}{t}", align_bytes=64, offset=LAST_BF + (LINK - 4 * P) * (3 - t) + LINK * (t - 2))
+                fy = first.tile([NP, P], F32, name=f"fy{b}{t}", align_bytes=64, offset=4 * P * t)
             else:
                 fy = keep.tile([NP, P], F32, name=f"fy{b}{t}_{m.start}", tag=f"fy{b}{t}_{m.start}")
             nc.vector.tensor_tensor(fy[:, m], banks[b, t][:, m], fine[b, t][:, m], MULT)
             fys[b, t, m.start] = fy
 
-        def finish_on_vector(b, t, res, queue, m=slice(0, P)):
-            nc.vector.scalar_tensor_tensor(res[:, m], fys[b, t, m.start][:, m], d_col[:, b, t : t + 1], fine[b, t][:, m], ADD, MULT)
+        def finish_on_vector(b, t, res, queue, m, fy):
+            nc.vector.scalar_tensor_tensor(res[:, m], fy[:, m], d_col[:, b, t : t + 1], fine[b, t][:, m], ADD, MULT)
             queue.dma_start(out_rows[b, t][:, m], res[:, m])
 
         def finish_on_gpsimd(b, t, res):
-            if b == 0:
+            if b == 0 and t < 2:
                 fyd = first.tile([NP, P], F32, name=f"fyd{b}{t}", align_bytes=64, offset=4 * P * t)
+            elif (b, t) == (1, 1):
+                fyd = late.tile([NP, P], F32, name="fyd11", align_bytes=64, offset=4 * P)
             else:
-                fyd = keep.tile([NP, P], F32, name=f"fyd{b}{t}", tag=f"fyd{b}{t}")
+                fyd = keep.tile([NP, P], F32, name=f"fyd{b}{t}")
             nc.scalar.activation(fyd[:], fys[b, t, 0][:], IDENT, bias=d_col[:, b, t : t + 1])
             nc.gpsimd.tensor_tensor(res[:], fyd[:], fine[b, t], MULT)
             nc.sync.dma_start(out_rows[b, t], res[:])
@@ -323,7 +324,7 @@ def tile_list_well_log_corrector_kernel(tc, tab_words, tab_scales, offs, pos1, p
         for t in range(4):
             for a in range(A2):
                 second_pass(a, 0, [t])
-        f03 = late.tile([NP, P], F32, name="fine03", align_bytes=64, offset=2 * X32 + 2 * LINK)
+        f03 = late.tile([NP, P], F32, name="fine03", align_bytes=64, offset=X32 + LINK - 4 * P)
         gather_fine(0, 3, f03[:])
         times_fine(0, 0)
         times_fine(0, 1)
@@ -339,18 +340,21 @@ def tile_list_well_log_corrector_kernel(tc, tab_words, tab_scales, offs, pos1, p
         for t, product in enumerate(("fy00_0", "fy01_0")):
             f = keep.tile([NP, P], F32, name=f"fine1{t}", tag=product)
             gather_fine(1, t, f[:])
-        for t in range(2):
-            times_fine(1, t)
-            finish_on_gpsimd(1, t, result(f"res1{t}"))
-        f12 = keep.tile([NP, P], F32, name="fine12", tag="fy10_0")
+        times_fine(1, 0)
+        finish_on_gpsimd(1, 0, result("res10"))
+        f12 = first.tile([NP, P], F32, name="fine12", align_bytes=64, offset=4 * P * 3)
         gather_fine(1, 2, f12[:])
-        times_fine(1, 2)
-        f13 = keep.tile([NP, P], F32, name="fine13", tag="fy11_0")
+        times_fine(1, 1)
+        finish_on_gpsimd(1, 1, result("res11"))
+        f13 = keep.tile([NP, P], F32, name="fine13", tag="fy10_0")
         gather_fine(1, 3, f13[:])
+        times_fine(1, 2)
         halves = [slice(0, P // 2), slice(P // 2, P)]
-        times_fine(1, 3, halves[0])
-        times_fine(1, 3, halves[1])
-        res12 = keep.tile([NP, P], F32, name="res12", tag="fyd11")
-        finish_on_vector(1, 2, res12, nc.scalar)
         for m in halves:
-            finish_on_vector(1, 3, result(f"res13_{m.start}"), nc.scalar, m)
+            times_fine(1, 3, m)
+        res12 = late.tile([NP, P], F32, name="res12", align_bytes=64, offset=LINK)
+        res13 = late.tile([NP, P], F32, name="res13", align_bytes=64, offset=8 * P - LINK)
+        for m in halves:
+            finish_on_vector(1, 2, res12, nc.scalar, m, fys[1, 2, 0])
+        for m in halves:
+            finish_on_vector(1, 3, res13, nc.scalar, m, fys[1, 3, m.start])

@@ -24,25 +24,28 @@ A2 = H // 512
 N = 512
 LINK = 64
 EARLY_TILES = 2
-EARLY_FINE = 2
-WEAVE_STEP = 32
-GPSIMD_COLS = 80
-OUT_PIECES = 5
-
+BANKS = 4
 PIECE = N // 2
+WEAVE_STEP = 32
+X_STEPS = 4
+GPSIMD_COLS = 88
+RING = 5
 QUADRANTS = (0, 2, 1, 3)
 
 WORDS = 4 * S
 WINDOW = 4 * T
 W4_RAW = A1 * H
 W4_PAIR = W4_RAW // 2
+TILE = 4 * P
+X32 = 4 * TILE
+X16 = 2 * TILE
+
 PAIRS = WORDS + 2 * WINDOW
-X32 = 16 * P
-X16 = 8 * P
-FINE00 = W4_PAIR - LINK + X16
 X_BF0 = PAIRS + 2 * W4_PAIR - LINK
-X_STEPS = 4
-GAIN1 = FINE00 + 8 * P - 2 * LINK + X16
+FINE00 = W4_PAIR - LINK + X16
+GAIN01 = FINE00 + TILE - LINK
+CODES10 = GAIN01 + TILE - LINK + X16
+GAIN13 = CODES10 + TILE - LINK
 LAST_BF = X32 + X16 + LINK
 
 
@@ -56,8 +59,8 @@ def tile_list_well_log_corrector_kernel(tc, tab_words, tab_scales, offs, pos1, p
         first = ctx.enter_context(tc.tile_pool(name="first", bufs=1))
         third = ctx.enter_context(tc.tile_pool(name="third", bufs=1))
         mid = ctx.enter_context(tc.tile_pool(name="mid", bufs=1))
-        ring = ctx.enter_context(tc.tile_pool(name="ring", bufs=OUT_PIECES))
-        psum = ctx.enter_context(tc.psum_pool(name="psum", bufs=2 * EARLY_TILES))
+        ring = ctx.enter_context(tc.tile_pool(name="ring", bufs=RING))
+        psum = ctx.enter_context(tc.psum_pool(name="psum", bufs=BANKS))
 
         offs_sb = lists.tile([NP, S // 16], U16, name="offs_sb")
         pos1_sb = lists.tile([NP, P // 16], U16, name="pos1_sb")
@@ -65,7 +68,7 @@ def tile_list_well_log_corrector_kernel(tc, tab_words, tab_scales, offs, pos1, p
         tab_rows = keep.tile([NP, T], U8, name="tab_rows", align_bytes=64)
         w4_rows = shared.tile([NP, H], U8, name="w4_rows", align_bytes=64, offset=S)
         gain_col = keep.tile([NP, A2, 8], F32, name="gain_col")
-        w4_raw = [keep.tile([NP, A1 - 1, H], U8, name="w4_raw0", align_bytes=64)]
+        w4_early = keep.tile([NP, A1 - 1, H], U8, name="w4_early", align_bytes=64)
         w4_src = w4_words.rearrange("a p (b c) -> b p a c", b=A2)
         window = [first.tile([NP, T], I32, name="window0", align_bytes=64, offset=W4_RAW - LINK),
                   third.tile([NP, T], I32, name="window1", align_bytes=64, offset=WINDOW - LINK)]
@@ -77,7 +80,7 @@ def tile_list_well_log_corrector_kernel(tc, tab_words, tab_scales, offs, pos1, p
         nc.sync.dma_start(pos1_sb[:], pos1)
         nc.scalar.dma_start(gain_col[:, :, :4], gain.rearrange("(b p t) -> p b t", b=A2, t=4))
         nc.sync.dma_start(pos2_sb[:], pos2)
-        nc.sync.dma_start(w4_raw[0][:].bitcast(I32), w4_src[0][:, : A1 - 1].bitcast(I32))
+        nc.sync.dma_start(w4_early[:].bitcast(I32), w4_src[0][:, : A1 - 1].bitcast(I32))
         for tile in (tab_rows, w4_rows):
             nc.vector.memset(tile[0:16, :].bitcast(I32), 0)
             nc.vector.memset(tile[64:128, :].bitcast(I32), 0)
@@ -99,7 +102,7 @@ def tile_list_well_log_corrector_kernel(tc, tab_words, tab_scales, offs, pos1, p
                  raw[:].bitcast(U16).rearrange("p a (m t) -> p t a m", t=4)[:, 2 * (g % 2) : 2 * (g % 2) + 2])
 
         for g in range(2):
-            order_w4(nc.scalar.copy, g, w4_raw[0], slice(0, A1 - 1))
+            order_w4(nc.scalar.copy, g, w4_early, slice(0, A1 - 1))
 
         picked_rows = shared.tile([NP, S], U8, name="picked_rows", align_bytes=64, offset=WORDS)
         both_rows = keep.tile([NP, S + H], U8, name="both_rows", align_bytes=64)
@@ -115,74 +118,69 @@ def tile_list_well_log_corrector_kernel(tc, tab_words, tab_scales, offs, pos1, p
         for q in QUADRANTS:
             nc.sync.dma_start(planes[32 * q : 32 * q + 4, 2, :].bitcast(I32), both_rows[48 + 4 * q : 52 + 4 * q, :].bitcast(I32))
 
-        gain1 = mid.tile([NP, 4, P], F32, name="gain1", align_bytes=64, offset=GAIN1)
         gain0 = [keep.tile([NP, P], F32, name="gain00", tag="w2_bf10", align_bytes=64),
-                 mid.tile([NP, P], F32, name="gain01", align_bytes=64, offset=FINE00 + 4 * P - LINK),
+                 mid.tile([NP, P], F32, name="gain01", align_bytes=64, offset=GAIN01),
                  keep.tile([NP, P], F32, name="gain02"),
                  keep.tile([NP, P], F32, name="gain03")]
-        gain_full = [[tile[:] for tile in gain0], [gain1[:, t, :] for t in range(4)]]
+        gain1 = [keep.tile([NP, P], F32, name=f"gain1{t}") for t in range(3)]
+        gain_last = [mid.tile([NP, P // 2], F32, name="gain13a", align_bytes=64, offset=GAIN13),
+                     keep.tile([NP, P // 2], F32, name="gain13b")]
+        gain_full = [[[tile] for tile in gain0], [[tile] for tile in gain1] + [gain_last]]
         for b in range(A2):
             for t in range(4):
-                nc.scalar.copy(gain_full[b][t], gain_col[:, b, t : t + 1].to_broadcast([NP, P]))
+                for tile in gain_full[b][t]:
+                    nc.scalar.copy(tile[:], gain_col[:, b, t : t + 1].to_broadcast(tile.shape))
 
-        words = [shared.tile([NP, S], U32, name="words0", align_bytes=64, offset=0)]
-        words.append(keep.tile([NP, S], U32, name="words1", align_bytes=64))
-        words_last = [keep.tile([NP, N], U32, name=f"words_last{c}", align_bytes=64) for c in range(2)]
+        words = [shared.tile([NP, S], U32, name="words0", align_bytes=64, offset=0),
+                 keep.tile([NP, S], U32, name="words1", align_bytes=64)]
+        words_last = [keep.tile([NP, N], U32, name=f"words_last{c}", align_bytes=64) for c in range(S // N)]
+
+        def last_words(low, high):
+            return words_last[low // N][:, low % N : low % N + high - low]
+
         nc.vector.tensor_copy(words[0][:], window[0][:].bitcast(U32).indirect(offs_sb[:]))
         w4_last = first.tile([NP, 1, H], U8, name="w4_last", align_bytes=64, offset=W4_RAW + WINDOW - 2 * LINK)
         nc.sync.dma_start(w4_last[:].bitcast(I32), w4_src[0][:, A1 - 1 :].bitcast(I32))
         for g in range(2):
             order_w4(nc.scalar.copy, g, w4_last, slice(A1 - 1, A1))
-        w4_raw.append(first.tile([NP, A1, H], U8, name="w4_raw1", align_bytes=64, offset=0))
-        nc.sync.dma_start(w4_raw[1][:].bitcast(I32), w4_src[1].bitcast(I32))
+        w4_second = first.tile([NP, A1, H], U8, name="w4_second", align_bytes=64, offset=0)
+        nc.sync.dma_start(w4_second[:].bitcast(I32), w4_src[1].bitcast(I32))
         nc.vector.tensor_copy(words[1][:], window[1][:].bitcast(U32).indirect(offs_sb[:]))
         for low in range(0, S, PIECE):
-            high = low + PIECE
-            nc.vector.tensor_copy(words_last[low // N][:, low % N : low % N + high - low],
-                                  window[2][:].bitcast(U32).indirect(offs_sb[:, low // 16 : high // 16]))
+            nc.vector.tensor_copy(last_words(low, low + PIECE),
+                                  window[2][:].bitcast(U32).indirect(offs_sb[:, low // 16 : (low + PIECE) // 16]))
 
         w4_pair.append(shared.tile([NP, 2, A1, 2 * NP], U8, name="w4_pair2", align_bytes=64, offset=PAIRS + W4_PAIR))
         w4_pair.append(shared.tile([NP, 2, A1, 2 * NP], U8, name="w4_pair3", align_bytes=64, offset=PAIRS))
         for g in (2, 3):
-            order_w4(nc.vector.tensor_copy, g, w4_raw[1], slice(0, A1))
+            order_w4(nc.vector.tensor_copy, g, w4_second, slice(0, A1))
 
         w2_src = w2.rearrange("(a p j) (b n) -> a b p j n", a=A2, j=4, b=A2)
         w2_raw = {}
-        for b in range(A2):
-            for a in range(A2):
-                if (a, b) == (0, 0):
-                    raw = third.tile([NP, 4, N], F32, name="w2_raw00", align_bytes=64, offset=0)
-                elif (a, b) == (1, 0):
-                    raw = third.tile([NP, 4, N], F32, name="w2_raw10", align_bytes=64, offset=2 * WINDOW - 2 * LINK)
-                elif (a, b) == (0, 1):
-                    raw = shared.tile([NP, 4, N], F32, name="w2_raw01", align_bytes=64, offset=WORDS + WINDOW)
-                else:
-                    raw = first.tile([NP, 4, N], F32, name="w2_raw11", align_bytes=64, offset=0)
-                nc.sync.dma_start(raw[:], w2_src[a, b])
-                w2_raw[a, b] = raw
+        for a, b, pool, offset in ((0, 0, third, 0), (1, 0, third, 2 * WINDOW - 2 * LINK), (0, 1, shared, WORDS + WINDOW), (1, 1, first, 0)):
+            w2_raw[a, b] = pool.tile([NP, 4, N], F32, name=f"w2_raw{a}{b}", align_bytes=64, offset=offset)
+            nc.sync.dma_start(w2_raw[a, b][:], w2_src[a, b])
 
         d_col = third.tile([NP, A2, 8], F32, name="d_col", align_bytes=64, offset=WINDOW + LINK)
         nc.sync.dma_start(d_col[:, :, :4], d.rearrange("(b p t) -> p b t", b=A2, t=4))
 
         def first_pass(acc, b, t, a, low, high):
             cols = slice(low, high)
-            moving = words_last[low // N][:, low % N : low % N + high - low] if a == A1 - 1 else words[a][:, cols]
+            moving = last_words(low, high) if a == A1 - 1 else words[a][:, cols]
             w4_cols = slice(S + N * b + NP * t, S + N * b + NP * (t + 1))
             nc.tensor.matmul_mx(out=acc[:], lhsT=w4_pair[2 * b + t // 2][:, t % 2, a, :].bitcast(FP4X4), lhsT_scale=planes[:, a, w4_cols],
                                 rhs=moving.bitcast(FP8X4), rhs_scale=planes[:, a, cols],
                                 start=(a == 0), stop=(a == A1 - 1))
 
-        hs, fine = {}, {}
+        hs, fine, w2_bf, w2_mx = {}, {}, {}, {}
 
         def gather_fine(b, t, dst):
-            nc.vector.tensor_copy(dst, hs[b, t][:].indirect(pos2_sb[:]))
+            nc.vector.tensor_copy(dst[:], hs[b, t][:].indirect(pos2_sb[:]))
             fine[b, t] = dst
 
-        w2_bf, w2_mx = {}, {}
-
-        def scalar_weave(dst, src, cols):
-            for start in range(0, cols, WEAVE_STEP):
-                part = slice(start, min(start + WEAVE_STEP, cols))
+        def scalar_weave(dst, src, cols, step):
+            for start in range(0, cols, step):
+                part = slice(start, min(start + step, cols))
                 nc.scalar.copy(dst.rearrange("p t m j -> p m j t")[:, part], src.rearrange("p t m j -> p m j t")[:, part])
 
         def gpsimd_weave(dst, src):
@@ -192,11 +190,9 @@ def tile_list_well_log_corrector_kernel(tc, tab_words, tab_scales, offs, pos1, p
             src = w2_raw[a, b][:].rearrange("p j (m t) -> p t m j", t=4)
             if (a, b) == (0, 0):
                 low = mid.tile([NP, 2, NP, 4], BF16, name="w2_bf00_low", align_bytes=64, offset=W4_PAIR - LINK)
-                high = mid.tile([NP, 2, NP, 4], BF16, name="w2_bf00_high", align_bytes=64, offset=FINE00 + 8 * P - 2 * LINK)
+                high = mid.tile([NP, 2, NP, 4], BF16, name="w2_bf00_high", align_bytes=64, offset=GAIN01 + TILE - LINK)
                 gpsimd_weave(high[:], src[:, 2:])
-                for start in range(0, NP, 2 * WEAVE_STEP):
-                    part = slice(start, start + 2 * WEAVE_STEP)
-                    nc.scalar.copy(low[:].rearrange("p t m j -> p m j t")[:, part], src[:, :2].rearrange("p t m j -> p m j t")[:, part])
+                scalar_weave(low[:], src[:, :2], NP, 2 * WEAVE_STEP)
                 w2_bf[a, b] = [low, high]
                 return
             if b == 0:
@@ -207,14 +203,14 @@ def tile_list_well_log_corrector_kernel(tc, tab_words, tab_scales, offs, pos1, p
             if (a, b) == (1, 1):
                 cols = NP - GPSIMD_COLS
                 gpsimd_weave(tile[:, :, cols:], src[:, :, cols:])
-            scalar_weave(tile[:], src, cols)
+            scalar_weave(tile[:], src, cols, WEAVE_STEP if b == 0 else NP)
             w2_bf[a, b] = [tile]
 
         def quantise_w2(a, b):
             if (a, b) == (0, 0):
                 codes = third.tile([NP, N], U32, name="w2_codes00", align_bytes=64, offset=0)
             elif (a, b) == (1, 0):
-                codes = mid.tile([NP, N], U32, name="w2_codes10", align_bytes=64, offset=GAIN1)
+                codes = mid.tile([NP, N], U32, name="w2_codes10", align_bytes=64, offset=CODES10)
             else:
                 codes = keep.tile([NP, N], U32, name=f"w2_codes{a}{b}", align_bytes=64)
             scales = keep.tile([NP, N], U8, name=f"w2_scales{a}{b}", align_bytes=64)
@@ -224,7 +220,7 @@ def tile_list_well_log_corrector_kernel(tc, tab_words, tab_scales, offs, pos1, p
                 nc.vector.quantize_mx(out=codes[:, cols].bitcast(FP8X4), scales=scales[:, cols], in_=tile[:].rearrange("p t m j -> p (t m j)"))
             w2_mx[a, b] = (codes, scales)
 
-        early = [(t, low + N * c, width) for c in range(2) for t, low, width in ((0, 0, PIECE), (0, PIECE, PIECE), (1, 0, N))]
+        early = [(t, low + N * c, width) for c in range(S // N) for t, low, width in ((0, 0, PIECE), (0, PIECE, PIECE), (1, 0, N))]
         accs = [psum.tile([NP, width], F32, name="bank1", tag="bank2" if low % N else "bank1") for t, low, width in early]
         for a in range(A1 - 1):
             for (t, low, width), acc in zip(early, accs):
@@ -247,12 +243,13 @@ def tile_list_well_log_corrector_kernel(tc, tab_words, tab_scales, offs, pos1, p
                             first_pass(acc, b, t, a, low, low + N)
                         nc.scalar.activation(hs[b, t][:, low : low + N], acc[:], TANH)
                 h = hs[b, t]
-                nc.vector.tensor_tensor(x_half[:, t, :], h[:].indirect(pos1_sb[:]), gain_full[b][t], MULT)
-                if 4 * b + t == EARLY_FINE - 1:
-                    f00 = mid.tile([NP, P], F32, name="fine00", align_bytes=64, offset=FINE00)
-                    f01 = keep.tile([NP, P], F32, name="fine01")
-                    gather_fine(0, 1, f01[:])
-                    gather_fine(0, 0, f00[:])
+                cuts = len(gain_full[b][t])
+                for i in range(cuts):
+                    m = slice(P // cuts * i, P // cuts * (i + 1))
+                    nc.vector.tensor_tensor(x_half[:, t, m], h[:].indirect(pos1_sb[:, m.start // 16 : m.stop // 16]), gain_full[b][t][i][:], MULT)
+                if (b, t) == (0, EARLY_TILES - 1):
+                    gather_fine(0, 1, keep.tile([NP, P], F32, name="fine01"))
+                    gather_fine(0, 0, mid.tile([NP, P], F32, name="fine00", align_bytes=64, offset=FINE00))
             x32.append(x_half)
 
         for a in range(A2):
@@ -265,20 +262,21 @@ def tile_list_well_log_corrector_kernel(tc, tab_words, tab_scales, offs, pos1, p
                 x_bf = shared.tile([NP, P, 4], BF16, name="x_bf0", align_bytes=64, offset=X_BF0)
             else:
                 x_bf = late.tile([NP, P, 4], BF16, name="x_bf1", align_bytes=64, offset=2 * X32)
-            steps = X_STEPS if a == 0 else 1
+            steps, cuts = ((X_STEPS, 1), (2, 2))[a]
             for step in range(steps):
                 part = slice(P // 4 // steps * step, P // 4 // steps * (step + 1))
                 nc.scalar.copy(x_bf[:].rearrange("p (c i) t -> p c t i", i=4)[:, part], x32[a][:].rearrange("p t (c i) -> p c t i", i=4)[:, part])
             if a == 0:
-                codes = mid.tile([NP, P], U32, name="x_codes0", align_bytes=64, offset=GAIN1 + 4 * N)
+                codes = mid.tile([NP, P], U32, name="x_codes0", align_bytes=64, offset=GAIN13 + TILE // 2 - LINK)
             else:
                 codes = keep.tile([NP, P], U32, name="x_codes1", align_bytes=64)
             scales = keep.tile([NP, P], U8, name=f"x_scales{a}", align_bytes=64)
-            nc.vector.quantize_mx(out=codes[:].bitcast(FP8X4), scales=scales[:], in_=x_bf[:].rearrange("p m t -> p (m t)"))
+            for i in range(cuts):
+                m = slice(P // cuts * i, P // cuts * (i + 1))
+                nc.vector.quantize_mx(out=codes[:, m].bitcast(FP8X4), scales=scales[:, m], in_=x_bf[:, m, :].rearrange("p m t -> p (m t)"))
             x_mx.append((codes, scales))
             if a == 0:
-                f02 = late.tile([NP, P], F32, name="fine02", align_bytes=64, offset=0)
-                gather_fine(0, 2, f02[:])
+                gather_fine(0, 2, late.tile([NP, P], F32, name="fine02", align_bytes=64, offset=0))
 
         for a in range(A2):
             weave_w2(a, 1)
@@ -286,75 +284,65 @@ def tile_list_well_log_corrector_kernel(tc, tab_words, tab_scales, offs, pos1, p
         out_rows = out.rearrange("(b p t) m -> b t p m", b=A2, t=4)
         banks, fys = {}, {}
 
-        def second_pass(a, b, tiles=range(4)):
-            for t in tiles:
-                if a == 0:
-                    banks[b, t] = psum.tile([NP, N], F32, name="bank2", tag=("bank2", "bank1")[b])
-                cols = slice(NP * t, NP * (t + 1))
-                nc.tensor.matmul_mx(out=banks[b, t][:], lhsT=w2_mx[a, b][0][:, cols].bitcast(FP8X4), lhsT_scale=w2_mx[a, b][1][:, cols],
-                                    rhs=x_mx[a][0][:].bitcast(FP8X4), rhs_scale=x_mx[a][1][:],
-                                    start=(a == 0), stop=(a == A2 - 1))
+        def second_pass(a, b, t):
+            if a == 0:
+                banks[b, t] = psum.tile([NP, N], F32, name="bank2", tag=("bank2", "bank1")[b])
+            cols = slice(NP * t, NP * (t + 1))
+            nc.tensor.matmul_mx(out=banks[b, t][:], lhsT=w2_mx[a, b][0][:, cols].bitcast(FP8X4), lhsT_scale=w2_mx[a, b][1][:, cols],
+                                rhs=x_mx[a][0][:].bitcast(FP8X4), rhs_scale=x_mx[a][1][:],
+                                start=(a == 0), stop=(a == A2 - 1))
 
-        def times_fine(b, t, m=slice(0, P)):
+        def times_fine(b, t):
             if b == 0 and t >= 2:
-                fy = first.tile([NP, P], F32, name=f"fy{b}{t}", align_bytes=64, offset=4 * P * t)
+                fy = first.tile([NP, P], F32, name=f"fy{b}{t}", align_bytes=64, offset=TILE * t)
             else:
-                fy = keep.tile([NP, P], F32, name=f"fy{b}{t}_{m.start}", tag=f"fy{b}{t}_{m.start}")
-            nc.vector.tensor_tensor(fy[:, m], banks[b, t][:, m], fine[b, t][:, m], MULT)
-            fys[b, t, m.start] = fy
+                fy = keep.tile([NP, P], F32, name=f"fy{b}{t}", tag=f"fy{b}{t}")
+            nc.vector.tensor_tensor(fy[:], banks[b, t][:], fine[b, t][:], MULT)
+            fys[b, t] = fy
 
-        def finish_on_vector(b, t, res, queue, m, fy):
-            nc.vector.scalar_tensor_tensor(res[:, m], fy[:, m], d_col[:, b, t : t + 1], fine[b, t][:, m], ADD, MULT)
-            queue.dma_start(out_rows[b, t][:, m], res[:, m])
+        def finish_on_vector(b, t, res):
+            for m in (slice(0, P // 2), slice(P // 2, P)):
+                nc.vector.scalar_tensor_tensor(res[:, m], fys[b, t][:, m], d_col[:, b, t : t + 1], fine[b, t][:, m], ADD, MULT)
+                nc.scalar.dma_start(out_rows[b, t][:, m], res[:, m])
 
         def finish_on_gpsimd(b, t, res):
             if b == 0 and t < 2:
-                fyd = first.tile([NP, P], F32, name=f"fyd{b}{t}", align_bytes=64, offset=4 * P * t)
+                fyd = first.tile([NP, P], F32, name=f"fyd{b}{t}", align_bytes=64, offset=TILE * t)
             elif (b, t) == (1, 1):
-                fyd = late.tile([NP, P], F32, name="fyd11", align_bytes=64, offset=4 * P)
+                fyd = late.tile([NP, P], F32, name="fyd11", align_bytes=64, offset=TILE)
             else:
                 fyd = keep.tile([NP, P], F32, name=f"fyd{b}{t}")
-            nc.scalar.activation(fyd[:], fys[b, t, 0][:], IDENT, bias=d_col[:, b, t : t + 1])
-            nc.gpsimd.tensor_tensor(res[:], fyd[:], fine[b, t], MULT)
+            nc.scalar.activation(fyd[:], fys[b, t][:], IDENT, bias=d_col[:, b, t : t + 1])
+            nc.gpsimd.tensor_tensor(res[:], fyd[:], fine[b, t][:], MULT)
             nc.sync.dma_start(out_rows[b, t], res[:])
 
-        def result(name):
-            return ring.tile([NP, P], F32, name=name, tag="res")
+        def result(b, t):
+            return ring.tile([NP, P], F32, name=f"res{b}{t}", tag="res")
 
         for t in range(4):
             for a in range(A2):
-                second_pass(a, 0, [t])
-        f03 = late.tile([NP, P], F32, name="fine03", align_bytes=64, offset=X32 + LINK - 4 * P)
-        gather_fine(0, 3, f03[:])
+                second_pass(a, 0, t)
+        gather_fine(0, 3, late.tile([NP, P], F32, name="fine03", align_bytes=64, offset=X32 + LINK - TILE))
         times_fine(0, 0)
         times_fine(0, 1)
         for a in range(A2):
             quantise_w2(a, 1)
-            second_pass(a, 1)
-        res00 = late.tile([NP, P], F32, name="res00", align_bytes=64, offset=LAST_BF + LINK + 4 * P)
-        finish_on_gpsimd(0, 0, res00)
-        finish_on_gpsimd(0, 1, result("res01"))
+            for t in range(4):
+                second_pass(a, 1, t)
+        finish_on_gpsimd(0, 0, late.tile([NP, P], F32, name="res00", align_bytes=64, offset=LAST_BF + LINK + TILE))
+        finish_on_gpsimd(0, 1, result(0, 1))
         for t in (2, 3):
             times_fine(0, t)
-            finish_on_gpsimd(0, t, result(f"res0{t}"))
-        for t, product in enumerate(("fy00_0", "fy01_0")):
-            f = keep.tile([NP, P], F32, name=f"fine1{t}", tag=product)
-            gather_fine(1, t, f[:])
+            finish_on_gpsimd(0, t, result(0, t))
+        for t in range(2):
+            gather_fine(1, t, keep.tile([NP, P], F32, name=f"fine1{t}", tag=f"fy0{t}"))
         times_fine(1, 0)
-        finish_on_gpsimd(1, 0, result("res10"))
-        f12 = first.tile([NP, P], F32, name="fine12", align_bytes=64, offset=4 * P * 3)
-        gather_fine(1, 2, f12[:])
+        finish_on_gpsimd(1, 0, result(1, 0))
+        gather_fine(1, 2, first.tile([NP, P], F32, name="fine12", align_bytes=64, offset=TILE * 3))
         times_fine(1, 1)
-        finish_on_gpsimd(1, 1, result("res11"))
-        f13 = keep.tile([NP, P], F32, name="fine13", tag="fy10_0")
-        gather_fine(1, 3, f13[:])
+        finish_on_gpsimd(1, 1, result(1, 1))
+        gather_fine(1, 3, keep.tile([NP, P], F32, name="fine13", tag="fy10"))
         times_fine(1, 2)
-        halves = [slice(0, P // 2), slice(P // 2, P)]
-        for m in halves:
-            times_fine(1, 3, m)
-        res12 = late.tile([NP, P], F32, name="res12", align_bytes=64, offset=LINK)
-        res13 = late.tile([NP, P], F32, name="res13", align_bytes=64, offset=8 * P - LINK)
-        for m in halves:
-            finish_on_vector(1, 2, res12, nc.scalar, m, fys[1, 2, 0])
-        for m in halves:
-            finish_on_vector(1, 3, res13, nc.scalar, m, fys[1, 3, m.start])
+        times_fine(1, 3)
+        finish_on_vector(1, 2, late.tile([NP, P], F32, name="res12", align_bytes=64, offset=LINK))
+        finish_on_vector(1, 3, late.tile([NP, P], F32, name="res13", align_bytes=64, offset=2 * TILE - LINK))

@@ -66,7 +66,7 @@ def tile_list_well_log_corrector_kernel(tc, tab_words, tab_scales, offs, pos1, p
         pos1_sb = lists.tile([NP, P // 16], U16, name="pos1_sb")
         pos2_sb = lists.tile([NP, P // 16], U16, name="pos2_sb")
         tab_rows = keep.tile([NP, T], U8, name="tab_rows", align_bytes=64)
-        w4_rows = shared.tile([NP, H], U8, name="w4_rows", align_bytes=64, offset=S)
+        w4_rows = keep.tile([NP, H], U8, name="w4_rows", align_bytes=64)
         gain_col = keep.tile([NP, A2, 8], F32, name="gain_col")
         w4_early = keep.tile([NP, A1 - 1, H], U8, name="w4_early", align_bytes=64)
         w4_src = w4_words.rearrange("a p (b c) -> b p a c", b=A2)

@@ -293,7 +293,7 @@ def tile_list_well_log_corrector_kernel(tc, tab_words, tab_scales, offs, pos1, p
                                 start=(a == 0), stop=(a == A2 - 1))
 
         def times_fine(b, t):
-            if b == 0 and t >= 2:
+            if (b, t) == (0, 3):
                 fy = first.tile([NP, P], F32, name=f"fy{b}{t}", align_bytes=64, offset=TILE * t)
             else:
                 fy = keep.tile([NP, P], F32, name=f"fy{b}{t}", tag=f"fy{b}{t}")
@@ -306,7 +306,7 @@ def tile_list_well_log_corrector_kernel(tc, tab_words, tab_scales, offs, pos1, p
                 nc.scalar.dma_start(out_rows[b, t][:, m], res[:, m])
 
         def finish_on_gpsimd(b, t, res):
-            if b == 0 and t < 2:
+            if b == 0 and t < 3:
                 fyd = first.tile([NP, P], F32, name=f"fyd{b}{t}", align_bytes=64, offset=TILE * t)
             elif (b, t) == (1, 1):
                 fyd = late.tile([NP, P], F32, name="fyd11", align_bytes=64, offset=TILE)
@@ -323,16 +323,16 @@ def tile_list_well_log_corrector_kernel(tc, tab_words, tab_scales, offs, pos1, p
             for a in range(A2):
                 second_pass(a, 0, t)
         gather_fine(0, 3, late.tile([NP, P], F32, name="fine03", align_bytes=64, offset=X32 + LINK - TILE))
-        times_fine(0, 0)
-        times_fine(0, 1)
+        for t in range(3):
+            times_fine(0, t)
         for a in range(A2):
             quantise_w2(a, 1)
             for t in range(4):
                 second_pass(a, 1, t)
         finish_on_gpsimd(0, 0, late.tile([NP, P], F32, name="res00", align_bytes=64, offset=LAST_BF + LINK + TILE))
         finish_on_gpsimd(0, 1, result(0, 1))
+        times_fine(0, 3)
         for t in (2, 3):
-            times_fine(0, t)
             finish_on_gpsimd(0, t, result(0, t))
         for t in range(2):
             gather_fine(1, t, keep.tile([NP, P], F32, name=f"fine1{t}", tag=f"fy0{t}"))

@@ -306,7 +306,7 @@ def tile_list_well_log_corrector_kernel(tc, tab_words, tab_scales, offs, pos1, p
                 nc.scalar.dma_start(out_rows[b, t][:, m], res[:, m])
 
         def finish_on_gpsimd(b, t, res):
-            if b == 0 and t < 3:
+            if b == 0 and t in (1, 2):
                 fyd = first.tile([NP, P], F32, name=f"fyd{b}{t}", align_bytes=64, offset=TILE * t)
             elif (b, t) == (1, 1):
                 fyd = late.tile([NP, P], F32, name="fyd11", align_bytes=64, offset=TILE)
@@ -329,7 +329,7 @@ def tile_list_well_log_corrector_kernel(tc, tab_words, tab_scales, offs, pos1, p
             quantise_w2(a, 1)
             for t in range(4):
                 second_pass(a, 1, t)
-        finish_on_gpsimd(0, 0, late.tile([NP, P], F32, name="res00", align_bytes=64, offset=LAST_BF + LINK + TILE))
+        finish_on_gpsimd(0, 0, late.tile([NP, P], F32, name="res00", align_bytes=64, offset=X32 + 2 * LINK))
         finish_on_gpsimd(0, 1, result(0, 1))
         times_fine(0, 3)
         for t in (2, 3):

from contextlib import ExitStack

import concourse.mybir as mybir

K, T, S, P, H = 1536, 2048, 1024, 512, 1024
FLOPS = 2 * K * H * S + 2 * H * H * P

F32 = mybir.dt.float32
BF16 = mybir.dt.bfloat16
I32 = mybir.dt.int32
U32 = mybir.dt.uint32
U16 = mybir.dt.uint16
U8 = mybir.dt.uint8
FP8X4 = mybir.dt.float8_e4m3fn_x4
FP4X4 = mybir.dt.float4_e2m1fn_x4
MULT = mybir.AluOpType.mult
ADD = mybir.AluOpType.add
TANH = mybir.ActivationFunctionType.Tanh
IDENT = mybir.ActivationFunctionType.Identity

NP = 128
A1 = K // 512
A2 = H // 512
N = 512
LINK = 64
EARLY_TILES = 2
BANKS = 4
PIECE = N // 2
WEAVE_STEP = 32
X_STEPS = 4
GPSIMD_COLS = 88
RING = 5
QUADRANTS = (0, 2, 1, 3)

WORDS = 4 * S
WINDOW = 4 * T
W4_RAW = A1 * H
W4_PAIR = W4_RAW // 2
TILE = 4 * P
X32 = 4 * TILE
X16 = 2 * TILE

PAIRS = WORDS + 2 * WINDOW
X_BF0 = PAIRS + 2 * W4_PAIR - LINK
FINE00 = W4_PAIR - LINK + X16
GAIN01 = FINE00 + TILE - LINK
CODES10 = GAIN01 + TILE - LINK + X16
GAIN13 = CODES10 + TILE - LINK
LAST_BF = X32 + X16 + LINK


def tile_list_well_log_corrector_kernel(tc, tab_words, tab_scales, offs, pos1, pos2, w4_words, w4_scales, gain, w2, d, out):
    nc = tc.nc
    with ExitStack() as ctx:
        lists = ctx.enter_context(tc.tile_pool(name="lists", bufs=1))
        keep = ctx.enter_context(tc.tile_pool(name="keep", bufs=1))
        shared = ctx.enter_context(tc.tile_pool(name="shared", bufs=1))
        late = ctx.enter_context(tc.tile_pool(name="late", bufs=1))
        first = ctx.enter_context(tc.tile_pool(name="first", bufs=1))
        third = ctx.enter_context(tc.tile_pool(name="third", bufs=1))
        mid = ctx.enter_context(tc.tile_pool(name="mid", bufs=1))
        ring = ctx.enter_context(tc.tile_pool(name="ring", bufs=RING))
        psum = ctx.enter_context(tc.psum_pool(name="psum", bufs=BANKS))

        offs_sb = lists.tile([NP, S // 16], U16, name="offs_sb")
        pos1_sb = lists.tile([NP, P // 16], U16, name="pos1_sb")
        pos2_sb = lists.tile([NP, P // 16], U16, name="pos2_sb")
        tab_rows = keep.tile([NP, T], U8, name="tab_rows", align_bytes=64)
        w4_rows = keep.tile([NP, H], U8, name="w4_rows", align_bytes=64)
        gain_col = keep.tile([NP, A2, 8], F32, name="gain_col")
        w4_early = keep.tile([NP, A1 - 1, H], U8, name="w4_early", align_bytes=64)
        w4_src = w4_words.rearrange("a p (b c) -> b p a c", b=A2)
        window = [first.tile([NP, T], I32, name="window0", align_bytes=64, offset=W4_RAW - LINK),
                  third.tile([NP, T], I32, name="window1", align_bytes=64, offset=WINDOW - LINK)]
        for queue, tile, rows in ((nc.sync, tab_rows, tab_scales), (nc.scalar, w4_rows, w4_scales)):
            queue.dma_start(tile[16:48, :].bitcast(I32), rows[0:2].rearrange("a s c -> s a c").bitcast(I32))
            queue.dma_start(tile[48:64, :].bitcast(I32), rows[2].bitcast(I32))
        nc.sync.dma_start(offs_sb[:], offs)
        nc.sync.dma_start(window[0][:], tab_words[0].rearrange("p t i -> p (t i)").bitcast(I32))
        nc.sync.dma_start(pos1_sb[:], pos1)
        nc.scalar.dma_start(gain_col[:, :, :4], gain.rearrange("(b p t) -> p b t", b=A2, t=4))
        nc.sync.dma_start(pos2_sb[:], pos2)
        nc.sync.dma_start(w4_early[:].bitcast(I32), w4_src[0][:, : A1 - 1].bitcast(I32))
        for tile in (tab_rows, w4_rows):
            nc.vector.memset(tile[0:16, :].bitcast(I32), 0)
            nc.vector.memset(tile[64:128, :].bitcast(I32), 0)

        warm_in = keep.tile([NP, 8], F32, name="warm_in")
        nc.vector.memset(warm_in[:], 0.0)
        warm_out = keep.tile([NP, 8], F32, name="warm_out")
        nc.scalar.activation(warm_out[:], warm_in[:], TANH)

        nc.sync.dma_start(window[1][:], tab_words[1].rearrange("p t i -> p (t i)").bitcast(I32))
        planes = keep.tile([NP, A1, S + H], U8, name="planes", align_bytes=64)
        nc.gpsimd.memset(planes[:].bitcast(I32), 0)

        w4_pair = [mid.tile([NP, 2, A1, 2 * NP], U8, name="w4_pair0", align_bytes=64, offset=0),
                   keep.tile([NP, 2, A1, 2 * NP], U8, name="w4_pair1", align_bytes=64)]

        def order_w4(copy, g, raw, passes):
            copy(w4_pair[g][:, :, passes].bitcast(U16),
                 raw[:].bitcast(U16).rearrange("p a (m t) -> p t a m", t=4)[:, 2 * (g % 2) : 2 * (g % 2) + 2])

        for g in range(2):
            order_w4(nc.scalar.copy, g, w4_early, slice(0, A1 - 1))

        picked_rows = shared.tile([NP, S], U8, name="picked_rows", align_bytes=64, offset=WORDS)
        both_rows = keep.tile([NP, S + H], U8, name="both_rows", align_bytes=64)
        nc.gpsimd.tensor_copy(
            both_rows[:, S:].rearrange("p (b t m) -> p b t m", b=A2, t=4),
            w4_rows[:].rearrange("p (b m t) -> p b t m", b=A2, t=4))
        nc.vector.tensor_copy(picked_rows[:], tab_rows[:].indirect(offs_sb[:]))
        nc.vector.tensor_copy(both_rows[:, :S].bitcast(I32), picked_rows[:].bitcast(I32))
        for q in QUADRANTS:
            nc.sync.dma_start(planes[32 * q : 32 * q + 4, 0:2, :].bitcast(I32), both_rows[16 + 8 * q : 24 + 8 * q, :].bitcast(I32))
        window.append(shared.tile([NP, T], I32, name="window2", align_bytes=64, offset=WORDS + LINK))
        nc.sync.dma_start(window[2][:], tab_words[2].rearrange("p t i -> p (t i)").bitcast(I32))
        for q in QUADRANTS:
            nc.sync.dma_start(planes[32 * q : 32 * q + 4, 2, :].bitcast(I32), both_rows[48 + 4 * q : 52 + 4 * q, :].bitcast(I32))

        gain0 = [keep.tile([NP, P], F32, name="gain00", tag="w2_bf10", align_bytes=64),
                 mid.tile([NP, P], F32, name="gain01", align_bytes=64, offset=GAIN01),
                 keep.tile([NP, P], F32, name="gain02"),
                 keep.tile([NP, P], F32, name="gain03")]
        gain1 = [keep.tile([NP, P], F32, name=f"gain1{t}") for t in range(3)]
        gain_last = [mid.tile([NP, P // 2], F32, name="gain13a", align_bytes=64, offset=GAIN13),
                     keep.tile([NP, P // 2], F32, name="gain13b")]
        gain_full = [[[tile] for tile in gain0], [[tile] for tile in gain1] + [gain_last]]
        for b in range(A2):
            for t in range(4):
                for tile in gain_full[b][t]:
                    nc.scalar.copy(tile[:], gain_col[:, b, t : t + 1].to_broadcast(tile.shape))

        words = [shared.tile([NP, S], U32, name="words0", align_bytes=64, offset=0),
                 keep.tile([NP, S], U32, name="words1", align_bytes=64)]
        words_last = [keep.tile([NP, N], U32, name=f"words_last{c}", align_bytes=64) for c in range(S // N)]

        def last_words(low, high):
            return words_last[low // N][:, low % N : low % N + high - low]

        nc.vector.tensor_copy(words[0][:], window[0][:].bitcast(U32).indirect(offs_sb[:]))
        w4_last = first.tile([NP, 1, H], U8, name="w4_last", align_bytes=64, offset=W4_RAW + WINDOW - 2 * LINK)
        nc.sync.dma_start(w4_last[:].bitcast(I32), w4_src[0][:, A1 - 1 :].bitcast(I32))
        for g in range(2):
            order_w4(nc.scalar.copy, g, w4_last, slice(A1 - 1, A1))
        w4_second = first.tile([NP, A1, H], U8, name="w4_second", align_bytes=64, offset=0)
        nc.sync.dma_start(w4_second[:].bitcast(I32), w4_src[1].bitcast(I32))
        nc.vector.tensor_copy(words[1][:], window[1][:].bitcast(U32).indirect(offs_sb[:]))
        for low in range(0, S, PIECE):
            nc.vector.tensor_copy(last_words(low, low + PIECE),
                                  window[2][:].bitcast(U32).indirect(offs_sb[:, low // 16 : (low + PIECE) // 16]))

        w4_pair.append(shared.tile([NP, 2, A1, 2 * NP], U8, name="w4_pair2", align_bytes=64, offset=PAIRS + W4_PAIR))
        w4_pair.append(shared.tile([NP, 2, A1, 2 * NP], U8, name="w4_pair3", align_bytes=64, offset=PAIRS))
        for g in (2, 3):
            order_w4(nc.vector.tensor_copy, g, w4_second, slice(0, A1))

        w2_src = w2.rearrange("(a p j) (b n) -> a b p j n", a=A2, j=4, b=A2)
        w2_raw = {}
        for a, b, pool, offset in ((0, 0, third, 0), (1, 0, third, 2 * WINDOW - 2 * LINK), (0, 1, shared, WORDS + WINDOW), (1, 1, first, 0)):
            w2_raw[a, b] = pool.tile([NP, 4, N], F32, name=f"w2_raw{a}{b}", align_bytes=64, offset=offset)
            nc.sync.dma_start(w2_raw[a, b][:], w2_src[a, b])

        d_col = third.tile([NP, A2, 8], F32, name="d_col", align_bytes=64, offset=WINDOW + LINK)
        nc.sync.dma_start(d_col[:, :, :4], d.rearrange("(b p t) -> p b t", b=A2, t=4))

        def first_pass(acc, b, t, a, low, high):
            cols = slice(low, high)
            moving = last_words(low, high) if a == A1 - 1 else words[a][:, cols]
            w4_cols = slice(S + N * b + NP * t, S + N * b + NP * (t + 1))
            nc.tensor.matmul_mx(out=acc[:], lhsT=w4_pair[2 * b + t // 2][:, t % 2, a, :].bitcast(FP4X4), lhsT_scale=planes[:, a, w4_cols],
                                rhs=moving.bitcast(FP8X4), rhs_scale=planes[:, a, cols],
                                start=(a == 0), stop=(a == A1 - 1))

        hs, fine, w2_bf, w2_mx = {}, {}, {}, {}

        def gather_fine(b, t, dst):
            nc.vector.tensor_copy(dst[:], hs[b, t][:].indirect(pos2_sb[:]))
            fine[b, t] = dst

        def scalar_weave(dst, src, cols, step):
            for start in range(0, cols, step):
                part = slice(start, min(start + step, cols))
                nc.scalar.copy(dst.rearrange("p t m j -> p m j t")[:, part], src.rearrange("p t m j -> p m j t")[:, part])

        def gpsimd_weave(dst, src):
            nc.gpsimd.tensor_scalar(dst.rearrange("p t m j -> p m t j"), src.rearrange("p t m j -> p m t j"), 1.0, 0.0, MULT, ADD)

        def weave_w2(a, b):
            src = w2_raw[a, b][:].rearrange("p j (m t) -> p t m j", t=4)
            if (a, b) == (0, 0):
                low = mid.tile([NP, 2, NP, 4], BF16, name="w2_bf00_low", align_bytes=64, offset=W4_PAIR - LINK)
                high = mid.tile([NP, 2, NP, 4], BF16, name="w2_bf00_high", align_bytes=64, offset=GAIN01 + TILE - LINK)
                gpsimd_weave(high[:], src[:, 2:])
                scalar_weave(low[:], src[:, :2], NP, 2 * WEAVE_STEP)
                w2_bf[a, b] = [low, high]
                return
            if b == 0:
                tile = keep.tile([NP, 4, NP, 4], BF16, name="w2_bf10", tag="w2_bf10", align_bytes=64)
            else:
                tile = late.tile([NP, 4, NP, 4], BF16, name=f"w2_bf{a}{b}", align_bytes=64, offset=(X32 + LINK, LAST_BF)[a])
            cols = NP
            if (a, b) == (1, 1):
                cols = NP - GPSIMD_COLS
                gpsimd_weave(tile[:, :, cols:], src[:, :, cols:])
            scalar_weave(tile[:], src, cols, WEAVE_STEP if b == 0 else NP)
            w2_bf[a, b] = [tile]

        def quantise_w2(a, b):
            if (a, b) == (0, 0):
                codes = third.tile([NP, N], U32, name="w2_codes00", align_bytes=64, offset=0)
            elif (a, b) == (1, 0):
                codes = mid.tile([NP, N], U32, name="w2_codes10", align_bytes=64, offset=CODES10)
            else:
                codes = keep.tile([NP, N], U32, name=f"w2_codes{a}{b}", align_bytes=64)
            scales = keep.tile([NP, N], U8, name=f"w2_scales{a}{b}", align_bytes=64)
            width = N // len(w2_bf[a, b])
            for i, tile in enumerate(w2_bf[a, b]):
                cols = slice(width * i, width * (i + 1))
                nc.vector.quantize_mx(out=codes[:, cols].bitcast(FP8X4), scales=scales[:, cols], in_=tile[:].rearrange("p t m j -> p (t m j)"))
            w2_mx[a, b] = (codes, scales)

        early = [(t, low + N * c, width) for c in range(S // N) for t, low, width in ((0, 0, PIECE), (0, PIECE, PIECE), (1, 0, N))]
        accs = [psum.tile([NP, width], F32, name="bank1", tag="bank2" if low % N else "bank1") for t, low, width in early]
        for a in range(A1 - 1):
            for (t, low, width), acc in zip(early, accs):
                first_pass(acc, 0, t, a, low, low + width)
        for t in range(EARLY_TILES):
            hs[0, t] = keep.tile([NP, S], F32, name=f"h0{t}")
        for (t, low, width), acc in zip(early, accs):
            first_pass(acc, 0, t, A1 - 1, low, low + width)
            nc.scalar.activation(hs[0, t][:, low : low + width], acc[:], TANH)

        x32 = []
        for b in range(A2):
            x_half = late.tile([NP, 4, P], F32, name=f"x32{b}", align_bytes=64, offset=X32 * b)
            for t in range(4):
                if (b, t) not in hs:
                    hs[b, t] = keep.tile([NP, S], F32, name=f"h{b}{t}")
                    for low in range(0, S, N):
                        acc = psum.tile([NP, N], F32, name="bank1", tag="bank1")
                        for a in range(A1):
                            first_pass(acc, b, t, a, low, low + N)
                        nc.scalar.activation(hs[b, t][:, low : low + N], acc[:], TANH)
                h = hs[b, t]
                cuts = len(gain_full[b][t])
                for i in range(cuts):
                    m = slice(P // cuts * i, P // cuts * (i + 1))
                    nc.vector.tensor_tensor(x_half[:, t, m], h[:].indirect(pos1_sb[:, m.start // 16 : m.stop // 16]), gain_full[b][t][i][:], MULT)
                if (b, t) == (0, EARLY_TILES - 1):
                    gather_fine(0, 1, keep.tile([NP, P], F32, name="fine01"))
                    gather_fine(0, 0, mid.tile([NP, P], F32, name="fine00", align_bytes=64, offset=FINE00))
            x32.append(x_half)

        for a in range(A2):
            weave_w2(a, 0)
            quantise_w2(a, 0)

        x_mx = []
        for a in range(A2):
            if a == 0:
                x_bf = shared.tile([NP, P, 4], BF16, name="x_bf0", align_bytes=64, offset=X_BF0)
            else:
                x_bf = late.tile([NP, P, 4], BF16, name="x_bf1", align_bytes=64, offset=2 * X32)
            steps, cuts = ((X_STEPS, 1), (2, 2))[a]
            for step in range(steps):
                part = slice(P // 4 // steps * step, P // 4 // steps * (step + 1))
                nc.scalar.copy(x_bf[:].rearrange("p (c i) t -> p c t i", i=4)[:, part], x32[a][:].rearrange("p t (c i) -> p c t i", i=4)[:, part])
            if a == 0:
                codes = mid.tile([NP, P], U32, name="x_codes0", align_bytes=64, offset=GAIN13 + TILE // 2 - LINK)
            else:
                codes = keep.tile([NP, P], U32, name="x_codes1", align_bytes=64)
            scales = keep.tile([NP, P], U8, name=f"x_scales{a}", align_bytes=64)
            for i in range(cuts):
                m = slice(P // cuts * i, P // cuts * (i + 1))
                nc.vector.quantize_mx(out=codes[:, m].bitcast(FP8X4), scales=scales[:, m], in_=x_bf[:, m, :].rearrange("p m t -> p (m t)"))
            x_mx.append((codes, scales))
            if a == 0:
                gather_fine(0, 2, late.tile([NP, P], F32, name="fine02", align_bytes=64, offset=0))

        for a in range(A2):
            weave_w2(a, 1)

        out_rows = out.rearrange("(b p t) m -> b t p m", b=A2, t=4)
        banks, fys = {}, {}

        def second_pass(a, b, t):
            if a == 0:
                banks[b, t] = psum.tile([NP, N], F32, name="bank2", tag=("bank2", "bank1")[b])
            cols = slice(NP * t, NP * (t + 1))
            nc.tensor.matmul_mx(out=banks[b, t][:], lhsT=w2_mx[a, b][0][:, cols].bitcast(FP8X4), lhsT_scale=w2_mx[a, b][1][:, cols],
                                rhs=x_mx[a][0][:].bitcast(FP8X4), rhs_scale=x_mx[a][1][:],
                                start=(a == 0), stop=(a == A2 - 1))

        def times_fine(b, t):
            if (b, t) == (0, 3):
                fy = first.tile([NP, P], F32, name=f"fy{b}{t}", align_bytes=64, offset=TILE * t)
            else:
                fy = keep.tile([NP, P], F32, name=f"fy{b}{t}", tag=f"fy{b}{t}")
            nc.vector.tensor_tensor(fy[:], banks[b, t][:], fine[b, t][:], MULT)
            fys[b, t] = fy

        def finish_on_vector(b, t, res):
            for m in (slice(0, P // 2), slice(P // 2, P)):
                nc.vector.scalar_tensor_tensor(res[:, m], fys[b, t][:, m], d_col[:, b, t : t + 1], fine[b, t][:, m], ADD, MULT)
                nc.scalar.dma_start(out_rows[b, t][:, m], res[:, m])

        def finish_on_gpsimd(b, t, res):
            if b == 0 and t in (1, 2):
                fyd = first.tile([NP, P], F32, name=f"fyd{b}{t}", align_bytes=64, offset=TILE * t)
            elif (b, t) == (1, 1):
                fyd = late.tile([NP, P], F32, name="fyd11", align_bytes=64, offset=TILE)
            else:
                fyd = keep.tile([NP, P], F32, name=f"fyd{b}{t}")
            nc.scalar.activation(fyd[:], fys[b, t][:], IDENT, bias=d_col[:, b, t : t + 1])
            nc.gpsimd.tensor_tensor(res[:], fyd[:], fine[b, t][:], MULT)
            nc.sync.dma_start(out_rows[b, t], res[:])

        def result(b, t):
            return ring.tile([NP, P], F32, name=f"res{b}{t}", tag="res")

        for t in range(4):
            for a in range(A2):
                second_pass(a, 0, t)
        gather_fine(0, 3, late.tile([NP, P], F32, name="fine03", align_bytes=64, offset=X32 + LINK - TILE))
        for t in range(3):
            times_fine(0, t)
        for a in range(A2):
            quantise_w2(a, 1)
            for t in range(4):
                second_pass(a, 1, t)
        finish_on_gpsimd(0, 0, late.tile([NP, P], F32, name="res00", align_bytes=64, offset=X32 + 2 * LINK))
        finish_on_gpsimd(0, 1, result(0, 1))
        times_fine(0, 3)
        for t in (2, 3):
            finish_on_gpsimd(0, t, result(0, t))
        for t in range(2):
            gather_fine(1, t, keep.tile([NP, P], F32, name=f"fine1{t}", tag=f"fy0{t}"))
        times_fine(1, 0)
        finish_on_gpsimd(1, 0, result(1, 0))
        gather_fine(1, 2, first.tile([NP, P], F32, name="fine12", align_bytes=64, offset=TILE * 3))
        times_fine(1, 1)
        finish_on_gpsimd(1, 1, result(1, 1))
        gather_fine(1, 3, keep.tile([NP, P], F32, name="fine13", tag="fy10"))
        times_fine(1, 2)
        times_fine(1, 3)
        finish_on_vector(1, 2, late.tile([NP, P], F32, name="res12", align_bytes=64, offset=LINK))
        finish_on_vector(1, 3, late.tile([NP, P], F32, name="res13", align_bytes=64, offset=2 * TILE - LINK))
